import numpy as np
import ml_dtypes


def mxq(x, axis, fmt="e4m3"):
    dtype, down = {"e4m3": (ml_dtypes.float8_e4m3fn, 7), "e5m2": (ml_dtypes.float8_e5m2, 14)}[fmt]
    v = np.moveaxis(np.asarray(x, np.float32).astype(ml_dtypes.bfloat16).astype(np.float64), axis, -1)
    blocks = v.reshape(v.shape[:-1] + (-1, 32))
    amax = np.abs(blocks).max(-1, keepdims=True)
    byte = np.maximum(np.where(amax > 0, np.frexp(amax)[1] - 1 + 127, 0) - down, 1)
    scale = np.exp2(byte - 127.0)
    codes = (blocks / scale).astype(np.float32).astype(dtype).astype(np.float64)
    return np.moveaxis((codes * scale).reshape(v.shape), -1, axis)


WIDE = False


def mx_kscale(k):
    if not WIDE:
        return np.ones(k)
    levels = np.array([10, -10, 5, -5, 0])
    if k % 512:
        return np.exp2(np.random.permutation(np.resize(levels, k // 32))).repeat(32)
    a = np.empty((k // 512, 16))
    for p in range(k // 512):
        a[p, :8] = np.random.permutation(np.resize(levels, 8))
        for g in range(8):
            far = levels[np.abs(levels - a[p, g]) >= 10]
            a[p, g + 8] = far[np.random.randint(len(far))]
    return np.exp2(a.ravel()).repeat(32)


BF16 = ml_dtypes.bfloat16


def bf(x):
    return np.asarray(x, np.float32).astype(BF16)


def f64(x):
    return np.asarray(x).astype(np.float64)


V, H, K, J, R = 4, 512, 1024, 1024, 512


def draw0():
    s, t = mx_kscale(K), mx_kscale(H)
    fade = np.exp(-2.0 * np.arange(H) / H)
    lasting = np.random.standard_normal((V, 1, K)) * fade[:, None]
    passing = 0.7 * np.random.standard_normal((V, H, K))
    size = np.random.uniform(0.5, 1.5, J)
    factor = np.random.standard_normal((K, J)) * size / np.sqrt(K)
    reach = (0.3 + np.tri(R, H)) * np.square(np.random.standard_normal((R, H)))
    return {"psi": bf((lasting + passing) * s * t[:, None]),
            "factor": bf(factor / s[:, None]),
            "cum": bf(reach / H / (t * t))}


def core(psi, factor, cum):
    theta = mxq(f64(psi), 2, "e4m3") @ mxq(f64(factor), 0, "e4m3")
    power = np.square(theta)
    var = mxq(f64(cum), 1, "e4m3") @ mxq(power, 1, "e4m3")
    level = np.mean(var, axis=2, keepdims=True)
    return var / level


def e4m3fn_bytes(y):
    return np.clip(np.asarray(y, np.float64), -448.0, 448.0).astype(np.float32).astype(ml_dtypes.float8_e4m3fn).view(np.uint8)


def e4m3fn_values(b):
    return np.asarray(b, np.uint8).view(ml_dtypes.float8_e4m3fn).astype(np.float64)


def setup_inputs():
    d = draw0()
    x0 = np.asarray(d['factor']).astype(np.float64)
    s = (np.max(np.abs(x0), axis=(1,), keepdims=True) / 448.0).astype(np.float32)
    out = {}
    for k, v in d.items():
        if k == 'factor':
            out['factor_bytes'] = e4m3fn_bytes(x0 / s.astype(np.float64))
            out['factor_scale'] = s
        else:
            out[k] = v
    return out


def reference(psi, factor_bytes, factor_scale, cum):
    return core(psi, e4m3fn_values(factor_bytes) * factor_scale.astype(np.float64), cum)

@@ -1,0 +1,347 @@
+from contextlib import ExitStack
+
+import concourse.mybir as mybir
+from concourse.masks import make_identity
+
+V, H, K, J, R = 4, 512, 1024, 1024, 512
+FLOPS = 2 * V * (H * K * J + R * H * J)
+
+F32 = mybir.dt.float32
+BF16 = mybir.dt.bfloat16
+U32 = mybir.dt.uint32
+U8 = mybir.dt.uint8
+FP8 = mybir.dt.float8_e4m3fn
+FP8X4 = mybir.dt.float8_e4m3fn_x4
+ACT = mybir.ActivationFunctionType
+ALU = mybir.AluOpType
+AX = mybir.AxisListType
+
+P = 128
+T = 4
+G = K // (P * T)
+CHUNK = 256
+N_CHUNKS = J // CHUNK
+N_UNIT = 128
+UNITS = J // N_UNIT
+HALF = 512
+UNITS_PER_HALF = HALF // N_UNIT
+
+
+CFG = {'chunks': [256, 256, 256, 256], 'fstep': [-1, -1, 0, 3], 'tr': {(1, 0): 4, (1, 1): -1, (1, 2): 1, (1, 3): 4, ('cum', 0): 1, ('cum', 1): 1, (2, 0): 2, (2, 1): 2, (2, 2): 4, (2, 3): 4, (3, 0): 4, (3, 1): 4, (3, 2): 8, (3, 3): 12}, 'cpv': [(3, 3), (2, 1)], 'pq': {1: 5, 2: 6, 3: 16}, 'cq': 1, 'sw': [(1, 0), (2, 0), (0, 0)], 'rv': [(2, 1), (3, 1), (4, 1), (5, 1), (3, 0), (6, 0), (5, 0), (1, 0), (0, 3), (0, 1), (1, 1), (4, 3), (0, 0)], 'lag2': 5, 'lagr': 1, 'red': [4, 6], 'nm': [4, 5, 6, 7], 'bufs': (3, 2, 3), 'sqf': 0
+}
+
+
+def tile_forecast_variance_shares_s7_kernel(tc, psi, factor_bytes, factor_scale, cum, out):
+    nc = tc.nc
+    with ExitStack() as ctx:
+        keep = ctx.enter_context(tc.tile_pool(name="keep", bufs=1))
+        pool = ctx.enter_context(tc.tile_pool(name="work", bufs=3))
+        keep4 = ctx.enter_context(tc.tile_pool(name="psi", bufs=4))
+        outs = ctx.enter_context(tc.tile_pool(name="outs", bufs=3))
+        ps_t = ctx.enter_context(tc.psum_pool(name="ps_t", bufs=CFG["bufs"][0]))
+        ps_a = ctx.enter_context(tc.psum_pool(name="ps_a", bufs=CFG["bufs"][1]))
+        ps_b = ctx.enter_context(tc.psum_pool(name="ps_b", bufs=CFG["bufs"][2]))
+
+        ident = keep.tile([P, P], F32, name="ident")
+        make_identity(nc, ident[:])
+        warm = keep.tile([P, 2], F32, name="warm")
+        nc.vector.memset(warm[:], 1.0)
+
+        ctx.enter_context(tc.manual_schedule())
+
+        nc.scalar.activation(warm[:, 1:2], warm[:, 0:1], ACT.Square)
+
+        fb = [keep.tile([P, G, T, 512], U8, name="fb%d" % h) for h in range(2)]
+        fs = keep.tile([P, G * T], F32, name="fs")
+        widths = CFG["chunks"]
+        starts = [sum(widths[:c]) for c in range(len(widths))]
+        fc = [keep.tile([P, G, n], U32, name="fc%d" % c, align_bytes=64) for c, n in enumerate(widths)]
+        fsc = [keep.tile([P, G, n], U8, name="fsc%d" % c, align_bytes=64) for c, n in enumerate(widths)]
+        cum_raw = keep.tile([P, T, H], BF16, name="cum_raw")
+        cum_g = keep.tile([P, T * H], BF16, name="cum_g", align_bytes=64)
+        cc = keep.tile([P, T, P], U32, name="cc", align_bytes=64)
+        cs = keep.tile([P, T, P], U8, name="cs", align_bytes=64)
+        psi_raw = [keep.tile([P, T, K], BF16, name="psi_raw%d" % v) for v in range(V)]
+
+        nc.sync.dma_start(out=fs[:].rearrange("p (g t) -> p g t", g=G), in_=factor_scale.rearrange("(g p t) o -> p g (t o)", p=P, t=T))
+        fb_src = factor_bytes.rearrange("(g p t) n -> p g t n", p=P, t=T)
+        psi_src = [psi[v].rearrange("(p t) k -> p t k", t=T) for v in range(V)]
+
+        def load_fb(h, g):
+            nc.sync.dma_start(out=fb[h][:, g], in_=fb_src[:, g, :, h * 512:(h + 1) * 512])
+
+        def load_psi(v, t, n=1):
+            nc.sync.dma_start(out=psi_raw[v][:, t:t + n, :], in_=psi_src[v][:, t:t + n, :])
+
+        load_psi(0, 0)
+        load_fb(0, 0)
+        load_fb(0, 1)
+        load_psi(0, 1)
+        load_psi(0, 2, 2)
+        load_psi(1, 0, 2)
+        load_psi(1, 2, 2)
+        load_fb(1, 0)
+        load_fb(1, 1)
+        nc.sync.dma_start(out=cum_raw[:], in_=cum.rearrange("(p t) h -> p t h", t=T))
+        load_psi(2, 0, 4)
+        load_psi(3, 0, 4)
+
+        psi_g = {}
+        psi_c = {}
+        psi_s = {}
+        banks = {}
+
+        def psi_tiles(v):
+            psi_g[v] = keep4.tile([P, T, K], BF16, name="psi_g", align_bytes=64)
+            psi_c[v] = keep4.tile([P, T, G, P], U32, name="psi_c", align_bytes=64)
+            psi_s[v] = keep4.tile([P, T, G, P], U8, name="psi_s", align_bytes=64)
+
+        def psi_transpose(v, t):
+            xt = ps_t.tile([P, 4, P], F32, name="xt")
+            words = psi_raw[v][:, t, :].bitcast(F32)
+            for g in range(G):
+                for u in range(2):
+                    nc.tensor.transpose(xt[:, 2 * g + u, :], words[:, 256 * g + u:256 * (g + 1):2], ident[:])
+            banks[v, t] = xt
+
+        def copy_out(eng, out, in_):
+            if eng == "s":
+                nc.scalar.copy(out, in_)
+            else:
+                nc.vector.tensor_copy(out, in_)
+
+        def psi_copy(v, t, eng):
+            copy_out(eng, psi_g[v][:, t, :].bitcast(F32).rearrange("p (g r u) -> p g r u", g=G, u=2),
+                     banks[v, t][:].rearrange("p (g u) r -> p g r u", g=G))
+
+        def psi_quant(v, t0, n=2):
+            nc.vector.quantize_mx(
+                out=psi_c[v][:, t0:t0 + n].rearrange("p t g r -> p (t g r)").bitcast(FP8X4),
+                scales=psi_s[v][:, t0:t0 + n].rearrange("p t g r -> p (t g r)"),
+                in_=psi_g[v][:, t0:t0 + n].rearrange("p t k -> p (t k)"))
+
+        def cum_transpose(b):
+            xt = ps_t.tile([P, 4, P], F32, name="xt")
+            for i in range(2):
+                words = cum_raw[:, 2 * b + i, :].bitcast(F32)
+                for u in range(2):
+                    nc.tensor.transpose(xt[:, 2 * i + u, :], words[:, u:256:2], ident[:])
+            banks["cum", b] = xt
+
+        def cum_copy(b, eng):
+            copy_out(eng, cum_g[:, 1024 * b:1024 * (b + 1)].bitcast(F32).rearrange("p (i r u) -> p i r u", i=2, u=2),
+                     banks["cum", b][:].rearrange("p (i u) r -> p i r u", i=2))
+
+        def cum_quant():
+            nc.vector.quantize_mx(out=cc[:].rearrange("p t r -> p (t r)").bitcast(FP8X4),
+                                  scales=cs[:].rearrange("p t r -> p (t r)"), in_=cum_g[:])
+
+        wides = {}
+        fgs = {}
+
+        def f_widen(c):
+            n = widths[c]
+            w = pool.tile([P, G, 2, n, 2], BF16, name="w")
+            for g in range(G):
+                for t in (0, 2, 1, 3):
+                    h, n0 = divmod(starts[c], 512)
+                    src = fb[h][:, g, t, n0:n0 + n].bitcast(FP8)
+                    sc = fs[:, g * T + t:g * T + t + 1]
+                    if (c, g) in CFG["sw"]:
+                        flat = w[:, g].rearrange("p b n e -> p (b n e)")
+                        nc.scalar.activation(flat[:, t * n:(t + 1) * n], src, ACT.Copy, scale=sc)
+                    else:
+                        nc.vector.tensor_scalar(w[:, g, t // 2, :, t % 2], src, sc, None, op0=ALU.mult)
+            wides[c] = w
+
+        def f_inter(c):
+            fg = pool.tile([P, G, widths[c] * T], BF16, name="fg", align_bytes=64)
+            for g in sorted(range(G), key=lambda g: (c, g) not in CFG["sw"]):
+                if (c, g) in CFG["sw"]:
+                    nc.vector.tensor_copy(fg[:, g, :].rearrange("p (n t) -> p n t", t=T),
+                                          wides[c][:, g].rearrange("p b n e -> p (b n e)").rearrange("p (t n) -> p n t", t=T))
+                else:
+                    nc.vector.tensor_copy(fg[:, g, :].bitcast(F32).rearrange("p (n b) -> p n b", b=2),
+                                          wides[c][:, g].rearrange("p b n e -> p (b n e)").bitcast(F32).rearrange("p (b n) -> p n b", b=2))
+            fgs[c] = fg
+
+        def f_quant(c):
+            for g in range(G):
+                nc.vector.quantize_mx(out=fc[c][:, g].bitcast(FP8X4), scales=fsc[c][:, g], in_=fgs[c][:, g])
+
+        pw = {}
+        pc = {}
+        psc = {}
+        var = {}
+        o = {}
+        sums = {}
+        recs = {}
+        read_done = set()
+
+        def stage1(i):
+            v, c = divmod(i, UNITS)
+            ps = ps_a.tile([P, T, N_UNIT], F32, name="theta")
+            ch = max(x for x in range(len(starts)) if starts[x] <= c * N_UNIT)
+            n0 = c * N_UNIT - starts[ch]
+            for t in range(T):
+                for g in range(G):
+                    nc.tensor.matmul_mx(
+                        out=ps[:, t, :],
+                        lhsT=psi_c[v][:, t, g, :].bitcast(FP8X4), lhsT_scale=psi_s[v][:, t, g, :],
+                        rhs=fc[ch][:, g, n0:n0 + N_UNIT].bitcast(FP8X4), rhs_scale=fsc[ch][:, g, n0:n0 + N_UNIT],
+                        start=(g == 0), stop=(g == G - 1))
+            banks["theta", i] = ps
+
+        def square(i):
+            q, a = divmod(i, UNITS_PER_HALF)
+            if a == 0:
+                pw[q] = pool.tile([P, UNITS_PER_HALF, N_UNIT, T], BF16, name="pw", align_bytes=64)
+            nc.scalar.activation(pw[q][:, a], banks["theta", i][:].rearrange("p t n -> p n t"), ACT.Square)
+
+        def pw_quant(q):
+            pc[q] = pool.tile([P, HALF], U32, name="pc", align_bytes=64)
+            psc[q] = pool.tile([P, HALF], U8, name="psc", align_bytes=64)
+            nc.vector.quantize_mx(out=pc[q][:].bitcast(FP8X4), scales=psc[q][:],
+                                  in_=pw[q][:].rearrange("p a n t -> p (a n t)"))
+
+        def stage2(q, m):
+            ps = ps_b.tile([P, HALF], F32, name="var")
+            nc.tensor.matmul_mx(out=ps[:], lhsT=cc[:, m, :].bitcast(FP8X4), lhsT_scale=cs[:, m, :],
+                                rhs=pc[q][:].bitcast(FP8X4), rhs_scale=psc[q][:], start=True, stop=True)
+            var[q, m] = ps
+
+        def read_var(q, m, eng):
+            v, h = divmod(q, 2)
+            if h == 0 and m == 0:
+                o[v] = outs.tile([P, T, J], F32, name="o")
+                sums[v] = outs.tile([P, T, 2], F32, name="sums")
+                recs[v] = outs.tile([P, 2, T], F32, name="recs")
+            read_done.add((q, m))
+            dst = o[v][:, m, h * HALF:(h + 1) * HALF]
+            if eng == "s":
+                nc.scalar.activation(dst, var[q, m][:], ACT.Copy, accum_out=sums[v][:, m, h:h + 1])
+            else:
+                nc.vector.tensor_scalar(dst, var[q, m][:], 1.0, None, op0=ALU.mult, op1=ALU.add, accum_out=sums[v][:, m, h:h + 1])
+
+        leveled = set()
+        normed = set()
+
+        def lv_red(v, m0, m1):
+            leveled.update((v, m) for m in range(m0, m1))
+            nc.vector.tensor_reduce(recs[v][:, 0, m0:m1], sums[v][:, m0:m1, :], axis=AX.X, op=ALU.add)
+
+        def lv_rec(v, m0, m1):
+            nc.vector.reciprocal(recs[v][:, 1, m0:m1], recs[v][:, 0, m0:m1])
+
+        def levels(v, m0, m1):
+            lv_red(v, m0, m1)
+            lv_rec(v, m0, m1)
+
+        def norm(v, m):
+            normed.add((v, m))
+            nc.vector.tensor_scalar(o[v][:, m, :], o[v][:, m, :], recs[v][:, 1, m:m + 1], float(J), op0=ALU.mult, op1=ALU.mult)
+            nc.sync.dma_start(out=out[v].rearrange("(p t) n -> p t n", t=T)[:, m, :], in_=o[v][:, m, :])
+
+        for v in range(V):
+            psi_tiles(v)
+        tr_at = {}
+        for key, s in CFG["tr"].items():
+            tr_at.setdefault(s, []).append(key)
+
+        def tr(step):
+            keys = tr_at.get(step, [])
+            for key in keys:
+                if key[0] == "cum":
+                    cum_transpose(key[1])
+                else:
+                    psi_transpose(*key)
+                e = "v" if key in CFG["cpv"] else "s"
+                if key[0] == "cum":
+                    cum_copy(key[1], e)
+                else:
+                    psi_copy(key[0], key[1], e)
+
+        def prep(c):
+            f_widen(c)
+            f_inter(c)
+            f_quant(c)
+
+        f_widen(0)
+        for t in range(T):
+            psi_transpose(0, t)
+            psi_copy(0, t, "s")
+        f_inter(0)
+        f_quant(0)
+        psi_quant(0, 0)
+        psi_quant(0, 2)
+        for c in range(1, len(widths)):
+            if CFG["fstep"][c] == -1:
+                prep(c)
+        tr(-1)
+
+        n_steps = V * UNITS
+        L = CFG["lag2"]
+        LR = L + CFG["lagr"]
+        for i in range(n_steps + 1):
+            v, j = divmod(i, UNITS)
+            if i < n_steps:
+                stage1(i)
+            q, m = divmod(i - LR, 4)
+            rd = 0 <= q < 2 * V - 1
+            eng = "v" if (q, m) in CFG["rv"] else "s"
+            if i < n_steps and CFG["sqf"]:
+                square(i)
+            if rd and eng == "s":
+                read_var(q, m, eng)
+            if i < n_steps and not CFG["sqf"]:
+                square(i)
+            if 1 <= v < V:
+                for h in range(2):
+                    if CFG["red"][h] == j:
+                        lv_red(v - 1, 2 * h, 2 * h + 2)
+            if i % 4 == 0 and 4 <= i <= n_steps:
+                pw_quant(i // 4 - 1)
+            if rd and eng == "v":
+                read_var(q, m, eng)
+            tr(i)
+            for c in range(1, len(widths)):
+                if CFG["fstep"][c] == i:
+                    prep(c)
+            if i == CFG["cq"]:
+                cum_quant()
+            for w in range(1, V):
+                if CFG["pq"][w] == i:
+                    psi_quant(w, 0, 4)
+            q, m = divmod(i - L, 4)
+            if 0 <= q < 2 * V - 1:
+                stage2(q, m)
+            if 1 <= v < V:
+                for h in range(2):
+                    if CFG["red"][h] == j:
+                        lv_rec(v - 1, 2 * h, 2 * h + 2)
+                for m in range(T):
+                    if CFG["nm"][m] == j:
+                        norm(v - 1, m)
+        q7 = 2 * V - 1
+        left = [(q7 - 1, m) for m in range(4) if (q7 - 1, m) not in read_done]
+        for q, m in left:
+            if (q, m) not in var:
+                stage2(q, m)
+        for q, m in left:
+            read_var(q, m, "v")
+        for m in range(T):
+            stage2(q7, m)
+        read_var(q7, 0, "s")
+        read_var(q7, 1, "v")
+        read_var(q7, 2, "s")
+        read_var(q7, 3, "s")
+        lv_red(V - 1, 0, 1)
+        lv_red(V - 1, 1, 2)
+        lv_rec(V - 1, 0, 1)
+        lv_rec(V - 1, 1, 2)
+        norm(V - 1, 0)
+        lv_red(V - 1, 2, 4)
+        norm(V - 1, 1)
+        lv_rec(V - 1, 2, 4)
+        norm(V - 1, 2)
+        norm(V - 1, 3)

@@ -14,334 +14,354 @@ FP8 = mybir.dt.float8_e4m3fn
 FP8X4 = mybir.dt.float8_e4m3fn_x4
 ACT = mybir.ActivationFunctionType
 ALU = mybir.AluOpType
-AX = mybir.AxisListType
 
 P = 128
 T = 4
 G = K // (P * T)
-CHUNK = 256
-N_CHUNKS = J // CHUNK
-N_UNIT = 128
-UNITS = J // N_UNIT
+UNIT = 128
 HALF = 512
-UNITS_PER_HALF = HALF // N_UNIT
-
-
-CFG = {'chunks': [256, 256, 256, 256], 'fstep': [-1, -1, 0, 3], 'tr': {(1, 0): 4, (1, 1): -1, (1, 2): 1, (1, 3): 4, ('cum', 0): 1, ('cum', 1): 1, (2, 0): 2, (2, 1): 2, (2, 2): 4, (2, 3): 4, (3, 0): 4, (3, 1): 4, (3, 2): 8, (3, 3): 12}, 'cpv': [(3, 3), (2, 1)], 'pq': {1: 5, 2: 6, 3: 16}, 'cq': 1, 'sw': [(1, 0), (2, 0), (0, 0)], 'rv': [(2, 1), (3, 1), (4, 1), (5, 1), (3, 0), (6, 0), (5, 0), (1, 0), (0, 3), (0, 1), (1, 1), (4, 3), (0, 0)], 'lag2': 5, 'lagr': 1, 'red': [4, 6], 'nm': [4, 5, 6, 7], 'bufs': (3, 2, 3), 'sqf': 0
-}
+UNITS = HALF // UNIT
+CHUNK = 256
+CHUNKS = J // CHUNK
+ORDER = [(v, h) for v in range(V) for h in range(2)]
+STEPS = len(ORDER) * UNITS
+LAG = 6
+WARM = 0
+SORTED = (2, 3)
+TURN0 = 5
+TURN_STEP = 2
+WP = (2, 1, 1)
+WT = (1, 1, 1, 0)
+SPLIT = 2
+FIN = 1
+SORT_LEAD = 2
+W3 = "vvs"
+PREP_AT = {2: 0, 3: 3}
+HEAD_INTER = "s"
+COPY_ENG = {1: "ssss", 2: "svsv", 3: "svsv", "cum": "ss"}
+READ_ENG = ["vsvs"] * 6 + ["ss"]
+NORM_LAG = 2
+PREP3 = 5
+PQ_AT = 0
+WARM2 = 2
+WARM2_AT = 1
 
 
 def tile_forecast_variance_shares_s7_kernel(tc, psi, factor_bytes, factor_scale, cum, out):
     nc = tc.nc
     with ExitStack() as ctx:
         keep = ctx.enter_context(tc.tile_pool(name="keep", bufs=1))
-        pool = ctx.enter_context(tc.tile_pool(name="work", bufs=3))
-        keep4 = ctx.enter_context(tc.tile_pool(name="psi", bufs=4))
+        work = ctx.enter_context(tc.tile_pool(name="work", bufs=3))
         outs = ctx.enter_context(tc.tile_pool(name="outs", bufs=3))
-        ps_t = ctx.enter_context(tc.psum_pool(name="ps_t", bufs=CFG["bufs"][0]))
-        ps_a = ctx.enter_context(tc.psum_pool(name="ps_a", bufs=CFG["bufs"][1]))
-        ps_b = ctx.enter_context(tc.psum_pool(name="ps_b", bufs=CFG["bufs"][2]))
+        psum = ctx.enter_context(tc.psum_pool(name="psum", bufs=8))
 
         ident = keep.tile([P, P], F32, name="ident")
         make_identity(nc, ident[:])
-        warm = keep.tile([P, 2], F32, name="warm")
-        nc.vector.memset(warm[:], 1.0)
+        if WARM:
+            zeros = keep.tile([P, HALF], BF16, name="zeros")
+            nc.vector.memset(zeros[:], 0.0)
 
         ctx.enter_context(tc.manual_schedule())
 
-        nc.scalar.activation(warm[:, 1:2], warm[:, 0:1], ACT.Square)
+        f_scale = keep.tile([P, G * T], F32, name="f_scale")
+        nc.scalar.dma_start(out=f_scale[:].rearrange("p (g t) -> p g t", g=G),
+                            in_=factor_scale.rearrange("(g p t) o -> p g (t o)", p=P, t=T))
+        f_src = factor_bytes.rearrange("(g p t) n -> g p t n", p=P, t=T)
+        f_bytes = {}
+        for g in range(G):
+            for b in range(2):
+                f_bytes[g, b] = keep.tile([P, 2, J], U8, name="f_bytes%d%d" % (g, b))
+                nc.sync.dma_start(out=f_bytes[g, b][:], in_=f_src[g][:, 2 * b:2 * b + 2, :])
 
-        fb = [keep.tile([P, G, T, 512], U8, name="fb%d" % h) for h in range(2)]
-        fs = keep.tile([P, G * T], F32, name="fs")
-        widths = CFG["chunks"]
-        starts = [sum(widths[:c]) for c in range(len(widths))]
-        fc = [keep.tile([P, G, n], U32, name="fc%d" % c, align_bytes=64) for c, n in enumerate(widths)]
-        fsc = [keep.tile([P, G, n], U8, name="fsc%d" % c, align_bytes=64) for c, n in enumerate(widths)]
-        cum_raw = keep.tile([P, T, H], BF16, name="cum_raw")
-        cum_g = keep.tile([P, T * H], BF16, name="cum_g", align_bytes=64)
-        cc = keep.tile([P, T, P], U32, name="cc", align_bytes=64)
-        cs = keep.tile([P, T, P], U8, name="cs", align_bytes=64)
-        psi_raw = [keep.tile([P, T, K], BF16, name="psi_raw%d" % v) for v in range(V)]
+        rows = {}
 
-        nc.sync.dma_start(out=fs[:].rearrange("p (g t) -> p g t", g=G), in_=factor_scale.rearrange("(g p t) o -> p g (t o)", p=P, t=T))
-        fb_src = factor_bytes.rearrange("(g p t) n -> p g t n", p=P, t=T)
-        psi_src = [psi[v].rearrange("(p t) k -> p t k", t=T) for v in range(V)]
+        def load_psi(v, t0, n):
+            tile = keep.tile([P, n * K], BF16, name="psi_rows%d%d" % (v, t0))
+            nc.sync.dma_start(out=tile[:], in_=psi[v].rearrange("(p t) k -> p (t k)", t=T)[:, t0 * K:(t0 + n) * K])
+            for i in range(n):
+                rows[v, t0 + i] = tile[:, i * K:(i + 1) * K]
 
-        def load_fb(h, g):
-            nc.sync.dma_start(out=fb[h][:, g], in_=fb_src[:, g, :, h * 512:(h + 1) * 512])
-
-        def load_psi(v, t, n=1):
-            nc.sync.dma_start(out=psi_raw[v][:, t:t + n, :], in_=psi_src[v][:, t:t + n, :])
-
-        load_psi(0, 0)
-        load_fb(0, 0)
-        load_fb(0, 1)
-        load_psi(0, 1)
-        load_psi(0, 2, 2)
+        for t in range(T):
+            load_psi(0, t, 1)
         load_psi(1, 0, 2)
         load_psi(1, 2, 2)
-        load_fb(1, 0)
-        load_fb(1, 1)
-        nc.sync.dma_start(out=cum_raw[:], in_=cum.rearrange("(p t) h -> p t h", t=T))
-        load_psi(2, 0, 4)
-        load_psi(3, 0, 4)
+        cum_rows = keep.tile([P, T * H], BF16, name="cum_rows")
+        nc.sync.dma_start(out=cum_rows[:], in_=cum.rearrange("(p t) h -> p (t h)", t=T))
+        rows["cum", 0] = cum_rows[:, :K]
+        rows["cum", 1] = cum_rows[:, K:]
+        load_psi(2, 0, T)
+        load_psi(3, 0, T)
 
-        psi_g = {}
-        psi_c = {}
-        psi_s = {}
-        banks = {}
+        def bank():
+            return psum.tile([P, HALF], F32, name="bank")
 
-        def psi_tiles(v):
-            psi_g[v] = keep4.tile([P, T, K], BF16, name="psi_g", align_bytes=64)
-            psi_c[v] = keep4.tile([P, T, G, P], U32, name="psi_c", align_bytes=64)
-            psi_s[v] = keep4.tile([P, T, G, P], U8, name="psi_s", align_bytes=64)
+        turned, grouped, codes, scales, ordered = {}, {}, {}, {}, {}
 
-        def psi_transpose(v, t):
-            xt = ps_t.tile([P, 4, P], F32, name="xt")
-            words = psi_raw[v][:, t, :].bitcast(F32)
-            for g in range(G):
+        def sort(key):
+            tile = work.tile([P, K // 2], F32, name="ordered")
+            nc.vector.tensor_copy(tile[:].rearrange("p (g u r) -> p g u r", g=2, u=2),
+                                  rows[key].bitcast(F32).rearrange("p (g r u) -> p g u r", g=2, u=2))
+            ordered[key] = tile
+
+        def turn(key):
+            ps = bank()
+            for g in range(2):
                 for u in range(2):
-                    nc.tensor.transpose(xt[:, 2 * g + u, :], words[:, 256 * g + u:256 * (g + 1):2], ident[:])
-            banks[v, t] = xt
-
-        def copy_out(eng, out, in_):
-            if eng == "s":
-                nc.scalar.copy(out, in_)
-            else:
-                nc.vector.tensor_copy(out, in_)
-
-        def psi_copy(v, t, eng):
-            copy_out(eng, psi_g[v][:, t, :].bitcast(F32).rearrange("p (g r u) -> p g r u", g=G, u=2),
-                     banks[v, t][:].rearrange("p (g u) r -> p g r u", g=G))
-
-        def psi_quant(v, t0, n=2):
-            nc.vector.quantize_mx(
-                out=psi_c[v][:, t0:t0 + n].rearrange("p t g r -> p (t g r)").bitcast(FP8X4),
-                scales=psi_s[v][:, t0:t0 + n].rearrange("p t g r -> p (t g r)"),
-                in_=psi_g[v][:, t0:t0 + n].rearrange("p t k -> p (t k)"))
-
-        def cum_transpose(b):
-            xt = ps_t.tile([P, 4, P], F32, name="xt")
-            for i in range(2):
-                words = cum_raw[:, 2 * b + i, :].bitcast(F32)
-                for u in range(2):
-                    nc.tensor.transpose(xt[:, 2 * i + u, :], words[:, u:256:2], ident[:])
-            banks["cum", b] = xt
-
-        def cum_copy(b, eng):
-            copy_out(eng, cum_g[:, 1024 * b:1024 * (b + 1)].bitcast(F32).rearrange("p (i r u) -> p i r u", i=2, u=2),
-                     banks["cum", b][:].rearrange("p (i u) r -> p i r u", i=2))
-
-        def cum_quant():
-            nc.vector.quantize_mx(out=cc[:].rearrange("p t r -> p (t r)").bitcast(FP8X4),
-                                  scales=cs[:].rearrange("p t r -> p (t r)"), in_=cum_g[:])
-
-        wides = {}
-        fgs = {}
-
-        def f_widen(c):
-            n = widths[c]
-            w = pool.tile([P, G, 2, n, 2], BF16, name="w")
-            for g in range(G):
-                for t in (0, 2, 1, 3):
-                    h, n0 = divmod(starts[c], 512)
-                    src = fb[h][:, g, t, n0:n0 + n].bitcast(FP8)
-                    sc = fs[:, g * T + t:g * T + t + 1]
-                    if (c, g) in CFG["sw"]:
-                        flat = w[:, g].rearrange("p b n e -> p (b n e)")
-                        nc.scalar.activation(flat[:, t * n:(t + 1) * n], src, ACT.Copy, scale=sc)
+                    if key in ordered:
+                        src = ordered[key][:, (2 * g + u) * P:(2 * g + u + 1) * P]
                     else:
-                        nc.vector.tensor_scalar(w[:, g, t // 2, :, t % 2], src, sc, None, op0=ALU.mult)
-            wides[c] = w
+                        src = rows[key].bitcast(F32)[:, 256 * g + u:256 * (g + 1):2]
+                    nc.tensor.transpose(ps[:, (2 * g + u) * P:(2 * g + u + 1) * P], src, ident[:])
+            turned[key] = ps
 
-        def f_inter(c):
-            fg = pool.tile([P, G, widths[c] * T], BF16, name="fg", align_bytes=64)
-            for g in sorted(range(G), key=lambda g: (c, g) not in CFG["sw"]):
-                if (c, g) in CFG["sw"]:
-                    nc.vector.tensor_copy(fg[:, g, :].rearrange("p (n t) -> p n t", t=T),
-                                          wides[c][:, g].rearrange("p b n e -> p (b n e)").rearrange("p (t n) -> p n t", t=T))
-                else:
-                    nc.vector.tensor_copy(fg[:, g, :].bitcast(F32).rearrange("p (n b) -> p n b", b=2),
-                                          wides[c][:, g].rearrange("p b n e -> p (b n e)").bitcast(F32).rearrange("p (b n) -> p n b", b=2))
-            fgs[c] = fg
+        def group(key, eng):
+            tile = work.tile([P, K], BF16, name="grouped", align_bytes=64, bufs=4)
+            dst = tile[:].bitcast(F32).rearrange("p (g r u) -> p g r u", g=2, u=2)
+            src = turned[key][:].rearrange("p (g u r) -> p g r u", g=2, u=2)
+            if eng == "s":
+                nc.scalar.copy(dst, src)
+            else:
+                nc.vector.tensor_copy(dst, src)
+            grouped[key] = tile
 
-        def f_quant(c):
-            for g in range(G):
-                nc.vector.quantize_mx(out=fc[c][:, g].bitcast(FP8X4), scales=fsc[c][:, g], in_=fgs[c][:, g])
+        def quantize(key, src):
+            n = src.shape[1] // T
+            name = "_".join(str(x) for x in key)
+            codes[key] = keep.tile([P, n], U32, name="codes_" + name, align_bytes=64)
+            scales[key] = keep.tile([P, n], U8, name="scales_" + name, align_bytes=64)
+            nc.vector.quantize_mx(out=codes[key][:].bitcast(FP8X4), scales=scales[key][:], in_=src)
 
-        pw = {}
-        pc = {}
-        psc = {}
-        var = {}
-        o = {}
-        sums = {}
-        recs = {}
-        read_done = set()
+        def quantize_rows(key):
+            quantize(key, grouped[key][:])
 
-        def stage1(i):
-            v, c = divmod(i, UNITS)
-            ps = ps_a.tile([P, T, N_UNIT], F32, name="theta")
-            ch = max(x for x in range(len(starts)) if starts[x] <= c * N_UNIT)
-            n0 = c * N_UNIT - starts[ch]
-            for t in range(T):
-                for g in range(G):
-                    nc.tensor.matmul_mx(
-                        out=ps[:, t, :],
-                        lhsT=psi_c[v][:, t, g, :].bitcast(FP8X4), lhsT_scale=psi_s[v][:, t, g, :],
-                        rhs=fc[ch][:, g, n0:n0 + N_UNIT].bitcast(FP8X4), rhs_scale=fsc[ch][:, g, n0:n0 + N_UNIT],
-                        start=(g == 0), stop=(g == G - 1))
-            banks["theta", i] = ps
+        pairs, woven = {}, {}
+
+        def widen(c, g, t):
+            if (c, g) not in pairs:
+                pairs[c, g] = work.tile([P, 2, CHUNK, 2], BF16, name="pairs", bufs=4)
+            nc.vector.tensor_scalar(pairs[c, g][:, t // 2, :, t % 2],
+                                    f_bytes[g, t // 2][:, t % 2, c * CHUNK:(c + 1) * CHUNK].bitcast(FP8),
+                                    f_scale[:, g * T + t:g * T + t + 1], None, op0=ALU.mult)
+
+        def weave(c, g, eng):
+            woven[c, g] = work.tile([P, CHUNK * T], BF16, name="woven", align_bytes=64, bufs=4)
+            dst = woven[c, g][:].bitcast(F32).rearrange("p (n b) -> p n b", b=2)
+            src = pairs[c, g][:].rearrange("p b n e -> p (b n e)").bitcast(F32).rearrange("p (b n) -> p n b", b=2)
+            if eng == "s":
+                nc.scalar.copy(dst, src)
+            else:
+                nc.vector.tensor_copy(dst, src)
+
+        def quantize_factor(c, g):
+            quantize(("factor", c, g), woven[c, g][:])
+
+        theta, power, var, res, sums, recs = {}, {}, {}, {}, {}, {}
+
+        def stage1(steps, slots=range(T)):
+            for i in steps:
+                if i not in theta:
+                    theta[i] = bank()
+            for t in slots:
+                for i in steps:
+                    v, h = ORDER[i // UNITS]
+                    c, n0 = divmod(h * HALF + i % UNITS * UNIT, CHUNK)
+                    for g in range(G):
+                        nc.tensor.matmul_mx(
+                            out=theta[i][:, t * UNIT:(t + 1) * UNIT],
+                            lhsT=codes[v, t][:, g * P:(g + 1) * P].bitcast(FP8X4), lhsT_scale=scales[v, t][:, g * P:(g + 1) * P],
+                            rhs=codes["factor", c, g][:, n0:n0 + UNIT].bitcast(FP8X4), rhs_scale=scales["factor", c, g][:, n0:n0 + UNIT],
+                            start=(g == 0), stop=(g == G - 1))
 
         def square(i):
-            q, a = divmod(i, UNITS_PER_HALF)
+            k, a = divmod(i, UNITS)
             if a == 0:
-                pw[q] = pool.tile([P, UNITS_PER_HALF, N_UNIT, T], BF16, name="pw", align_bytes=64)
-            nc.scalar.activation(pw[q][:, a], banks["theta", i][:].rearrange("p t n -> p n t"), ACT.Square)
+                power[k] = work.tile([P, HALF * T], BF16, name="power", align_bytes=64)
+            nc.scalar.activation(power[k][:, a * UNIT * T:(a + 1) * UNIT * T].rearrange("p (n t) -> p n t", t=T),
+                                 theta[i][:].rearrange("p (t n) -> p n t", t=T), ACT.Square)
 
-        def pw_quant(q):
-            pc[q] = pool.tile([P, HALF], U32, name="pc", align_bytes=64)
-            psc[q] = pool.tile([P, HALF], U8, name="psc", align_bytes=64)
-            nc.vector.quantize_mx(out=pc[q][:].bitcast(FP8X4), scales=psc[q][:],
-                                  in_=pw[q][:].rearrange("p a n t -> p (a n t)"))
+        def quantize_power(k, n0, n):
+            quantize(("power", k, n0), power[k][:, n0 * T:(n0 + n) * T])
 
-        def stage2(q, m):
-            ps = ps_b.tile([P, HALF], F32, name="var")
-            nc.tensor.matmul_mx(out=ps[:], lhsT=cc[:, m, :].bitcast(FP8X4), lhsT_scale=cs[:, m, :],
-                                rhs=pc[q][:].bitcast(FP8X4), rhs_scale=psc[q][:], start=True, stop=True)
-            var[q, m] = ps
+        def stage2(ps, k, n0, m):
+            cols = slice(m % 2 * P, (m % 2 + 1) * P)
+            nc.tensor.matmul_mx(out=ps, lhsT=codes["cum", m // 2][:, cols].bitcast(FP8X4), lhsT_scale=scales["cum", m // 2][:, cols],
+                                rhs=codes["power", k, n0][:].bitcast(FP8X4), rhs_scale=scales["power", k, n0][:],
+                                start=True, stop=True)
+            var[k, n0, m] = ps
 
-        def read_var(q, m, eng):
-            v, h = divmod(q, 2)
-            if h == 0 and m == 0:
-                o[v] = outs.tile([P, T, J], F32, name="o")
-                sums[v] = outs.tile([P, T, 2], F32, name="sums")
-                recs[v] = outs.tile([P, 2, T], F32, name="recs")
-            read_done.add((q, m))
-            dst = o[v][:, m, h * HALF:(h + 1) * HALF]
+        def read(k, n0, m, eng, slot, first=None):
+            v, h = ORDER[k]
+            if v not in res:
+                res[v] = outs.tile([P, T * J], F32, name="res")
+                sums[v] = keep.tile([P, T * 8], F32, name="sums%d" % v)
+                recs[v] = keep.tile([P, 2 * T], F32, name="recs%d" % v)
+            src = var[k, n0, m]
+            c0 = m * J + h * HALF + n0
+            dst = res[v][:, c0:c0 + src.shape[1]]
+            acc = sums[v][:, slot * T + m:slot * T + m + 1]
             if eng == "s":
-                nc.scalar.activation(dst, var[q, m][:], ACT.Copy, accum_out=sums[v][:, m, h:h + 1])
+                nc.scalar.activation(dst, src, ACT.Copy, accum_out=acc)
             else:
-                nc.vector.tensor_scalar(dst, var[q, m][:], 1.0, None, op0=ALU.mult, op1=ALU.add, accum_out=sums[v][:, m, h:h + 1])
+                init = None if first is None else sums[v][:, first * T + m:first * T + m + 1]
+                nc.vector.tensor_scalar(dst, src, 1.0, init, op0=ALU.mult, op1=ALU.add, accum_out=acc)
 
-        leveled = set()
-        normed = set()
+        def add_halves(v, m0, m1):
+            nc.vector.tensor_tensor(recs[v][:, m0:m1], sums[v][:, m0:m1], sums[v][:, T + m0:T + m1], op=ALU.add)
 
-        def lv_red(v, m0, m1):
-            leveled.update((v, m) for m in range(m0, m1))
-            nc.vector.tensor_reduce(recs[v][:, 0, m0:m1], sums[v][:, m0:m1, :], axis=AX.X, op=ALU.add)
+        def invert(v, m0, m1, src=None):
+            nc.vector.reciprocal(recs[v][:, T + m0:T + m1], recs[v][:, m0:m1] if src is None else src)
 
-        def lv_rec(v, m0, m1):
-            nc.vector.reciprocal(recs[v][:, 1, m0:m1], recs[v][:, 0, m0:m1])
+        def finish(v, m):
+            row = res[v][:, m * J:(m + 1) * J]
+            nc.vector.tensor_scalar(row, row, recs[v][:, T + m:T + m + 1], float(J), op0=ALU.mult, op1=ALU.mult)
+            nc.sync.dma_start(out=out[v].rearrange("(p t) n -> p t n", t=T)[:, m, :], in_=row)
 
-        def levels(v, m0, m1):
-            lv_red(v, m0, m1)
-            lv_rec(v, m0, m1)
+        planes = {}
 
-        def norm(v, m):
-            normed.add((v, m))
-            nc.vector.tensor_scalar(o[v][:, m, :], o[v][:, m, :], recs[v][:, 1, m:m + 1], float(J), op0=ALU.mult, op1=ALU.mult)
-            nc.sync.dma_start(out=out[v].rearrange("(p t) n -> p t n", t=T)[:, m, :], in_=o[v][:, m, :])
+        def widen_plane(c, g, t):
+            if (c, g) not in planes:
+                planes[c, g] = keep.tile([P, T * CHUNK], BF16, name="planes%d%d" % (c, g))
+            nc.scalar.activation(planes[c, g][:, t * CHUNK:(t + 1) * CHUNK],
+                                 f_bytes[g, t // 2][:, t % 2, c * CHUNK:(c + 1) * CHUNK].bitcast(FP8), ACT.Copy,
+                                 scale=f_scale[:, g * T + t:g * T + t + 1])
 
-        for v in range(V):
-            psi_tiles(v)
-        tr_at = {}
-        for key, s in CFG["tr"].items():
-            tr_at.setdefault(s, []).append(key)
+        def weave_planes(c, g):
+            woven[c, g] = work.tile([P, CHUNK * T], BF16, name="woven", align_bytes=64, bufs=4)
+            nc.vector.tensor_copy(woven[c, g][:].rearrange("p (n t) -> p n t", t=T),
+                                  planes[c, g][:].rearrange("p (t n) -> p n t", t=T))
 
-        def tr(step):
-            keys = tr_at.get(step, [])
-            for key in keys:
-                if key[0] == "cum":
-                    cum_transpose(key[1])
-                else:
-                    psi_transpose(*key)
-                e = "v" if key in CFG["cpv"] else "s"
-                if key[0] == "cum":
-                    cum_copy(key[1], e)
-                else:
-                    psi_copy(key[0], key[1], e)
+        def warm(n, src=None):
+            for i in range(n if WARM else 0):
+                nc.tensor.matmul(spare[:], zeros[:, :P], zeros[:] if src is None else src, start=True, stop=True)
 
-        def prep(c):
-            f_widen(c)
-            f_inter(c)
-            f_quant(c)
+        def pair_half(c, g, b):
+            return pairs[c, g][:, b].rearrange("p n e -> p (n e)")
 
-        f_widen(0)
+        def turn_pair(v, b):
+            for t in (2 * b, 2 * b + 1):
+                turn((v, t))
+                group((v, t), COPY_ENG[v][t])
+
+        if WARM:
+            spare = bank()
+        warm(WARM)
         for t in range(T):
-            psi_transpose(0, t)
-            psi_copy(0, t, "s")
-        f_inter(0)
-        f_quant(0)
-        psi_quant(0, 0)
-        psi_quant(0, 2)
-        for c in range(1, len(widths)):
-            if CFG["fstep"][c] == -1:
-                prep(c)
-        tr(-1)
-
-        n_steps = V * UNITS
-        L = CFG["lag2"]
-        LR = L + CFG["lagr"]
-        for i in range(n_steps + 1):
-            v, j = divmod(i, UNITS)
-            if i < n_steps:
-                stage1(i)
-            q, m = divmod(i - LR, 4)
-            rd = 0 <= q < 2 * V - 1
-            eng = "v" if (q, m) in CFG["rv"] else "s"
-            if i < n_steps and CFG["sqf"]:
+            widen(0, 0, t)
+            widen_plane(1, 0, t)
+            if t % 2:
+                warm(WP[t // 2], pair_half(0, 0, t // 2))
+        weave(0, 0, "s")
+        widen(0, 1, 0)
+        widen(0, 1, 1)
+        warm(WP[2], pair_half(0, 1, 0))
+        weave_planes(1, 0)
+        widen(0, 1, 2)
+        widen(0, 1, 3)
+        weave(0, 1, "s")
+        quantize_factor(0, 0)
+        for t in range(T):
+            widen(1, 1, t)
+        turn((0, 0))
+        group((0, 0), "s")
+        warm(WT[0])
+        weave(1, 1, "s")
+        quantize_factor(1, 0)
+        quantize_factor(0, 1)
+        for t in range(1, T):
+            turn((0, t))
+            group((0, t), "s")
+            warm(WT[t])
+        quantize_rows((0, 0))
+        quantize_factor(1, 1)
+        quantize_rows((0, 1))
+        for t in range(2, T):
+            widen(2, 0, 2 * t - 4)
+            widen(2, 0, 2 * t - 3)
+            quantize_rows((0, t))
+        stage1(range(UNITS), range(SPLIT))
+        weave(2, 0, "s")
+        for t in range(T):
+            widen(2, 1, t)
+        turn_pair(1, 0)
+        stage1(range(UNITS), range(SPLIT, T))
+        weave(2, 1, W3[2])
+        for t in range(T):
+            widen(3, 0, t)
+        quantize_factor(2, 0)
+        for t in range(T):
+            widen(3, 1, t)
+        quantize_factor(2, 1)
+        weave(3, 0, W3[0])
+        weave(3, 1, W3[1])
+        for i in range(UNITS):
+            square(i)
+        quantize_factor(3, 0)
+        quantize_factor(3, 1)
+        quantize_rows((1, 0))
+        quantize_rows((1, 1))
+        for b in range(2):
+            turn(("cum", b))
+            group(("cum", b), COPY_ENG["cum"][b])
+        last = len(ORDER) - 1
+        per = 2 * UNITS
+        turns = {TURN0 + TURN_STEP * n: divmod(3 + n, 2) for n in range(2 * V - 3)}
+        for i in range(UNITS, STEPS + LAG - UNITS):
+            k, a = divmod(i, UNITS)
+            if i in turns:
+                turn_pair(*turns[i])
+            if i == per:
+                stage1([i, i + 1])
                 square(i)
-            if rd and eng == "s":
-                read_var(q, m, eng)
-            if i < n_steps and not CFG["sqf"]:
+                square(i + 1)
+            elif i != per + 1 and i < STEPS:
+                stage1([i])
                 square(i)
-            if 1 <= v < V:
-                for h in range(2):
-                    if CFG["red"][h] == j:
-                        lv_red(v - 1, 2 * h, 2 * h + 2)
-            if i % 4 == 0 and 4 <= i <= n_steps:
-                pw_quant(i // 4 - 1)
-            if rd and eng == "v":
-                read_var(q, m, eng)
-            tr(i)
-            for c in range(1, len(widths)):
-                if CFG["fstep"][c] == i:
-                    prep(c)
-            if i == CFG["cq"]:
-                cum_quant()
-            for w in range(1, V):
-                if CFG["pq"][w] == i:
-                    psi_quant(w, 0, 4)
-            q, m = divmod(i - L, 4)
-            if 0 <= q < 2 * V - 1:
-                stage2(q, m)
-            if 1 <= v < V:
-                for h in range(2):
-                    if CFG["red"][h] == j:
-                        lv_rec(v - 1, 2 * h, 2 * h + 2)
-                for m in range(T):
-                    if CFG["nm"][m] == j:
-                        norm(v - 1, m)
-        q7 = 2 * V - 1
-        left = [(q7 - 1, m) for m in range(4) if (q7 - 1, m) not in read_done]
-        for q, m in left:
-            if (q, m) not in var:
-                stage2(q, m)
-        for q, m in left:
-            read_var(q, m, "v")
+            if a == 0 and k <= last:
+                quantize_power(k - 1, 0, HALF)
+            if i == UNITS:
+                quantize_rows(("cum", 0))
+                quantize_rows(("cum", 1))
+            if i == STEPS - 2:
+                quantize_power(last, 0, HALF // 2)
+            if i == STEPS:
+                quantize_power(last, HALF // 2, HALF // 2)
+            w, n = divmod(i - LAG - UNITS - NORM_LAG, per)
+            if 0 <= w < V - 1 and n in (0, 2):
+                add_halves(w, n, n + 2)
+            q, m = divmod(i - LAG, UNITS)
+            if 0 <= q < last and i < STEPS:
+                stage2(bank()[:], q, 0, m)
+                read(q, 0, m, READ_ENG[q][m], ORDER[q][1])
+            if 0 <= w < V - 1 and n in (0, 2):
+                invert(w, n, n + 2)
+            if i - 1 in turns:
+                v, b = turns[i - 1]
+                quantize_rows((v, 2 * b))
+                quantize_rows((v, 2 * b + 1))
+            if i + SORT_LEAD in turns and turns[i + SORT_LEAD][0] in SORTED:
+                v, b = turns[i + SORT_LEAD]
+                sort((v, 2 * b))
+                sort((v, 2 * b + 1))
+            if 0 <= w < V - 1 and FIN <= n < FIN + T:
+                finish(w, n - FIN)
+        v = V - 1
+        late = range((STEPS - LAG) % UNITS, T)
+        for m in late:
+            stage2(bank()[:], last - 1, 0, m)
+        for part in range(2):
+            for b in range(2):
+                ps = bank()
+                for e in range(2):
+                    stage2(ps[:, e * 256:(e + 1) * 256], last, part * 256, 2 * b + e)
         for m in range(T):
-            stage2(q7, m)
-        read_var(q7, 0, "s")
-        read_var(q7, 1, "v")
-        read_var(q7, 2, "s")
-        read_var(q7, 3, "s")
-        lv_red(V - 1, 0, 1)
-        lv_red(V - 1, 1, 2)
-        lv_rec(V - 1, 0, 1)
-        lv_rec(V - 1, 1, 2)
-        norm(V - 1, 0)
-        lv_red(V - 1, 2, 4)
-        norm(V - 1, 1)
-        lv_rec(V - 1, 2, 4)
-        norm(V - 1, 2)
-        norm(V - 1, 3)
+            if m in late:
+                read(last - 1, 0, m, "s", 0)
+            read(last, 0, m, "s", 1)
+        for b in range(2):
+            nc.vector.tensor_tensor(sums[v][:, 2 * T + 2 * b:2 * T + 2 * b + 2], sums[v][:, 2 * b:2 * b + 2], sums[v][:, T + 2 * b:T + 2 * b + 2], op=ALU.add)
+            for m in (2 * b, 2 * b + 1):
+                read(last, 256, m, "v", 3, 2)
+            for m in (2 * b, 2 * b + 1):
+                invert(v, m, m + 1, sums[v][:, 3 * T + m:3 * T + m + 1])
+            finish(v, 2 * b)
+            finish(v, 2 * b + 1)

@@ -26,7 +26,7 @@ CHUNKS = J // CHUNK
 ORDER = [(v, h) for v in range(V) for h in range(2)]
 STEPS = len(ORDER) * UNITS
 LAG = 6
-WARM = 0
+WARM = 3
 SORTED = (2, 3)
 TURN0 = 5
 TURN_STEP = 2

@@ -28,18 +28,25 @@ STEPS = len(ORDER) * UNITS
 LAG = 6
 WARM = 3
 SORTED = (2, 3)
-TURN0 = 5
+TURN0 = 9
 TURN_STEP = 2
+LONG = 0
 WP = (2, 1, 1)
-WT = (1, 1, 1, 0)
+WT = (1, 1, 0, 0)
 SPLIT = 2
+ON_G = ()
 FIN = 1
-SORT_LEAD = 2
+SORT_LEAD = 3
 W3 = "vvs"
+RUN = 4
+S20 = 2
+E20 = "s"
+E21 = "s"
+PREP_ENG = "vvvv"
 PREP_AT = {2: 0, 3: 3}
 HEAD_INTER = "s"
-COPY_ENG = {1: "ssss", 2: "svsv", 3: "svsv", "cum": "ss"}
-READ_ENG = ["vsvs"] * 6 + ["ss"]
+COPY_ENG = {1: "ssss", 2: "ssss", 3: "ssss", "cum": "ss"}
+READ_ENG = ["vsvs"] * 7
 NORM_LAG = 2
 PREP3 = 5
 PQ_AT = 0
@@ -98,7 +105,7 @@ def tile_forecast_variance_shares_s7_kernel(tc, psi, factor_bytes, factor_scale,
         turned, grouped, codes, scales, ordered = {}, {}, {}, {}, {}
 
         def sort(key):
-            tile = work.tile([P, K // 2], F32, name="ordered")
+            tile = work.tile([P, K // 2], F32, name="ordered", bufs=4)
             nc.vector.tensor_copy(tile[:].rearrange("p (g u r) -> p g u r", g=2, u=2),
                                   rows[key].bitcast(F32).rearrange("p (g r u) -> p g u r", g=2, u=2))
             ordered[key] = tile
@@ -134,23 +141,27 @@ def tile_forecast_variance_shares_s7_kernel(tc, psi, factor_bytes, factor_scale,
         def quantize_rows(key):
             quantize(key, grouped[key][:])
 
-        pairs, woven = {}, {}
+        planes, woven = {}, {}
 
-        def widen(c, g, t):
-            if (c, g) not in pairs:
-                pairs[c, g] = work.tile([P, 2, CHUNK, 2], BF16, name="pairs", bufs=4)
-            nc.vector.tensor_scalar(pairs[c, g][:, t // 2, :, t % 2],
-                                    f_bytes[g, t // 2][:, t % 2, c * CHUNK:(c + 1) * CHUNK].bitcast(FP8),
-                                    f_scale[:, g * T + t:g * T + t + 1], None, op0=ALU.mult)
-
-        def weave(c, g, eng):
-            woven[c, g] = work.tile([P, CHUNK * T], BF16, name="woven", align_bytes=64, bufs=4)
-            dst = woven[c, g][:].bitcast(F32).rearrange("p (n b) -> p n b", b=2)
-            src = pairs[c, g][:].rearrange("p b n e -> p (b n e)").bitcast(F32).rearrange("p (b n) -> p n b", b=2)
+        def widen(c, g, t, eng):
+            if (c, g) not in planes:
+                planes[c, g] = keep.tile([P, T * CHUNK], BF16, name="planes%d%d" % (c, g))
+            dst = planes[c, g][:, t * CHUNK:(t + 1) * CHUNK]
+            src = f_bytes[g, t // 2][:, t % 2, c * CHUNK:(c + 1) * CHUNK].bitcast(FP8)
+            scale = f_scale[:, g * T + t:g * T + t + 1]
             if eng == "s":
-                nc.scalar.copy(dst, src)
+                nc.scalar.activation(dst, src, ACT.Copy, scale=scale)
             else:
-                nc.vector.tensor_copy(dst, src)
+                nc.vector.tensor_scalar(dst, src, scale, None, op0=ALU.mult)
+
+        def widen_all(c, g, eng):
+            for t in range(T):
+                widen(c, g, t, eng)
+
+        def weave(c, g):
+            woven[c, g] = work.tile([P, CHUNK * T], BF16, name="woven", align_bytes=64, bufs=4)
+            nc.vector.tensor_copy(woven[c, g][:].rearrange("p (n i t) -> p n t i", t=T, i=RUN),
+                                  planes[c, g][:].rearrange("p (t n i) -> p n t i", t=T, i=RUN))
 
         def quantize_factor(c, g):
             quantize(("factor", c, g), woven[c, g][:])
@@ -211,120 +222,97 @@ def tile_forecast_variance_shares_s7_kernel(tc, psi, factor_bytes, factor_scale,
         def invert(v, m0, m1, src=None):
             nc.vector.reciprocal(recs[v][:, T + m0:T + m1], recs[v][:, m0:m1] if src is None else src)
 
+        finished = set()
+
         def finish(v, m):
+            finished.add((v, m))
             row = res[v][:, m * J:(m + 1) * J]
-            nc.vector.tensor_scalar(row, row, recs[v][:, T + m:T + m + 1], float(J), op0=ALU.mult, op1=ALU.mult)
+            eng = nc.gpsimd if (v, m) in ON_G else nc.vector
+            eng.tensor_scalar(row, row, recs[v][:, T + m:T + m + 1], float(J), op0=ALU.mult, op1=ALU.mult)
             nc.sync.dma_start(out=out[v].rearrange("(p t) n -> p t n", t=T)[:, m, :], in_=row)
-
-        planes = {}
-
-        def widen_plane(c, g, t):
-            if (c, g) not in planes:
-                planes[c, g] = keep.tile([P, T * CHUNK], BF16, name="planes%d%d" % (c, g))
-            nc.scalar.activation(planes[c, g][:, t * CHUNK:(t + 1) * CHUNK],
-                                 f_bytes[g, t // 2][:, t % 2, c * CHUNK:(c + 1) * CHUNK].bitcast(FP8), ACT.Copy,
-                                 scale=f_scale[:, g * T + t:g * T + t + 1])
-
-        def weave_planes(c, g):
-            woven[c, g] = work.tile([P, CHUNK * T], BF16, name="woven", align_bytes=64, bufs=4)
-            nc.vector.tensor_copy(woven[c, g][:].rearrange("p (n t) -> p n t", t=T),
-                                  planes[c, g][:].rearrange("p (t n) -> p n t", t=T))
 
         def warm(n, src=None):
             for i in range(n if WARM else 0):
                 nc.tensor.matmul(spare[:], zeros[:, :P], zeros[:] if src is None else src, start=True, stop=True)
 
-        def pair_half(c, g, b):
-            return pairs[c, g][:, b].rearrange("p n e -> p (n e)")
-
-        def turn_pair(v, b):
-            for t in (2 * b, 2 * b + 1):
+        def turn_run(v, slots):
+            for t in slots:
                 turn((v, t))
+            for t in slots:
                 group((v, t), COPY_ENG[v][t])
 
         if WARM:
             spare = bank()
         warm(WARM)
-        for t in range(T):
-            widen(0, 0, t)
-            widen_plane(1, 0, t)
-            if t % 2:
-                warm(WP[t // 2], pair_half(0, 0, t // 2))
-        weave(0, 0, "s")
-        widen(0, 1, 0)
-        widen(0, 1, 1)
-        warm(WP[2], pair_half(0, 1, 0))
-        weave_planes(1, 0)
-        widen(0, 1, 2)
-        widen(0, 1, 3)
-        weave(0, 1, "s")
+        for b in range(2):
+            for t in (2 * b, 2 * b + 1):
+                widen(0, 0, t, "v")
+                widen(1, 0, t, "s")
+            warm(WP[b], planes[0, 0][:, b * HALF:(b + 1) * HALF])
+        widen(0, 1, 0, "v")
+        widen(0, 1, 1, "v")
+        warm(WP[2], planes[0, 1][:, :HALF])
+        weave(0, 0)
+        widen(0, 1, 2, "v")
+        widen(0, 1, 3, "v")
+        widen_all(1, 1, "s")
         quantize_factor(0, 0)
-        for t in range(T):
-            widen(1, 1, t)
-        turn((0, 0))
-        group((0, 0), "s")
-        warm(WT[0])
-        weave(1, 1, "s")
-        quantize_factor(1, 0)
+        weave(0, 1)
+        weave(1, 0)
         quantize_factor(0, 1)
-        for t in range(1, T):
+        for t in range(S20):
+            widen(2, 0, t, "s")
+        for t in range(T):
             turn((0, t))
             group((0, t), "s")
             warm(WT[t])
+        for t in range(S20, T):
+            widen(2, 0, t, E20)
+        if E21 == "s":
+            widen_all(2, 1, "s")
         quantize_rows((0, 0))
-        quantize_factor(1, 1)
         quantize_rows((0, 1))
-        for t in range(2, T):
-            widen(2, 0, 2 * t - 4)
-            widen(2, 0, 2 * t - 3)
-            quantize_rows((0, t))
-        stage1(range(UNITS), range(SPLIT))
-        weave(2, 0, "s")
-        for t in range(T):
-            widen(2, 1, t)
-        turn_pair(1, 0)
-        stage1(range(UNITS), range(SPLIT, T))
-        weave(2, 1, W3[2])
-        for t in range(T):
-            widen(3, 0, t)
-        quantize_factor(2, 0)
-        for t in range(T):
-            widen(3, 1, t)
-        quantize_factor(2, 1)
-        weave(3, 0, W3[0])
-        weave(3, 1, W3[1])
-        for i in range(UNITS):
-            square(i)
-        quantize_factor(3, 0)
-        quantize_factor(3, 1)
-        quantize_rows((1, 0))
-        quantize_rows((1, 1))
-        for b in range(2):
-            turn(("cum", b))
-            group(("cum", b), COPY_ENG["cum"][b])
+        quantize_factor(1, 0)
+        quantize_rows((0, 2))
+        weave(1, 1)
+        quantize_rows((0, 3))
+        quantize_factor(1, 1)
         last = len(ORDER) - 1
         per = 2 * UNITS
-        turns = {TURN0 + TURN_STEP * n: divmod(3 + n, 2) for n in range(2 * V - 3)}
-        for i in range(UNITS, STEPS + LAG - UNITS):
+        turns = {2: (1, (0, 1)), 4: ("cum", (0, 1)), 6: (1, (2, 3))}
+        if LONG:
+            turns.update({TURN0 + TURN_STEP * n: (2 + n, range(T)) for n in range(2)})
+        else:
+            turns.update({TURN0 + TURN_STEP * n: (2 + n // 2, (n % 2 * 2, n % 2 * 2 + 1)) for n in range(4)})
+        for i in range(STEPS):
             k, a = divmod(i, UNITS)
             if i in turns:
-                turn_pair(*turns[i])
-            if i == per:
+                turn_run(*turns[i])
+            if i in (0, per):
                 stage1([i, i + 1])
                 square(i)
                 square(i + 1)
-            elif i != per + 1 and i < STEPS:
+            elif i not in (1, per + 1) and i < STEPS:
                 stage1([i])
                 square(i)
-            if a == 0 and k <= last:
+            if i < 4:
+                c, g = 2 + i // 2, i % 2
+                if i > 0:
+                    if (c, g) not in planes:
+                        widen_all(c, g, PREP_ENG[i])
+                    quantize_factor(2 + (i - 1) // 2, (i - 1) % 2)
+                weave(c, g)
+            if i == 4:
+                quantize_factor(3, 1)
+            for lead in (SORT_LEAD, SORT_LEAD - 1):
+                if i + lead in turns and turns[i + lead][0] in SORTED:
+                    v, slots = turns[i + lead]
+                    for t in (slots[:2] if lead == SORT_LEAD else slots[2:]):
+                        sort((v, t))
+            if a == 0 and 1 <= k <= last:
                 quantize_power(k - 1, 0, HALF)
-            if i == UNITS:
-                quantize_rows(("cum", 0))
-                quantize_rows(("cum", 1))
             if i == STEPS - 2:
                 quantize_power(last, 0, HALF // 2)
-            if i == STEPS:
-                quantize_power(last, HALF // 2, HALF // 2)
             w, n = divmod(i - LAG - UNITS - NORM_LAG, per)
             if 0 <= w < V - 1 and n in (0, 2):
                 add_halves(w, n, n + 2)
@@ -335,33 +323,50 @@ def tile_forecast_variance_shares_s7_kernel(tc, psi, factor_bytes, factor_scale,
             if 0 <= w < V - 1 and n in (0, 2):
                 invert(w, n, n + 2)
             if i - 1 in turns:
-                v, b = turns[i - 1]
-                quantize_rows((v, 2 * b))
-                quantize_rows((v, 2 * b + 1))
-            if i + SORT_LEAD in turns and turns[i + SORT_LEAD][0] in SORTED:
-                v, b = turns[i + SORT_LEAD]
-                sort((v, 2 * b))
-                sort((v, 2 * b + 1))
+                v, slots = turns[i - 1]
+                for t in slots[:2]:
+                    quantize_rows((v, t))
+            if i - 2 in turns:
+                v, slots = turns[i - 2]
+                for t in slots[2:]:
+                    quantize_rows((v, t))
             if 0 <= w < V - 1 and FIN <= n < FIN + T:
                 finish(w, n - FIN)
         v = V - 1
+        quantize_power(last, HALF // 2, HALF // 2)
         late = range((STEPS - LAG) % UNITS, T)
-        for m in late:
-            stage2(bank()[:], last - 1, 0, m)
-        for part in range(2):
-            for b in range(2):
-                ps = bank()
-                for e in range(2):
-                    stage2(ps[:, e * 256:(e + 1) * 256], last, part * 256, 2 * b + e)
+        for b in range(2):
+            for m in (2 * b, 2 * b + 1):
+                if m in late:
+                    stage2(bank()[:], last - 1, 0, m)
+            ps = bank()
+            for e in range(2):
+                stage2(ps[:, e * 256:(e + 1) * 256], last, 0, 2 * b + e)
+        for b in range(2):
+            ps = bank()
+            for e in range(2):
+                stage2(ps[:, e * 256:(e + 1) * 256], last, 256, 2 * b + e)
         for m in range(T):
             if m in late:
                 read(last - 1, 0, m, "s", 0)
             read(last, 0, m, "s", 1)
+
+        def add_parts(m):
+            nc.vector.tensor_tensor(sums[v][:, 2 * T + m:2 * T + m + 1], sums[v][:, m:m + 1], sums[v][:, T + m:T + m + 1], op=ALU.add)
+
+        add_parts(0)
+        for m in range(T):
+            if (v - 1, m) not in finished:
+                finish(v - 1, m)
+        add_parts(1)
         for b in range(2):
-            nc.vector.tensor_tensor(sums[v][:, 2 * T + 2 * b:2 * T + 2 * b + 2], sums[v][:, 2 * b:2 * b + 2], sums[v][:, T + 2 * b:T + 2 * b + 2], op=ALU.add)
             for m in (2 * b, 2 * b + 1):
                 read(last, 256, m, "v", 3, 2)
             for m in (2 * b, 2 * b + 1):
                 invert(v, m, m + 1, sums[v][:, 3 * T + m:3 * T + m + 1])
             finish(v, 2 * b)
+            if b == 0:
+                add_parts(2)
             finish(v, 2 * b + 1)
+            if b == 0:
+                add_parts(3)

@@ -23,30 +23,34 @@ HALF = 512
 UNITS = HALF // UNIT
 CHUNK = 256
 CHUNKS = J // CHUNK
-ORDER = [(v, h) for v in range(V) for h in range(2)]
+ORDER = [(0, 0), (1, 0), (0, 1), (1, 1), (2, 0), (2, 1), (3, 0), (3, 1)]
 STEPS = len(ORDER) * UNITS
 LAG = 6
 WARM = 3
-SORTED = (2, 3)
-TURN0 = 9
+SORTED = ((2, 0), (2, 2), (3, 0), (3, 2))
+TURN0 = 10
 TURN_STEP = 2
 LONG = 0
-WP = (2, 1, 1)
-WT = (1, 1, 0, 0)
+WP = (2, 0)
+WT = (0, 1, 0, 0)
 SPLIT = 2
 ON_G = ()
 FIN = 1
 SORT_LEAD = 3
 W3 = "vvs"
 RUN = 4
-S20 = 2
+S20 = 4
+S10 = 3
+RF = (1, 1, 2, 3)
+PREP0 = 3
+PREP_AT = (1, 2, 3, 5)
+H1_FIRST = 2
 E20 = "s"
 E21 = "s"
 PREP_ENG = "vvvv"
-PREP_AT = {2: 0, 3: 3}
 HEAD_INTER = "s"
-COPY_ENG = {1: "ssss", 2: "ssss", 3: "ssss", "cum": "ss"}
-READ_ENG = ["vsvs"] * 7
+COPY_ENG = {1: "ssss", 2: "svsv", 3: "svsv", "cum": "ss"}
+READ_ENG = ["vsvs"] * 4 + ["ssss", "", "vs"]
 NORM_LAG = 2
 PREP3 = 5
 PQ_AT = 0
@@ -75,11 +79,13 @@ def tile_forecast_variance_shares_s7_kernel(tc, psi, factor_bytes, factor_scale,
                             in_=factor_scale.rearrange("(g p t) o -> p g (t o)", p=P, t=T))
         f_src = factor_bytes.rearrange("(g p t) n -> g p t n", p=P, t=T)
         f_bytes = {}
-        for g in range(G):
-            for b in range(2):
-                f_bytes[g, b] = keep.tile([P, 2, J], U8, name="f_bytes%d%d" % (g, b))
-                nc.sync.dma_start(out=f_bytes[g, b][:], in_=f_src[g][:, 2 * b:2 * b + 2, :])
 
+        def load_factor(h, passes=range(G)):
+            for g in passes:
+                f_bytes[h, g] = keep.tile([P, T, HALF], U8, name="f_bytes%d%d" % (h, g))
+                nc.sync.dma_start(out=f_bytes[h, g][:], in_=f_src[g][:, :, h * HALF:(h + 1) * HALF])
+
+        load_factor(0)
         rows = {}
 
         def load_psi(v, t0, n):
@@ -91,11 +97,17 @@ def tile_forecast_variance_shares_s7_kernel(tc, psi, factor_bytes, factor_scale,
         for t in range(T):
             load_psi(0, t, 1)
         load_psi(1, 0, 2)
+        if H1_FIRST == 2:
+            load_factor(1, (0,))
         load_psi(1, 2, 2)
+        if H1_FIRST:
+            load_factor(1, (1,) if H1_FIRST == 2 else (0, 1))
         cum_rows = keep.tile([P, T * H], BF16, name="cum_rows")
         nc.sync.dma_start(out=cum_rows[:], in_=cum.rearrange("(p t) h -> p (t h)", t=T))
         rows["cum", 0] = cum_rows[:, :K]
         rows["cum", 1] = cum_rows[:, K:]
+        if not H1_FIRST:
+            load_factor(1)
         load_psi(2, 0, T)
         load_psi(3, 0, T)
 
@@ -147,7 +159,7 @@ def tile_forecast_variance_shares_s7_kernel(tc, psi, factor_bytes, factor_scale,
             if (c, g) not in planes:
                 planes[c, g] = keep.tile([P, T * CHUNK], BF16, name="planes%d%d" % (c, g))
             dst = planes[c, g][:, t * CHUNK:(t + 1) * CHUNK]
-            src = f_bytes[g, t // 2][:, t % 2, c * CHUNK:(c + 1) * CHUNK].bitcast(FP8)
+            src = f_bytes[c // 2, g][:, t, c % 2 * CHUNK:(c % 2 + 1) * CHUNK].bitcast(FP8)
             scale = f_scale[:, g * T + t:g * T + t + 1]
             if eng == "s":
                 nc.scalar.activation(dst, src, ACT.Copy, scale=scale)
@@ -244,94 +256,121 @@ def tile_forecast_variance_shares_s7_kernel(tc, psi, factor_bytes, factor_scale,
         if WARM:
             spare = bank()
         warm(WARM)
-        for b in range(2):
-            for t in (2 * b, 2 * b + 1):
-                widen(0, 0, t, "v")
-                widen(1, 0, t, "s")
-            warm(WP[b], planes[0, 0][:, b * HALF:(b + 1) * HALF])
-        widen(0, 1, 0, "v")
-        widen(0, 1, 1, "v")
-        warm(WP[2], planes[0, 1][:, :HALF])
+        widen_all(0, 0, "v")
+        for t in range(S10):
+            widen(1, 0, t, "s")
+        warm(WP[0], planes[0, 0][:, :HALF])
+        for t in range(S10, T):
+            widen(1, 0, t, "v")
         weave(0, 0)
-        widen(0, 1, 2, "v")
-        widen(0, 1, 3, "v")
-        widen_all(1, 1, "s")
+        warm(WP[1], woven[0, 0][:, :HALF])
+        widen_all(0, 1, "s")
+        widen_all(1, 1, "v")
         quantize_factor(0, 0)
         weave(0, 1)
-        weave(1, 0)
-        quantize_factor(0, 1)
-        for t in range(S20):
-            widen(2, 0, t, "s")
         for t in range(T):
             turn((0, t))
             group((0, t), "s")
             warm(WT[t])
-        for t in range(S20, T):
-            widen(2, 0, t, E20)
-        if E21 == "s":
-            widen_all(2, 1, "s")
+        for t in range(S20):
+            widen(2, 0, t, "s")
         quantize_rows((0, 0))
+        quantize_factor(0, 1)
         quantize_rows((0, 1))
-        quantize_factor(1, 0)
-        quantize_rows((0, 2))
         weave(1, 1)
+        quantize_rows((0, 2))
         quantize_rows((0, 3))
+        weave(1, 0)
         quantize_factor(1, 1)
+        if (1, 2) in SORTED:
+            sort((1, 2))
+        quantize_factor(1, 0)
+        if (1, 2) in SORTED:
+            sort((1, 3))
+        for t in range(S20, T):
+            widen(2, 0, t, "v")
         last = len(ORDER) - 1
-        per = 2 * UNITS
-        turns = {2: (1, (0, 1)), 4: ("cum", (0, 1)), 6: (1, (2, 3))}
-        if LONG:
-            turns.update({TURN0 + TURN_STEP * n: (2 + n, range(T)) for n in range(2)})
-        else:
-            turns.update({TURN0 + TURN_STEP * n: (2 + n // 2, (n % 2 * 2, n % 2 * 2 + 1)) for n in range(4)})
+        turns = {2: (1, (0, 1)), 3: (1, (2, 3)), 4: ("cum", (0, 1))}
+        turns.update({TURN0 + TURN_STEP * n: (2 + n // 2, (n % 2 * 2, n % 2 * 2 + 1)) for n in range(4)})
+        ends = {UNITS * ORDER.index((v, 1)): v for v in range(V - 2)}
+        rush = UNITS * (last - 2) + LAG
         for i in range(STEPS):
             k, a = divmod(i, UNITS)
             if i in turns:
                 turn_run(*turns[i])
-            if i in (0, per):
+            if i in (0, UNITS):
                 stage1([i, i + 1])
                 square(i)
                 square(i + 1)
-            elif i not in (1, per + 1) and i < STEPS:
+            elif i not in (1, UNITS + 1):
                 stage1([i])
                 square(i)
-            if i < 4:
-                c, g = 2 + i // 2, i % 2
-                if i > 0:
-                    if (c, g) not in planes:
-                        widen_all(c, g, PREP_ENG[i])
-                    quantize_factor(2 + (i - 1) // 2, (i - 1) % 2)
-                weave(c, g)
-            if i == 4:
-                quantize_factor(3, 1)
-            for lead in (SORT_LEAD, SORT_LEAD - 1):
-                if i + lead in turns and turns[i + lead][0] in SORTED:
-                    v, slots = turns[i + lead]
-                    for t in (slots[:2] if lead == SORT_LEAD else slots[2:]):
+            if i <= UNITS:
+                for j in range(4):
+                    if PREP_AT[j] == i:
+                        if (2 + j // 2, j % 2) not in planes:
+                            widen_all(2 + j // 2, j % 2, "v")
+                        if j > 0 and PREP_AT[j - 1] == i - 1:
+                            quantize_factor(2 + (j - 1) // 2, (j - 1) % 2)
+                        weave(2 + j // 2, j % 2)
+                    elif PREP_AT[j] == i - 1 and i not in PREP_AT:
+                        quantize_factor(2 + j // 2, j % 2)
+            if i + SORT_LEAD in turns and i + SORT_LEAD > 3:
+                v, slots = turns[i + SORT_LEAD]
+                for t in slots:
+                    if (v, slots[0]) in SORTED:
                         sort((v, t))
+            if i < UNITS and i in turns:
+                for t in turns[i][1]:
+                    quantize_rows((1, t))
+            if i == rush + 1:
+                invert(V - 2, 0, 2, sums[V - 2][:, T:T + 2])
+            if i == rush + 2:
+                add_halves(V - 2, 2, 4)
             if a == 0 and 1 <= k <= last:
                 quantize_power(k - 1, 0, HALF)
+            if i == rush + 2:
+                invert(V - 2, 2, 4)
             if i == STEPS - 2:
                 quantize_power(last, 0, HALF // 2)
-            w, n = divmod(i - LAG - UNITS - NORM_LAG, per)
-            if 0 <= w < V - 1 and n in (0, 2):
-                add_halves(w, n, n + 2)
+            closing = [(ends[i - LAG - NORM_LAG - j], j) for j in range(T + FIN) if i - LAG - NORM_LAG - j in ends]
+            for w, n in closing:
+                if n in (0, 2):
+                    add_halves(w, n, n + 2)
             q, m = divmod(i - LAG, UNITS)
-            if 0 <= q < last and i < STEPS:
+            if q == last - 2:
+                for n2 in range(2 * m, min(2 * m + 2, T)):
+                    stage2(bank()[:], q, 0, n2)
+                    if n2 < 2:
+                        read(q, 0, n2, "v", 1, 0)
+                    else:
+                        read(q, 0, n2, "s", 1)
+                for n2 in range(T):
+                    if RF[n2] == m:
+                        finish(V - 2, n2)
+            elif 0 <= q < last:
                 stage2(bank()[:], q, 0, m)
                 read(q, 0, m, READ_ENG[q][m], ORDER[q][1])
-            if 0 <= w < V - 1 and n in (0, 2):
-                invert(w, n, n + 2)
-            if i - 1 in turns:
+            for w, n in closing:
+                if n in (0, 2):
+                    invert(w, n, n + 2)
+            if i - 1 in turns and i > UNITS:
                 v, slots = turns[i - 1]
-                for t in slots[:2]:
+                for t in slots:
                     quantize_rows((v, t))
-            if i - 2 in turns:
-                v, slots = turns[i - 2]
-                for t in slots[2:]:
-                    quantize_rows((v, t))
-            if 0 <= w < V - 1 and FIN <= n < FIN + T:
-                finish(w, n - FIN)
+            if i > UNITS:
+                for j in range(4):
+                    if PREP_AT[j] == i:
+                        if (2 + j // 2, j % 2) not in planes:
+                            widen_all(2 + j // 2, j % 2, "v")
+                        if j > 0 and PREP_AT[j - 1] == i - 1:
+                            quantize_factor(2 + (j - 1) // 2, (j - 1) % 2)
+                        weave(2 + j // 2, j % 2)
+                    elif PREP_AT[j] == i - 1 and i not in PREP_AT:
+                        quantize_factor(2 + j // 2, j % 2)
+            for w, n in closing:
+                if FIN <= n:
+                    finish(w, n - FIN)
         v = V - 1
         quantize_power(last, HALF // 2, HALF // 2)
         late = range((STEPS - LAG) % UNITS, T)

@@ -41,7 +41,15 @@ W3 = "vvs"
 RUN = 4
 S20 = 4
 S10 = 3
-RF = (1, 1, 2, 3)
+RF = (2, 3, 4, 5)
+RF2 = (1, 2, 4, 9)
+RUSH = 1
+LONG1 = 0
+SPLIT0 = 0
+QA_FIRST = 1
+INV0 = 1
+ADD_AT = 3
+ADD2 = 3
 PREP0 = 3
 PREP_AT = (1, 2, 3, 5)
 H1_FIRST = 2
@@ -49,8 +57,8 @@ E20 = "s"
 E21 = "s"
 PREP_ENG = "vvvv"
 HEAD_INTER = "s"
-COPY_ENG = {1: "ssss", 2: "svsv", 3: "svsv", "cum": "ss"}
-READ_ENG = ["vsvs"] * 4 + ["ssss", "", "vs"]
+COPY_ENG = {1: "ssss", 2: "svsv", 3: "ssss", "cum": "ss"}
+READ_ENG = ["vsvs", "vsvs", "", "", "vsvs"]
 NORM_LAG = 2
 PREP3 = 5
 PQ_AT = 0
@@ -236,12 +244,12 @@ def tile_forecast_variance_shares_s7_kernel(tc, psi, factor_bytes, factor_scale,
 
         finished = set()
 
-        def finish(v, m):
+        def finish(v, m, c0=0, c1=J):
             finished.add((v, m))
-            row = res[v][:, m * J:(m + 1) * J]
+            row = res[v][:, m * J + c0:m * J + c1]
             eng = nc.gpsimd if (v, m) in ON_G else nc.vector
             eng.tensor_scalar(row, row, recs[v][:, T + m:T + m + 1], float(J), op0=ALU.mult, op1=ALU.mult)
-            nc.sync.dma_start(out=out[v].rearrange("(p t) n -> p t n", t=T)[:, m, :], in_=row)
+            nc.sync.dma_start(out=out[v].rearrange("(p t) n -> p t n", t=T)[:, m, c0:c1], in_=row)
 
         def warm(n, src=None):
             for i in range(n if WARM else 0):
@@ -291,9 +299,13 @@ def tile_forecast_variance_shares_s7_kernel(tc, psi, factor_bytes, factor_scale,
             widen(2, 0, t, "v")
         last = len(ORDER) - 1
         turns = {2: (1, (0, 1)), 3: (1, (2, 3)), 4: ("cum", (0, 1))}
-        turns.update({TURN0 + TURN_STEP * n: (2 + n // 2, (n % 2 * 2, n % 2 * 2 + 1)) for n in range(4)})
-        ends = {UNITS * ORDER.index((v, 1)): v for v in range(V - 2)}
-        rush = UNITS * (last - 2) + LAG
+        if LONG1:
+            turns = {2: (1, (0, 1, 2, 3)), 4: ("cum", (0, 1))}
+        if LONG:
+            turns.update({TURN0 + TURN_STEP * n: (2 + n, (0, 1, 2, 3)) for n in range(2)})
+        else:
+            turns.update({TURN0 + TURN_STEP * n: (2 + n // 2, (n % 2 * 2, n % 2 * 2 + 1)) for n in range(4)})
+        pending = []
         for i in range(STEPS):
             k, a = divmod(i, UNITS)
             if i in turns:
@@ -315,48 +327,49 @@ def tile_forecast_variance_shares_s7_kernel(tc, psi, factor_bytes, factor_scale,
                         weave(2 + j // 2, j % 2)
                     elif PREP_AT[j] == i - 1 and i not in PREP_AT:
                         quantize_factor(2 + j // 2, j % 2)
-            if i + SORT_LEAD in turns and i + SORT_LEAD > 3:
-                v, slots = turns[i + SORT_LEAD]
-                for t in slots:
-                    if (v, slots[0]) in SORTED:
-                        sort((v, t))
-            if i < UNITS and i in turns:
-                for t in turns[i][1]:
-                    quantize_rows((1, t))
-            if i == rush + 1:
-                invert(V - 2, 0, 2, sums[V - 2][:, T:T + 2])
-            if i == rush + 2:
-                add_halves(V - 2, 2, 4)
+            for lead in (SORT_LEAD, SORT_LEAD - 1):
+                if i + lead in turns and i + lead > 3:
+                    v, slots = turns[i + lead]
+                    for t in (slots[:2] if lead == SORT_LEAD else slots[2:]):
+                        if (v, slots[0]) in SORTED:
+                            sort((v, t))
+            if i in (2, 3):
+                quantize_rows((1, 2 * i - 4))
+                quantize_rows((1, 2 * i - 3))
+            q, m = divmod(i - LAG, UNITS)
+            closing = [(w, i - LAG - UNITS * ORDER.index((w, 1))) for w in range(V - 1)]
+            for w, n in closing:
+                if n == INV0:
+                    invert(w, 0, 2, sums[w][:, T:T + 2])
+                if n == ADD_AT:
+                    add_halves(w, 2, 4)
             if a == 0 and 1 <= k <= last:
                 quantize_power(k - 1, 0, HALF)
-            if i == rush + 2:
-                invert(V - 2, 2, 4)
-            if i == STEPS - 2:
+            for w, n in closing:
+                if n == ADD_AT:
+                    invert(w, 2, 4)
+            if i == STEPS - 2 and QA_FIRST:
                 quantize_power(last, 0, HALF // 2)
-            closing = [(ends[i - LAG - NORM_LAG - j], j) for j in range(T + FIN) if i - LAG - NORM_LAG - j in ends]
-            for w, n in closing:
-                if n in (0, 2):
-                    add_halves(w, n, n + 2)
-            q, m = divmod(i - LAG, UNITS)
-            if q == last - 2:
-                for n2 in range(2 * m, min(2 * m + 2, T)):
-                    stage2(bank()[:], q, 0, n2)
-                    if n2 < 2:
-                        read(q, 0, n2, "v", 1, 0)
+            if 0 <= q < last - 1:
+                if ORDER[q][1] == 0:
+                    due = [m]
+                else:
+                    due = [(0, 1), (2, 3), (), ()][m] if RUSH or q == last - 2 else [m]
+                for n in due:
+                    stage2(bank()[:], q, 0, n)
+                    if ORDER[q][1] == 0:
+                        read(q, 0, n, READ_ENG[q][n], 0)
+                    elif n < 2:
+                        read(q, 0, n, "v", 1, 0)
                     else:
-                        read(q, 0, n2, "s", 1)
-                for n2 in range(T):
-                    if RF[n2] == m:
-                        finish(V - 2, n2)
-            elif 0 <= q < last:
-                stage2(bank()[:], q, 0, m)
-                read(q, 0, m, READ_ENG[q][m], ORDER[q][1])
-            for w, n in closing:
-                if n in (0, 2):
-                    invert(w, n, n + 2)
+                        read(q, 0, n, "s", 1)
             if i - 1 in turns and i > UNITS:
                 v, slots = turns[i - 1]
-                for t in slots:
+                for t in slots[:2]:
+                    quantize_rows((v, t))
+            if i - 2 in turns and i > UNITS:
+                v, slots = turns[i - 2]
+                for t in slots[2:]:
                     quantize_rows((v, t))
             if i > UNITS:
                 for j in range(4):
@@ -369,43 +382,53 @@ def tile_forecast_variance_shares_s7_kernel(tc, psi, factor_bytes, factor_scale,
                     elif PREP_AT[j] == i - 1 and i not in PREP_AT:
                         quantize_factor(2 + j // 2, j % 2)
             for w, n in closing:
-                if FIN <= n:
-                    finish(w, n - FIN)
+                if n == 2:
+                    pending.extend((w, j) for j in range(T))
+            if pending and i < STEPS - 1 and all(n != 0 for w, n in closing):
+                finish(*pending[0])
+                pending.remove(pending[0])
+            if i == STEPS - 2 and not QA_FIRST:
+                quantize_power(last, 0, HALF // 2)
         v = V - 1
         quantize_power(last, HALF // 2, HALF // 2)
-        late = range((STEPS - LAG) % UNITS, T)
         for b in range(2):
-            for m in (2 * b, 2 * b + 1):
-                if m in late:
-                    stage2(bank()[:], last - 1, 0, m)
+            stage2(bank()[:], last - 1, 0, 2 * b)
             ps = bank()
             for e in range(2):
                 stage2(ps[:, e * 256:(e + 1) * 256], last, 0, 2 * b + e)
-        for b in range(2):
+            stage2(bank()[:], last - 1, 0, 2 * b + 1)
             ps = bank()
             for e in range(2):
                 stage2(ps[:, e * 256:(e + 1) * 256], last, 256, 2 * b + e)
-        for m in range(T):
-            if m in late:
+            for m in (2 * b, 2 * b + 1):
                 read(last - 1, 0, m, "s", 0)
-            read(last, 0, m, "s", 1)
+                read(last, 0, m, "s", 1)
+                if b == 1:
+                    read(last, 256, m, "s", 2)
 
         def add_parts(m):
-            nc.vector.tensor_tensor(sums[v][:, 2 * T + m:2 * T + m + 1], sums[v][:, m:m + 1], sums[v][:, T + m:T + m + 1], op=ALU.add)
+            nc.vector.tensor_reduce(recs[v][:, m:m + 1], sums[v][:, :3 * T].rearrange("p (h m) -> p m h", h=3)[:, m, :],
+                                    axis=mybir.AxisListType.X, op=ALU.add)
 
-        add_parts(0)
         for m in range(T):
             if (v - 1, m) not in finished:
                 finish(v - 1, m)
+        add_halves(v, 0, 1)
+        nc.vector.tensor_scalar(res[v][:, HALF + 256:J], var[last, 256, 0], 1.0, recs[v][:, 0:1], op0=ALU.mult, op1=ALU.add,
+                                accum_out=sums[v][:, 3 * T:3 * T + 1])
+        read(last, 256, 1, "v", 2)
+        invert(v, 0, 1, sums[v][:, 3 * T:3 * T + 1])
+        if SPLIT0:
+            finish(v, 0, 0, SPLIT0)
+            finish(v, 0, SPLIT0, J)
+        else:
+            finish(v, 0)
         add_parts(1)
-        for b in range(2):
-            for m in (2 * b, 2 * b + 1):
-                read(last, 256, m, "v", 3, 2)
-            for m in (2 * b, 2 * b + 1):
-                invert(v, m, m + 1, sums[v][:, 3 * T + m:3 * T + m + 1])
-            finish(v, 2 * b)
-            if b == 0:
-                add_parts(2)
-            finish(v, 2 * b + 1)
-            if b == 0:
-                add_parts(3)
+        add_parts(2)
+        invert(v, 1, 2)
+        invert(v, 2, 3)
+        finish(v, 1)
+        add_parts(3)
+        finish(v, 2)
+        invert(v, 3, 4)
+        finish(v, 3)

@@ -111,7 +111,7 @@ def tile_forecast_variance_shares_s7_kernel(tc, psi, factor_bytes, factor_scale,
         if H1_FIRST:
             load_factor(1, (1,) if H1_FIRST == 2 else (0, 1))
         cum_rows = keep.tile([P, T * H], BF16, name="cum_rows")
-        nc.sync.dma_start(out=cum_rows[:], in_=cum.rearrange("(p t) h -> p (t h)", t=T))
+        nc.sync.dma_start(out=cum_rows[:].rearrange("p (m h) -> p m h", m=T), in_=cum.rearrange("(m p) h -> p m h", p=P))
         rows["cum", 0] = cum_rows[:, :K]
         rows["cum", 1] = cum_rows[:, K:]
         if not H1_FIRST:
@@ -249,7 +249,7 @@ def tile_forecast_variance_shares_s7_kernel(tc, psi, factor_bytes, factor_scale,
             row = res[v][:, m * J + c0:m * J + c1]
             eng = nc.gpsimd if (v, m) in ON_G else nc.vector
             eng.tensor_scalar(row, row, recs[v][:, T + m:T + m + 1], float(J), op0=ALU.mult, op1=ALU.mult)
-            nc.sync.dma_start(out=out[v].rearrange("(p t) n -> p t n", t=T)[:, m, c0:c1], in_=row)
+            nc.sync.dma_start(out=out[v][m * P:(m + 1) * P, c0:c1], in_=row)
 
         def warm(n, src=None):
             for i in range(n if WARM else 0):

@@ -18,83 +18,44 @@ ALU = mybir.AluOpType
 P = 128
 T = 4
 G = K // (P * T)
+M = R // P
 UNIT = 128
 HALF = 512
 UNITS = HALF // UNIT
 CHUNK = 256
-CHUNKS = J // CHUNK
+RUN = 4
 ORDER = [(0, 0), (1, 0), (0, 1), (1, 1), (2, 0), (2, 1), (3, 0), (3, 1)]
 STEPS = len(ORDER) * UNITS
 LAG = 6
-WARM = 3
-SORTED = ((2, 0), (2, 2), (3, 0), (3, 2))
-TURN0 = 10
-TURN_STEP = 2
-LONG = 0
-WP = (2, 0)
-WT = (0, 1, 0, 0)
-SPLIT = 2
-ON_G = ()
-FIN = 1
+LATE_TURNS = 10
 SORT_LEAD = 3
-W3 = "vvs"
-RUN = 4
-S20 = 4
-S10 = 3
-RF = (2, 3, 4, 5)
-RF2 = (1, 2, 4, 9)
-RUSH = 1
-LONG1 = 0
-SPLIT0 = 0
-QA_FIRST = 1
-INV0 = 1
-ADD_AT = 3
-ADD2 = 3
-PREP0 = 3
-PREP_AT = (1, 2, 3, 5)
-H1_FIRST = 2
-E20 = "s"
-E21 = "s"
-PREP_ENG = "vvvv"
-HEAD_INTER = "s"
-COPY_ENG = {1: "ssss", 2: "svsv", 3: "ssss", "cum": "ss"}
-READ_ENG = ["vsvs", "vsvs", "", "", "vsvs"]
-NORM_LAG = 2
-PREP3 = 5
-PQ_AT = 0
-WARM2 = 2
-WARM2_AT = 1
+SCALAR_PIECES = ((1, 0), (1, 1), (2, 0))
+LATE_PIECES = {1: (2, 0), 2: (2, 1), 3: (3, 0), 5: (3, 1)}
 
 
 def tile_forecast_variance_shares_s7_kernel(tc, psi, factor_bytes, factor_scale, cum, out):
     nc = tc.nc
     with ExitStack() as ctx:
         keep = ctx.enter_context(tc.tile_pool(name="keep", bufs=1))
-        work = ctx.enter_context(tc.tile_pool(name="work", bufs=3))
+        work = ctx.enter_context(tc.tile_pool(name="work", bufs=4))
         outs = ctx.enter_context(tc.tile_pool(name="outs", bufs=3))
         psum = ctx.enter_context(tc.psum_pool(name="psum", bufs=8))
 
         ident = keep.tile([P, P], F32, name="ident")
         make_identity(nc, ident[:])
-        if WARM:
-            zeros = keep.tile([P, HALF], BF16, name="zeros")
-            nc.vector.memset(zeros[:], 0.0)
 
         ctx.enter_context(tc.manual_schedule())
 
         f_scale = keep.tile([P, G * T], F32, name="f_scale")
         nc.scalar.dma_start(out=f_scale[:].rearrange("p (g t) -> p g t", g=G),
                             in_=factor_scale.rearrange("(g p t) o -> p g (t o)", p=P, t=T))
-        f_src = factor_bytes.rearrange("(g p t) n -> g p t n", p=P, t=T)
         f_bytes = {}
-
-        def load_factor(h, passes=range(G)):
-            for g in passes:
-                f_bytes[h, g] = keep.tile([P, T, HALF], U8, name="f_bytes%d%d" % (h, g))
-                nc.sync.dma_start(out=f_bytes[h, g][:], in_=f_src[g][:, :, h * HALF:(h + 1) * HALF])
-
-        load_factor(0)
         rows = {}
+
+        def load_factor(h, g):
+            f_bytes[h, g] = keep.tile([P, T, HALF], U8, name="f_bytes%d%d" % (h, g))
+            nc.sync.dma_start(out=f_bytes[h, g][:],
+                              in_=factor_bytes.rearrange("(g p t) n -> g p t n", p=P, t=T)[g][:, :, h * HALF:(h + 1) * HALF])
 
         def load_psi(v, t0, n):
             tile = keep.tile([P, n * K], BF16, name="psi_rows%d%d" % (v, t0))
@@ -102,54 +63,25 @@ def tile_forecast_variance_shares_s7_kernel(tc, psi, factor_bytes, factor_scale,
             for i in range(n):
                 rows[v, t0 + i] = tile[:, i * K:(i + 1) * K]
 
+        load_factor(0, 0)
+        load_factor(0, 1)
         for t in range(T):
             load_psi(0, t, 1)
         load_psi(1, 0, 2)
-        if H1_FIRST == 2:
-            load_factor(1, (0,))
+        load_factor(1, 0)
         load_psi(1, 2, 2)
-        if H1_FIRST:
-            load_factor(1, (1,) if H1_FIRST == 2 else (0, 1))
-        cum_rows = keep.tile([P, T * H], BF16, name="cum_rows")
-        nc.sync.dma_start(out=cum_rows[:].rearrange("p (m h) -> p m h", m=T), in_=cum.rearrange("(m p) h -> p m h", p=P))
-        rows["cum", 0] = cum_rows[:, :K]
-        rows["cum", 1] = cum_rows[:, K:]
-        if not H1_FIRST:
-            load_factor(1)
+        load_factor(1, 1)
+        cum_rows = keep.tile([P, M * H], BF16, name="cum_rows")
+        nc.sync.dma_start(out=cum_rows[:].rearrange("p (m h) -> p m h", m=M), in_=cum.rearrange("(m p) h -> p m h", p=P))
+        rows["cum", 0] = cum_rows[:, :2 * H]
+        rows["cum", 1] = cum_rows[:, 2 * H:]
         load_psi(2, 0, T)
         load_psi(3, 0, T)
 
         def bank():
             return psum.tile([P, HALF], F32, name="bank")
 
-        turned, grouped, codes, scales, ordered = {}, {}, {}, {}, {}
-
-        def sort(key):
-            tile = work.tile([P, K // 2], F32, name="ordered", bufs=4)
-            nc.vector.tensor_copy(tile[:].rearrange("p (g u r) -> p g u r", g=2, u=2),
-                                  rows[key].bitcast(F32).rearrange("p (g r u) -> p g u r", g=2, u=2))
-            ordered[key] = tile
-
-        def turn(key):
-            ps = bank()
-            for g in range(2):
-                for u in range(2):
-                    if key in ordered:
-                        src = ordered[key][:, (2 * g + u) * P:(2 * g + u + 1) * P]
-                    else:
-                        src = rows[key].bitcast(F32)[:, 256 * g + u:256 * (g + 1):2]
-                    nc.tensor.transpose(ps[:, (2 * g + u) * P:(2 * g + u + 1) * P], src, ident[:])
-            turned[key] = ps
-
-        def group(key, eng):
-            tile = work.tile([P, K], BF16, name="grouped", align_bytes=64, bufs=4)
-            dst = tile[:].bitcast(F32).rearrange("p (g r u) -> p g r u", g=2, u=2)
-            src = turned[key][:].rearrange("p (g u r) -> p g r u", g=2, u=2)
-            if eng == "s":
-                nc.scalar.copy(dst, src)
-            else:
-                nc.vector.tensor_copy(dst, src)
-            grouped[key] = tile
+        codes, scales = {}, {}
 
         def quantize(key, src):
             n = src.shape[1] // T
@@ -158,277 +90,252 @@ def tile_forecast_variance_shares_s7_kernel(tc, psi, factor_bytes, factor_scale,
             scales[key] = keep.tile([P, n], U8, name="scales_" + name, align_bytes=64)
             nc.vector.quantize_mx(out=codes[key][:].bitcast(FP8X4), scales=scales[key][:], in_=src)
 
-        def quantize_rows(key):
-            quantize(key, grouped[key][:])
+        sorted_words, turned, grouped = {}, {}, {}
 
-        planes, woven = {}, {}
+        def sort(key):
+            sorted_words[key] = work.tile([P, K // 2], F32, name="sorted_words")
+            nc.vector.tensor_copy(sorted_words[key][:].rearrange("p (g u r) -> p g u r", g=2, u=2),
+                                  rows[key].bitcast(F32).rearrange("p (g r u) -> p g u r", g=2, u=2))
 
-        def widen(c, g, t, eng):
-            if (c, g) not in planes:
-                planes[c, g] = keep.tile([P, T * CHUNK], BF16, name="planes%d%d" % (c, g))
-            dst = planes[c, g][:, t * CHUNK:(t + 1) * CHUNK]
-            src = f_bytes[c // 2, g][:, t, c % 2 * CHUNK:(c % 2 + 1) * CHUNK].bitcast(FP8)
-            scale = f_scale[:, g * T + t:g * T + t + 1]
-            if eng == "s":
-                nc.scalar.activation(dst, src, ACT.Copy, scale=scale)
+        def turn(key):
+            turned[key] = bank()
+            for g in range(2):
+                for u in range(2):
+                    cols = slice((2 * g + u) * P, (2 * g + u + 1) * P)
+                    if key in sorted_words:
+                        src = sorted_words[key][:, cols]
+                    else:
+                        src = rows[key].bitcast(F32)[:, 2 * P * g + u:2 * P * (g + 1):2]
+                    nc.tensor.transpose(turned[key][:, cols], src, ident[:])
+
+        def group(key):
+            grouped[key] = work.tile([P, K], BF16, name="grouped", align_bytes=64)
+            dst = grouped[key][:].bitcast(F32).rearrange("p (g r u) -> p g r u", g=2, u=2)
+            src = turned[key][:].rearrange("p (g u r) -> p g r u", g=2, u=2)
+            if key[0] == 2 and key[1] % 2:
+                nc.vector.tensor_copy(dst, src)
             else:
-                nc.vector.tensor_scalar(dst, src, scale, None, op0=ALU.mult)
+                nc.scalar.copy(dst, src)
 
-        def widen_all(c, g, eng):
-            for t in range(T):
-                widen(c, g, t, eng)
+        def turn_pair(keys):
+            for key in keys:
+                turn(key)
+            for key in keys:
+                group(key)
+
+        def quantize_rows(*keys):
+            for key in keys:
+                quantize(key, grouped[key][:])
+
+        widened, woven = {}, {}
+
+        def widen(c, g, slots=range(T)):
+            if (c, g) not in widened:
+                widened[c, g] = keep.tile([P, T * CHUNK], BF16, name="widened%d%d" % (c, g))
+            h, n0 = divmod(c * CHUNK, HALF)
+            for t in slots:
+                src = f_bytes[h, g][:, t, n0:n0 + CHUNK].bitcast(FP8)
+                scale = f_scale[:, g * T + t:g * T + t + 1]
+                if (c, g) in SCALAR_PIECES:
+                    nc.scalar.activation(widened[c, g][:, t * CHUNK:(t + 1) * CHUNK], src, ACT.Copy, scale=scale)
+                else:
+                    dst = widened[c, g][:].rearrange("p (b n e) -> p b n e", b=2, e=2)[:, t // 2, :, t % 2]
+                    nc.vector.tensor_scalar(dst, src, scale, None, op0=ALU.mult)
 
         def weave(c, g):
-            woven[c, g] = work.tile([P, CHUNK * T], BF16, name="woven", align_bytes=64, bufs=4)
-            nc.vector.tensor_copy(woven[c, g][:].rearrange("p (n i t) -> p n t i", t=T, i=RUN),
-                                  planes[c, g][:].rearrange("p (t n i) -> p n t i", t=T, i=RUN))
+            woven[c, g] = work.tile([P, CHUNK * T], BF16, name="woven", align_bytes=64)
+            if (c, g) in SCALAR_PIECES:
+                nc.vector.tensor_copy(woven[c, g][:].rearrange("p (n i t) -> p n t i", t=T, i=RUN),
+                                      widened[c, g][:].rearrange("p (t n i) -> p n t i", t=T, i=RUN))
+            else:
+                dst = woven[c, g][:].bitcast(F32).rearrange("p (n b) -> p n b", b=2)
+                src = widened[c, g][:].bitcast(F32).rearrange("p (b n) -> p n b", b=2)
+                if (c, g) == (2, 1):
+                    nc.scalar.copy(dst, src)
+                else:
+                    nc.vector.tensor_copy(dst, src)
 
         def quantize_factor(c, g):
             quantize(("factor", c, g), woven[c, g][:])
 
         theta, power, var, res, sums, recs = {}, {}, {}, {}, {}, {}
 
-        def stage1(steps, slots=range(T)):
+        def stage1(*steps):
             for i in steps:
-                if i not in theta:
-                    theta[i] = bank()
-            for t in slots:
+                theta[i] = bank()
+            for t in range(T):
                 for i in steps:
                     v, h = ORDER[i // UNITS]
                     c, n0 = divmod(h * HALF + i % UNITS * UNIT, CHUNK)
                     for g in range(G):
                         nc.tensor.matmul_mx(
                             out=theta[i][:, t * UNIT:(t + 1) * UNIT],
-                            lhsT=codes[v, t][:, g * P:(g + 1) * P].bitcast(FP8X4), lhsT_scale=scales[v, t][:, g * P:(g + 1) * P],
-                            rhs=codes["factor", c, g][:, n0:n0 + UNIT].bitcast(FP8X4), rhs_scale=scales["factor", c, g][:, n0:n0 + UNIT],
+                            lhsT=codes[v, t][:, g * P:(g + 1) * P].bitcast(FP8X4),
+                            lhsT_scale=scales[v, t][:, g * P:(g + 1) * P],
+                            rhs=codes["factor", c, g][:, n0:n0 + UNIT].bitcast(FP8X4),
+                            rhs_scale=scales["factor", c, g][:, n0:n0 + UNIT],
                             start=(g == 0), stop=(g == G - 1))
+            for i in steps:
+                q, a = divmod(i, UNITS)
+                if a == 0:
+                    power[q] = work.tile([P, HALF * T], BF16, name="power", align_bytes=64, bufs=3)
+                nc.scalar.activation(power[q][:, a * UNIT * T:(a + 1) * UNIT * T].rearrange("p (n t) -> p n t", t=T),
+                                     theta[i][:].rearrange("p (t n) -> p n t", t=T), ACT.Square)
 
-        def square(i):
-            k, a = divmod(i, UNITS)
-            if a == 0:
-                power[k] = work.tile([P, HALF * T], BF16, name="power", align_bytes=64)
-            nc.scalar.activation(power[k][:, a * UNIT * T:(a + 1) * UNIT * T].rearrange("p (n t) -> p n t", t=T),
-                                 theta[i][:].rearrange("p (t n) -> p n t", t=T), ACT.Square)
+        def quantize_power(q, n0=0, n=HALF):
+            quantize(("power", q, n0), power[q][:, n0 * T:(n0 + n) * T])
 
-        def quantize_power(k, n0, n):
-            quantize(("power", k, n0), power[k][:, n0 * T:(n0 + n) * T])
-
-        def stage2(ps, k, n0, m):
+        def stage2(ps, q, n0, m):
             cols = slice(m % 2 * P, (m % 2 + 1) * P)
-            nc.tensor.matmul_mx(out=ps, lhsT=codes["cum", m // 2][:, cols].bitcast(FP8X4), lhsT_scale=scales["cum", m // 2][:, cols],
-                                rhs=codes["power", k, n0][:].bitcast(FP8X4), rhs_scale=scales["power", k, n0][:],
+            nc.tensor.matmul_mx(out=ps, lhsT=codes["cum", m // 2][:, cols].bitcast(FP8X4),
+                                lhsT_scale=scales["cum", m // 2][:, cols],
+                                rhs=codes["power", q, n0][:].bitcast(FP8X4), rhs_scale=scales["power", q, n0][:],
                                 start=True, stop=True)
-            var[k, n0, m] = ps
+            var[q, n0, m] = ps
 
-        def read(k, n0, m, eng, slot, first=None):
-            v, h = ORDER[k]
+        def part(v, j, m0, m1):
+            return sums[v][:, j * M + m0:j * M + m1]
+
+        def read(q, n0, m, j, on_vector, start=None):
+            v, h = ORDER[q]
             if v not in res:
-                res[v] = outs.tile([P, T * J], F32, name="res")
-                sums[v] = keep.tile([P, T * 8], F32, name="sums%d" % v)
-                recs[v] = keep.tile([P, 2 * T], F32, name="recs%d" % v)
-            src = var[k, n0, m]
+                res[v] = outs.tile([P, M * J], F32, name="res")
+                sums[v] = keep.tile([P, 4 * M], F32, name="sums%d" % v)
+                recs[v] = keep.tile([P, 2 * M], F32, name="recs%d" % v)
+            src = var[q, n0, m]
             c0 = m * J + h * HALF + n0
             dst = res[v][:, c0:c0 + src.shape[1]]
-            acc = sums[v][:, slot * T + m:slot * T + m + 1]
-            if eng == "s":
-                nc.scalar.activation(dst, src, ACT.Copy, accum_out=acc)
+            if on_vector:
+                nc.vector.tensor_scalar(dst, src, 1.0, start, op0=ALU.mult, op1=ALU.add, accum_out=part(v, j, m, m + 1))
             else:
-                init = None if first is None else sums[v][:, first * T + m:first * T + m + 1]
-                nc.vector.tensor_scalar(dst, src, 1.0, init, op0=ALU.mult, op1=ALU.add, accum_out=acc)
+                nc.scalar.activation(dst, src, ACT.Copy, accum_out=part(v, j, m, m + 1))
 
-        def add_halves(v, m0, m1):
-            nc.vector.tensor_tensor(recs[v][:, m0:m1], sums[v][:, m0:m1], sums[v][:, T + m0:T + m1], op=ALU.add)
+        def add_two(v, m0, m1):
+            nc.vector.tensor_tensor(recs[v][:, m0:m1], part(v, 0, m0, m1), part(v, 1, m0, m1), op=ALU.add)
 
-        def invert(v, m0, m1, src=None):
-            nc.vector.reciprocal(recs[v][:, T + m0:T + m1], recs[v][:, m0:m1] if src is None else src)
+        def add_three(v, m):
+            nc.vector.tensor_reduce(recs[v][:, m:m + 1], sums[v][:, :3 * M].rearrange("p (j m) -> p m j", j=3)[:, m, :],
+                                    axis=mybir.AxisListType.X, op=ALU.add)
 
-        finished = set()
+        def invert(v, m0, m1, total):
+            nc.vector.reciprocal(recs[v][:, M + m0:M + m1], total)
 
-        def finish(v, m, c0=0, c1=J):
-            finished.add((v, m))
-            row = res[v][:, m * J + c0:m * J + c1]
-            eng = nc.gpsimd if (v, m) in ON_G else nc.vector
-            eng.tensor_scalar(row, row, recs[v][:, T + m:T + m + 1], float(J), op0=ALU.mult, op1=ALU.mult)
-            nc.sync.dma_start(out=out[v][m * P:(m + 1) * P, c0:c1], in_=row)
+        def finish(v, m):
+            row = res[v][:, m * J:(m + 1) * J]
+            nc.vector.tensor_scalar(row, row, recs[v][:, M + m:M + m + 1], float(J), op0=ALU.mult, op1=ALU.mult)
+            nc.sync.dma_start(out=out[v][m * P:(m + 1) * P, :], in_=row)
 
-        def warm(n, src=None):
-            for i in range(n if WARM else 0):
-                nc.tensor.matmul(spare[:], zeros[:, :P], zeros[:] if src is None else src, start=True, stop=True)
-
-        def turn_run(v, slots):
-            for t in slots:
-                turn((v, t))
-            for t in slots:
-                group((v, t), COPY_ENG[v][t])
-
-        if WARM:
-            spare = bank()
-        warm(WARM)
-        widen_all(0, 0, "v")
-        for t in range(S10):
-            widen(1, 0, t, "s")
-        warm(WP[0], planes[0, 0][:, :HALF])
-        for t in range(S10, T):
-            widen(1, 0, t, "v")
+        widen(0, 0)
+        widen(1, 0)
+        widen(0, 1, range(2))
         weave(0, 0)
-        warm(WP[1], woven[0, 0][:, :HALF])
-        widen_all(0, 1, "s")
-        widen_all(1, 1, "v")
+        widen(0, 1, range(2, T))
+        widen(1, 1)
         quantize_factor(0, 0)
         weave(0, 1)
+        weave(1, 0)
         for t in range(T):
             turn((0, t))
-            group((0, t), "s")
-            warm(WT[t])
-        for t in range(S20):
-            widen(2, 0, t, "s")
+            group((0, t))
+        widen(2, 0)
         quantize_rows((0, 0))
         quantize_factor(0, 1)
-        quantize_rows((0, 1))
-        weave(1, 1)
-        quantize_rows((0, 2))
-        quantize_rows((0, 3))
-        weave(1, 0)
-        quantize_factor(1, 1)
-        if (1, 2) in SORTED:
-            sort((1, 2))
+        quantize_rows((0, 1), (0, 2))
         quantize_factor(1, 0)
-        if (1, 2) in SORTED:
-            sort((1, 3))
-        for t in range(S20, T):
-            widen(2, 0, t, "v")
+        quantize_rows((0, 3))
+        weave(1, 1)
+        quantize_factor(1, 1)
+
+        turns = {2: ((1, 0), (1, 1)), 3: ((1, 2), (1, 3)), 4: (("cum", 0), ("cum", 1))}
+        for n in range(2 * (V - 2)):
+            v, b = divmod(n, 2)
+            turns[LATE_TURNS + 2 * n] = ((2 + v, 2 * b), (2 + v, 2 * b + 1))
         last = len(ORDER) - 1
-        turns = {2: (1, (0, 1)), 3: (1, (2, 3)), 4: ("cum", (0, 1))}
-        if LONG1:
-            turns = {2: (1, (0, 1, 2, 3)), 4: ("cum", (0, 1))}
-        if LONG:
-            turns.update({TURN0 + TURN_STEP * n: (2 + n, (0, 1, 2, 3)) for n in range(2)})
-        else:
-            turns.update({TURN0 + TURN_STEP * n: (2 + n // 2, (n % 2 * 2, n % 2 * 2 + 1)) for n in range(4)})
-        pending = []
+
+        def late_piece(i):
+            if i in LATE_PIECES and LATE_PIECES[i] not in widened:
+                widen(*LATE_PIECES[i])
+            if i - 1 in LATE_PIECES:
+                quantize_factor(*LATE_PIECES[i - 1])
+            if i in LATE_PIECES:
+                weave(*LATE_PIECES[i])
+
+        waiting = []
         for i in range(STEPS):
-            k, a = divmod(i, UNITS)
             if i in turns:
-                turn_run(*turns[i])
+                turn_pair(turns[i])
             if i in (0, UNITS):
-                stage1([i, i + 1])
-                square(i)
-                square(i + 1)
+                stage1(i, i + 1)
             elif i not in (1, UNITS + 1):
-                stage1([i])
-                square(i)
+                stage1(i)
             if i <= UNITS:
-                for j in range(4):
-                    if PREP_AT[j] == i:
-                        if (2 + j // 2, j % 2) not in planes:
-                            widen_all(2 + j // 2, j % 2, "v")
-                        if j > 0 and PREP_AT[j - 1] == i - 1:
-                            quantize_factor(2 + (j - 1) // 2, (j - 1) % 2)
-                        weave(2 + j // 2, j % 2)
-                    elif PREP_AT[j] == i - 1 and i not in PREP_AT:
-                        quantize_factor(2 + j // 2, j % 2)
-            for lead in (SORT_LEAD, SORT_LEAD - 1):
-                if i + lead in turns and i + lead > 3:
-                    v, slots = turns[i + lead]
-                    for t in (slots[:2] if lead == SORT_LEAD else slots[2:]):
-                        if (v, slots[0]) in SORTED:
-                            sort((v, t))
-            if i in (2, 3):
-                quantize_rows((1, 2 * i - 4))
-                quantize_rows((1, 2 * i - 3))
-            q, m = divmod(i - LAG, UNITS)
-            closing = [(w, i - LAG - UNITS * ORDER.index((w, 1))) for w in range(V - 1)]
-            for w, n in closing:
-                if n == INV0:
-                    invert(w, 0, 2, sums[w][:, T:T + 2])
-                if n == ADD_AT:
-                    add_halves(w, 2, 4)
-            if a == 0 and 1 <= k <= last:
-                quantize_power(k - 1, 0, HALF)
-            for w, n in closing:
-                if n == ADD_AT:
-                    invert(w, 2, 4)
-            if i == STEPS - 2 and QA_FIRST:
+                late_piece(i)
+            if i + SORT_LEAD >= LATE_TURNS and i + SORT_LEAD in turns:
+                for key in turns[i + SORT_LEAD]:
+                    sort(key)
+            if i < UNITS and i in turns:
+                quantize_rows(*turns[i])
+
+            q, n = divmod(i - LAG, UNITS)
+            v, h = ORDER[q]
+            closing = q >= 0 and h == 1
+            if closing and n == 1:
+                invert(v, 0, 2, part(v, 1, 0, 2))
+            if closing and n == 3:
+                add_two(v, 2, M)
+            if i % UNITS == 0 and i > 0:
+                quantize_power(i // UNITS - 1)
+            if closing and n == 3:
+                invert(v, 2, M, recs[v][:, 2:M])
+            if i == STEPS - 2:
                 quantize_power(last, 0, HALF // 2)
-            if 0 <= q < last - 1:
-                if ORDER[q][1] == 0:
-                    due = [m]
-                else:
-                    due = [(0, 1), (2, 3), (), ()][m] if RUSH or q == last - 2 else [m]
-                for n in due:
-                    stage2(bank()[:], q, 0, n)
-                    if ORDER[q][1] == 0:
-                        read(q, 0, n, READ_ENG[q][n], 0)
-                    elif n < 2:
-                        read(q, 0, n, "v", 1, 0)
-                    else:
-                        read(q, 0, n, "s", 1)
-            if i - 1 in turns and i > UNITS:
-                v, slots = turns[i - 1]
-                for t in slots[:2]:
-                    quantize_rows((v, t))
-            if i - 2 in turns and i > UNITS:
-                v, slots = turns[i - 2]
-                for t in slots[2:]:
-                    quantize_rows((v, t))
+            if closing and n < 2:
+                for m in (2 * n, 2 * n + 1):
+                    stage2(bank()[:], q, 0, m)
+                    read(q, 0, m, 1, n == 0, part(v, 0, m, m + 1))
+            elif 0 <= q < last - 1 and h == 0:
+                stage2(bank()[:], q, 0, n)
+                read(q, 0, n, 0, n == M - 1 if v == 2 else n % 2 == 0)
             if i > UNITS:
-                for j in range(4):
-                    if PREP_AT[j] == i:
-                        if (2 + j // 2, j % 2) not in planes:
-                            widen_all(2 + j // 2, j % 2, "v")
-                        if j > 0 and PREP_AT[j - 1] == i - 1:
-                            quantize_factor(2 + (j - 1) // 2, (j - 1) % 2)
-                        weave(2 + j // 2, j % 2)
-                    elif PREP_AT[j] == i - 1 and i not in PREP_AT:
-                        quantize_factor(2 + j // 2, j % 2)
-            for w, n in closing:
-                if n == 2:
-                    pending.extend((w, j) for j in range(T))
-            if pending and i < STEPS - 1 and all(n != 0 for w, n in closing):
-                finish(*pending[0])
-                pending.remove(pending[0])
-            if i == STEPS - 2 and not QA_FIRST:
-                quantize_power(last, 0, HALF // 2)
+                if i - 1 in turns:
+                    quantize_rows(*turns[i - 1])
+                late_piece(i)
+            if closing and n == 2:
+                waiting.extend((v, m) for m in range(M))
+            if waiting and i < STEPS - 1 and not (closing and n == 0):
+                finish(*waiting[0])
+                waiting.remove(waiting[0])
+
         v = V - 1
-        quantize_power(last, HALF // 2, HALF // 2)
+        quarter = HALF // 2
+        quantize_power(last, quarter, quarter)
         for b in range(2):
             stage2(bank()[:], last - 1, 0, 2 * b)
             ps = bank()
             for e in range(2):
-                stage2(ps[:, e * 256:(e + 1) * 256], last, 0, 2 * b + e)
+                stage2(ps[:, e * quarter:(e + 1) * quarter], last, 0, 2 * b + e)
             stage2(bank()[:], last - 1, 0, 2 * b + 1)
             ps = bank()
             for e in range(2):
-                stage2(ps[:, e * 256:(e + 1) * 256], last, 256, 2 * b + e)
+                stage2(ps[:, e * quarter:(e + 1) * quarter], last, quarter, 2 * b + e)
             for m in (2 * b, 2 * b + 1):
-                read(last - 1, 0, m, "s", 0)
-                read(last, 0, m, "s", 1)
+                read(last - 1, 0, m, 0, False)
+                read(last, 0, m, 1, False)
                 if b == 1:
-                    read(last, 256, m, "s", 2)
-
-        def add_parts(m):
-            nc.vector.tensor_reduce(recs[v][:, m:m + 1], sums[v][:, :3 * T].rearrange("p (h m) -> p m h", h=3)[:, m, :],
-                                    axis=mybir.AxisListType.X, op=ALU.add)
-
-        for m in range(T):
-            if (v - 1, m) not in finished:
-                finish(v - 1, m)
-        add_halves(v, 0, 1)
-        nc.vector.tensor_scalar(res[v][:, HALF + 256:J], var[last, 256, 0], 1.0, recs[v][:, 0:1], op0=ALU.mult, op1=ALU.add,
-                                accum_out=sums[v][:, 3 * T:3 * T + 1])
-        read(last, 256, 1, "v", 2)
-        invert(v, 0, 1, sums[v][:, 3 * T:3 * T + 1])
-        if SPLIT0:
-            finish(v, 0, 0, SPLIT0)
-            finish(v, 0, SPLIT0, J)
-        else:
-            finish(v, 0)
-        add_parts(1)
-        add_parts(2)
-        invert(v, 1, 2)
-        invert(v, 2, 3)
+                    read(last, quarter, m, 2, False)
+        for tile in waiting:
+            finish(*tile)
+        add_two(v, 0, 1)
+        read(last, quarter, 0, 3, True, recs[v][:, 0:1])
+        read(last, quarter, 1, 2, True)
+        invert(v, 0, 1, part(v, 3, 0, 1))
+        finish(v, 0)
+        add_three(v, 1)
+        add_three(v, 2)
+        invert(v, 1, 2, recs[v][:, 1:2])
+        invert(v, 2, 3, recs[v][:, 2:3])
         finish(v, 1)
-        add_parts(3)
+        add_three(v, 3)
         finish(v, 2)
-        invert(v, 3, 4)
+        invert(v, 3, 4, recs[v][:, 3:4])
         finish(v, 3)

@@ -28,9 +28,9 @@ ORDER = [(0, 0), (1, 0), (0, 1), (1, 1), (2, 0), (2, 1), (3, 0), (3, 1)]
 STEPS = len(ORDER) * UNITS
 LAG = 6
 LATE_TURNS = 10
-SORT_LEAD = 3
-SCALAR_PIECES = ((1, 0), (1, 1), (2, 0))
-LATE_PIECES = {1: (2, 0), 2: (2, 1), 3: (3, 0), 5: (3, 1)}
+SORT_LEAD = 2
+PIECES = [(c, g) for c in range(J // CHUNK) for g in range(G)]
+SCALAR_PIECES = PIECES[G:G + 3]
 
 
 def tile_forecast_variance_shares_s7_kernel(tc, psi, factor_bytes, factor_scale, cum, out):
@@ -46,16 +46,18 @@ def tile_forecast_variance_shares_s7_kernel(tc, psi, factor_bytes, factor_scale,
 
         ctx.enter_context(tc.manual_schedule())
 
-        f_scale = keep.tile([P, G * T], F32, name="f_scale")
-        nc.scalar.dma_start(out=f_scale[:].rearrange("p (g t) -> p g t", g=G),
+        f_scale = keep.tile([P, G, 2 * T], F32, name="f_scale")
+        nc.scalar.dma_start(out=f_scale[:, :, :T],
                             in_=factor_scale.rearrange("(g p t) o -> p g (t o)", p=P, t=T))
         f_bytes = {}
         rows = {}
 
-        def load_factor(h, g):
-            f_bytes[h, g] = keep.tile([P, T, HALF], U8, name="f_bytes%d%d" % (h, g))
-            nc.sync.dma_start(out=f_bytes[h, g][:],
-                              in_=factor_bytes.rearrange("(g p t) n -> g p t n", p=P, t=T)[g][:, :, h * HALF:(h + 1) * HALF])
+        def load_factor(h, g, t0, n):
+            tile = keep.tile([P, n, HALF], U8, name="f_bytes%d%d%d" % (h, g, t0))
+            src = factor_bytes.rearrange("(g p t) n -> g p t n", p=P, t=T)[g]
+            nc.sync.dma_start(out=tile[:], in_=src[:, t0:t0 + n, h * HALF:(h + 1) * HALF])
+            for i in range(n):
+                f_bytes[h, g, t0 + i] = tile[:, i, :]
 
         def load_psi(v, t0, n):
             tile = keep.tile([P, n * K], BF16, name="psi_rows%d%d" % (v, t0))
@@ -63,14 +65,15 @@ def tile_forecast_variance_shares_s7_kernel(tc, psi, factor_bytes, factor_scale,
             for i in range(n):
                 rows[v, t0 + i] = tile[:, i * K:(i + 1) * K]
 
-        load_factor(0, 0)
-        load_factor(0, 1)
+        for g in range(G):
+            load_factor(0, g, 0, 2)
+            load_factor(0, g, 2, 2)
         for t in range(T):
             load_psi(0, t, 1)
         load_psi(1, 0, 2)
-        load_factor(1, 0)
+        load_factor(1, 0, 0, T)
         load_psi(1, 2, 2)
-        load_factor(1, 1)
+        load_factor(1, 1, 0, T)
         cum_rows = keep.tile([P, M * H], BF16, name="cum_rows")
         nc.sync.dma_start(out=cum_rows[:].rearrange("p (m h) -> p m h", m=M), in_=cum.rearrange("(m p) h -> p m h", p=P))
         rows["cum", 0] = cum_rows[:, :2 * H]
@@ -112,10 +115,7 @@ def tile_forecast_variance_shares_s7_kernel(tc, psi, factor_bytes, factor_scale,
             grouped[key] = work.tile([P, K], BF16, name="grouped", align_bytes=64)
             dst = grouped[key][:].bitcast(F32).rearrange("p (g r u) -> p g r u", g=2, u=2)
             src = turned[key][:].rearrange("p (g u r) -> p g r u", g=2, u=2)
-            if key[0] == 2 and key[1] % 2:
-                nc.vector.tensor_copy(dst, src)
-            else:
-                nc.scalar.copy(dst, src)
+            nc.scalar.copy(dst, src)
 
         def turn_pair(keys):
             for key in keys:
@@ -134,26 +134,17 @@ def tile_forecast_variance_shares_s7_kernel(tc, psi, factor_bytes, factor_scale,
                 widened[c, g] = keep.tile([P, T * CHUNK], BF16, name="widened%d%d" % (c, g))
             h, n0 = divmod(c * CHUNK, HALF)
             for t in slots:
-                src = f_bytes[h, g][:, t, n0:n0 + CHUNK].bitcast(FP8)
-                scale = f_scale[:, g * T + t:g * T + t + 1]
+                dst = widened[c, g][:, t * CHUNK:(t + 1) * CHUNK]
+                src = f_bytes[h, g, t][:, n0:n0 + CHUNK].bitcast(FP8)
                 if (c, g) in SCALAR_PIECES:
-                    nc.scalar.activation(widened[c, g][:, t * CHUNK:(t + 1) * CHUNK], src, ACT.Copy, scale=scale)
+                    nc.scalar.activation(dst, src, ACT.Copy, scale=f_scale[:, g, t:t + 1])
                 else:
-                    dst = widened[c, g][:].rearrange("p (b n e) -> p b n e", b=2, e=2)[:, t // 2, :, t % 2]
-                    nc.vector.tensor_scalar(dst, src, scale, None, op0=ALU.mult)
+                    nc.vector.tensor_scalar(dst, src, f_scale[:, g, t:t + 1], None, op0=ALU.mult)
 
         def weave(c, g):
             woven[c, g] = work.tile([P, CHUNK * T], BF16, name="woven", align_bytes=64)
-            if (c, g) in SCALAR_PIECES:
-                nc.vector.tensor_copy(woven[c, g][:].rearrange("p (n i t) -> p n t i", t=T, i=RUN),
-                                      widened[c, g][:].rearrange("p (t n i) -> p n t i", t=T, i=RUN))
-            else:
-                dst = woven[c, g][:].bitcast(F32).rearrange("p (n b) -> p n b", b=2)
-                src = widened[c, g][:].bitcast(F32).rearrange("p (b n) -> p n b", b=2)
-                if (c, g) == (2, 1):
-                    nc.scalar.copy(dst, src)
-                else:
-                    nc.vector.tensor_copy(dst, src)
+            nc.vector.tensor_copy(woven[c, g][:].rearrange("p (n i t) -> p n t i", t=T, i=RUN),
+                                  widened[c, g][:].rearrange("p (t n i) -> p n t i", t=T, i=RUN))
 
         def quantize_factor(c, g):
             quantize(("factor", c, g), woven[c, g][:])
@@ -252,14 +243,8 @@ def tile_forecast_variance_shares_s7_kernel(tc, psi, factor_bytes, factor_scale,
             turns[LATE_TURNS + 2 * n] = ((2 + v, 2 * b), (2 + v, 2 * b + 1))
         last = len(ORDER) - 1
 
-        def late_piece(i):
-            if i in LATE_PIECES and LATE_PIECES[i] not in widened:
-                widen(*LATE_PIECES[i])
-            if i - 1 in LATE_PIECES:
-                quantize_factor(*LATE_PIECES[i - 1])
-            if i in LATE_PIECES:
-                weave(*LATE_PIECES[i])
-
+        to_weave = PIECES[len(PIECES) // 2:]
+        to_quantize = []
         waiting = []
         for i in range(STEPS):
             if i in turns:
@@ -268,13 +253,9 @@ def tile_forecast_variance_shares_s7_kernel(tc, psi, factor_bytes, factor_scale,
                 stage1(i, i + 1)
             elif i not in (1, UNITS + 1):
                 stage1(i)
-            if i <= UNITS:
-                late_piece(i)
             if i + SORT_LEAD >= LATE_TURNS and i + SORT_LEAD in turns:
                 for key in turns[i + SORT_LEAD]:
                     sort(key)
-            if i < UNITS and i in turns:
-                quantize_rows(*turns[i])
 
             q, n = divmod(i - LAG, UNITS)
             v, h = ORDER[q]
@@ -295,11 +276,20 @@ def tile_forecast_variance_shares_s7_kernel(tc, psi, factor_bytes, factor_scale,
                     read(q, 0, m, 1, n == 0, part(v, 0, m, m + 1))
             elif 0 <= q < last - 1 and h == 0:
                 stage2(bank()[:], q, 0, n)
-                read(q, 0, n, 0, n == M - 1 if v == 2 else n % 2 == 0)
-            if i > UNITS:
-                if i - 1 in turns:
-                    quantize_rows(*turns[i - 1])
-                late_piece(i)
+                read(q, 0, n, 0, n % 2 == 0)
+            if i > UNITS and i - 1 in turns:
+                quantize_rows(*turns[i - 1])
+            piece = to_weave[0] if to_weave and i % UNITS else None
+            if piece and piece not in widened:
+                widen(*piece)
+            for done in to_quantize:
+                quantize_factor(*done)
+            to_quantize = [piece] if piece else []
+            if piece:
+                weave(*piece)
+                to_weave = to_weave[1:]
+            if i < UNITS and i in turns:
+                quantize_rows(*turns[i])
             if closing and n == 2:
                 waiting.extend((v, m) for m in range(M))
             if waiting and i < STEPS - 1 and not (closing and n == 0):

@@ -26,11 +26,11 @@ CHUNK = 256
 RUN = 4
 ORDER = [(0, 0), (1, 0), (0, 1), (1, 1), (2, 0), (2, 1), (3, 0), (3, 1)]
 STEPS = len(ORDER) * UNITS
+CLOSING = (((0, 1), (2, 3), (), ()), ((0, 1, 2), (3,), (), ()))
 LAG = 6
+FIRST_STAGE2 = 10
 LATE_TURNS = 10
-SORT_LEAD = 2
-PIECES = [(c, g) for c in range(J // CHUNK) for g in range(G)]
-SCALAR_PIECES = PIECES[G:G + 3]
+SORT_LEAD = 3
 
 
 def tile_forecast_variance_shares_s7_kernel(tc, psi, factor_bytes, factor_scale, cum, out):
@@ -50,7 +50,7 @@ def tile_forecast_variance_shares_s7_kernel(tc, psi, factor_bytes, factor_scale,
         nc.scalar.dma_start(out=f_scale[:, :, :T],
                             in_=factor_scale.rearrange("(g p t) o -> p g (t o)", p=P, t=T))
         f_bytes = {}
-        rows = {}
+        rows, row_pairs = {}, {}
 
         def load_factor(h, g, t0, n):
             tile = keep.tile([P, n, HALF], U8, name="f_bytes%d%d%d" % (h, g, t0))
@@ -64,20 +64,22 @@ def tile_forecast_variance_shares_s7_kernel(tc, psi, factor_bytes, factor_scale,
             nc.sync.dma_start(out=tile[:], in_=psi[v].rearrange("(p t) k -> p (t k)", t=T)[:, t0 * K:(t0 + n) * K])
             for i in range(n):
                 rows[v, t0 + i] = tile[:, i * K:(i + 1) * K]
+            for b in range(n // 2):
+                row_pairs[v, t0 // 2 + b] = tile[:, 2 * b * K:2 * (b + 1) * K]
 
         for g in range(G):
             load_factor(0, g, 0, 2)
             load_factor(0, g, 2, 2)
-        for t in range(T):
-            load_psi(0, t, 1)
-        load_psi(1, 0, 2)
-        load_factor(1, 0, 0, T)
-        load_psi(1, 2, 2)
-        load_factor(1, 1, 0, T)
+            load_psi(0, 2 * g, 1)
+            load_psi(0, 2 * g + 1, 1)
+        for g in range(G):
+            load_psi(1, 2 * g, 2)
+            load_factor(1, g, 0, T)
         cum_rows = keep.tile([P, M * H], BF16, name="cum_rows")
         nc.sync.dma_start(out=cum_rows[:].rearrange("p (m h) -> p m h", m=M), in_=cum.rearrange("(m p) h -> p m h", p=P))
         rows["cum", 0] = cum_rows[:, :2 * H]
         rows["cum", 1] = cum_rows[:, 2 * H:]
+        row_pairs["cum", 0] = cum_rows[:]
         load_psi(2, 0, T)
         load_psi(3, 0, T)
 
@@ -86,19 +88,26 @@ def tile_forecast_variance_shares_s7_kernel(tc, psi, factor_bytes, factor_scale,
 
         codes, scales = {}, {}
 
-        def quantize(key, src):
+        def quantize(src, *keys):
             n = src.shape[1] // T
-            name = "_".join(str(x) for x in key)
-            codes[key] = keep.tile([P, n], U32, name="codes_" + name, align_bytes=64)
-            scales[key] = keep.tile([P, n], U8, name="scales_" + name, align_bytes=64)
-            nc.vector.quantize_mx(out=codes[key][:].bitcast(FP8X4), scales=scales[key][:], in_=src)
+            name = "_".join(str(x) for x in keys[0])
+            code_tile = keep.tile([P, n], U32, name="codes_" + name, align_bytes=64)
+            scale_tile = keep.tile([P, n], U8, name="scales_" + name, align_bytes=64)
+            nc.vector.quantize_mx(out=code_tile[:].bitcast(FP8X4), scales=scale_tile[:], in_=src)
+            each = n // len(keys)
+            for i, key in enumerate(keys):
+                codes[key] = code_tile[:, i * each:(i + 1) * each]
+                scales[key] = scale_tile[:, i * each:(i + 1) * each]
 
         sorted_words, turned, grouped = {}, {}, {}
 
-        def sort(key):
-            sorted_words[key] = work.tile([P, K // 2], F32, name="sorted_words")
-            nc.vector.tensor_copy(sorted_words[key][:].rearrange("p (g u r) -> p g u r", g=2, u=2),
-                                  rows[key].bitcast(F32).rearrange("p (g r u) -> p g u r", g=2, u=2))
+        def sort(keys):
+            v, t0 = keys[0]
+            words = work.tile([P, K], F32, name="sorted_words", bufs=2)
+            nc.vector.tensor_copy(words[:].rearrange("p (g u r) -> p g u r", g=4, u=2),
+                                  row_pairs[v, t0 // 2].bitcast(F32).rearrange("p (g r u) -> p g u r", g=4, u=2))
+            for i, key in enumerate(keys):
+                sorted_words[key] = words[:, i * K // 2:(i + 1) * K // 2]
 
         def turn(key):
             turned[key] = bank()
@@ -112,10 +121,15 @@ def tile_forecast_variance_shares_s7_kernel(tc, psi, factor_bytes, factor_scale,
                     nc.tensor.transpose(turned[key][:, cols], src, ident[:])
 
         def group(key):
-            grouped[key] = work.tile([P, K], BF16, name="grouped", align_bytes=64)
-            dst = grouped[key][:].bitcast(F32).rearrange("p (g r u) -> p g r u", g=2, u=2)
+            v, t = key
+            if t % 2 == 0:
+                grouped[v, t // 2] = work.tile([P, 2 * K], BF16, name="grouped", align_bytes=64, bufs=3)
+            dst = grouped[v, t // 2][:, t % 2 * K:(t % 2 + 1) * K].bitcast(F32).rearrange("p (g r u) -> p g r u", g=2, u=2)
             src = turned[key][:].rearrange("p (g u r) -> p g r u", g=2, u=2)
             nc.scalar.copy(dst, src)
+
+        def pair(v, b):
+            return (v, 2 * b), (v, 2 * b + 1)
 
         def turn_pair(keys):
             for key in keys:
@@ -124,19 +138,18 @@ def tile_forecast_variance_shares_s7_kernel(tc, psi, factor_bytes, factor_scale,
                 group(key)
 
         def quantize_rows(*keys):
-            for key in keys:
-                quantize(key, grouped[key][:])
+            v, t = keys[0]
+            quantize(grouped[v, t // 2][:, t % 2 * K:(t % 2 + len(keys)) * K], *keys)
 
         widened, woven = {}, {}
 
-        def widen(c, g, slots=range(T)):
-            if (c, g) not in widened:
-                widened[c, g] = keep.tile([P, T * CHUNK], BF16, name="widened%d%d" % (c, g))
+        def widen(c, g, on_scalar=False):
+            widened[c, g] = keep.tile([P, T * CHUNK], BF16, name="widened%d%d" % (c, g))
             h, n0 = divmod(c * CHUNK, HALF)
-            for t in slots:
+            for t in range(T):
                 dst = widened[c, g][:, t * CHUNK:(t + 1) * CHUNK]
                 src = f_bytes[h, g, t][:, n0:n0 + CHUNK].bitcast(FP8)
-                if (c, g) in SCALAR_PIECES:
+                if on_scalar:
                     nc.scalar.activation(dst, src, ACT.Copy, scale=f_scale[:, g, t:t + 1])
                 else:
                     nc.vector.tensor_scalar(dst, src, f_scale[:, g, t:t + 1], None, op0=ALU.mult)
@@ -147,7 +160,7 @@ def tile_forecast_variance_shares_s7_kernel(tc, psi, factor_bytes, factor_scale,
                                   widened[c, g][:].rearrange("p (t n i) -> p n t i", t=T, i=RUN))
 
         def quantize_factor(c, g):
-            quantize(("factor", c, g), woven[c, g][:])
+            quantize(woven[c, g][:], ("factor", c, g))
 
         theta, power, var, res, sums, recs = {}, {}, {}, {}, {}, {}
 
@@ -166,6 +179,8 @@ def tile_forecast_variance_shares_s7_kernel(tc, psi, factor_bytes, factor_scale,
                             rhs=codes["factor", c, g][:, n0:n0 + UNIT].bitcast(FP8X4),
                             rhs_scale=scales["factor", c, g][:, n0:n0 + UNIT],
                             start=(g == 0), stop=(g == G - 1))
+
+        def square(*steps):
             for i in steps:
                 q, a = divmod(i, UNITS)
                 if a == 0:
@@ -174,13 +189,13 @@ def tile_forecast_variance_shares_s7_kernel(tc, psi, factor_bytes, factor_scale,
                                      theta[i][:].rearrange("p (t n) -> p n t", t=T), ACT.Square)
 
         def quantize_power(q, n0=0, n=HALF):
-            quantize(("power", q, n0), power[q][:, n0 * T:(n0 + n) * T])
+            quantize(power[q][:, n0 * T:(n0 + n) * T], ("power", q, n0))
 
         def stage2(ps, q, n0, m):
             cols = slice(m % 2 * P, (m % 2 + 1) * P)
             nc.tensor.matmul_mx(out=ps, lhsT=codes["cum", m // 2][:, cols].bitcast(FP8X4),
                                 lhsT_scale=scales["cum", m // 2][:, cols],
-                                rhs=codes["power", q, n0][:].bitcast(FP8X4), rhs_scale=scales["power", q, n0][:],
+                                rhs=codes["power", q, n0].bitcast(FP8X4), rhs_scale=scales["power", q, n0],
                                 start=True, stop=True)
             var[q, n0, m] = ps
 
@@ -191,7 +206,7 @@ def tile_forecast_variance_shares_s7_kernel(tc, psi, factor_bytes, factor_scale,
             v, h = ORDER[q]
             if v not in res:
                 res[v] = outs.tile([P, M * J], F32, name="res")
-                sums[v] = keep.tile([P, 4 * M], F32, name="sums%d" % v)
+                sums[v] = keep.tile([P, 3 * M], F32, name="sums%d" % v)
                 recs[v] = keep.tile([P, 2 * M], F32, name="recs%d" % v)
             src = var[q, n0, m]
             c0 = m * J + h * HALF + n0
@@ -204,128 +219,153 @@ def tile_forecast_variance_shares_s7_kernel(tc, psi, factor_bytes, factor_scale,
         def add_two(v, m0, m1):
             nc.vector.tensor_tensor(recs[v][:, m0:m1], part(v, 0, m0, m1), part(v, 1, m0, m1), op=ALU.add)
 
-        def add_three(v, m):
-            nc.vector.tensor_reduce(recs[v][:, m:m + 1], sums[v][:, :3 * M].rearrange("p (j m) -> p m j", j=3)[:, m, :],
-                                    axis=mybir.AxisListType.X, op=ALU.add)
-
         def invert(v, m0, m1, total):
             nc.vector.reciprocal(recs[v][:, M + m0:M + m1], total)
 
-        def finish(v, m):
-            row = res[v][:, m * J:(m + 1) * J]
+        def finish(v, m, n0=0, n=J):
+            row = res[v][:, m * J + n0:m * J + n0 + n]
             nc.vector.tensor_scalar(row, row, recs[v][:, M + m:M + m + 1], float(J), op0=ALU.mult, op1=ALU.mult)
-            nc.sync.dma_start(out=out[v][m * P:(m + 1) * P, :], in_=row)
+            nc.sync.dma_start(out=out[v][m * P:(m + 1) * P, n0:n0 + n], in_=row)
+
+        def report(q, m, on_vector):
+            v, h = ORDER[q]
+            stage2(bank()[:], q, 0, m)
+            read(q, 0, m, h, on_vector, part(v, 0, m, m + 1) if h else None)
 
         widen(0, 0)
-        widen(1, 0)
-        widen(0, 1, range(2))
+        widen(1, 0, True)
         weave(0, 0)
-        widen(0, 1, range(2, T))
-        widen(1, 1)
-        quantize_factor(0, 0)
-        weave(0, 1)
+        for key in pair(0, 0):
+            turn(key)
+            group(key)
         weave(1, 0)
-        for t in range(T):
-            turn((0, t))
-            group((0, t))
-        widen(2, 0)
+        quantize_factor(0, 0)
+        widen(0, 1)
         quantize_rows((0, 0))
+        weave(0, 1)
+        widen(1, 1, True)
+        for key in pair(0, 1):
+            turn(key)
+            group(key)
+        quantize_rows((0, 1))
         quantize_factor(0, 1)
-        quantize_rows((0, 1), (0, 2))
         quantize_factor(1, 0)
+        quantize_rows((0, 2))
         quantize_rows((0, 3))
         weave(1, 1)
+        widen(2, 0, True)
+
+        stage1(0, 1)
+        square(0, 1)
         quantize_factor(1, 1)
+        weave(2, 0)
+        turn_pair(pair(1, 0))
+        stage1(2)
+        square(2)
+        widen(2, 1)
+        quantize_factor(2, 0)
+        weave(2, 1)
+        quantize_rows(*pair(1, 0))
+        turn_pair(pair(1, 1))
+        stage1(3)
+        square(3)
+        widen(3, 1)
+        quantize_factor(2, 1)
+        quantize_rows((1, 2))
+        quantize_rows((1, 3))
+        widen(3, 0, True)
+        sort(pair("cum", 0))
+        weave(3, 1)
+        stage1(4, 5, 6, 7)
+        square(4, 5)
+        weave(3, 0)
+        quantize_factor(3, 1)
+        sort(pair(2, 0))
+        quantize_factor(3, 0)
+        quantize_power(0)
+        turn_pair(pair("cum", 0))
+        square(6, 7)
+        stage1(8)
+        square(8)
+        quantize_rows(*pair("cum", 0))
+        quantize_power(1)
+        stage1(9)
+        square(9)
+        sort(pair(2, 1))
 
-        turns = {2: ((1, 0), (1, 1)), 3: ((1, 2), (1, 3)), 4: (("cum", 0), ("cum", 1))}
-        for n in range(2 * (V - 2)):
-            v, b = divmod(n, 2)
-            turns[LATE_TURNS + 2 * n] = ((2 + v, 2 * b), (2 + v, 2 * b + 1))
+        turns = {LATE_TURNS + 2 * n: pair(2 + n // 2, n % 2) for n in range(2 * (V - 2))}
         last = len(ORDER) - 1
-
-        to_weave = PIECES[len(PIECES) // 2:]
-        to_quantize = []
+        quarter = HALF // 2
         waiting = []
-        for i in range(STEPS):
+        for i in range(FIRST_STAGE2, STEPS):
             if i in turns:
                 turn_pair(turns[i])
-            if i in (0, UNITS):
-                stage1(i, i + 1)
-            elif i not in (1, UNITS + 1):
-                stage1(i)
-            if i + SORT_LEAD >= LATE_TURNS and i + SORT_LEAD in turns:
-                for key in turns[i + SORT_LEAD]:
-                    sort(key)
-
+            stage1(i)
+            square(i)
+            long_ones = 0
+            if i % UNITS == 0:
+                quantize_power(i // UNITS - 1)
+                long_ones += 1
+            if i == STEPS - 2:
+                quantize_power(last, 0, quarter)
             q, n = divmod(i - LAG, UNITS)
             v, h = ORDER[q]
-            closing = q >= 0 and h == 1
-            if closing and n == 1:
-                invert(v, 0, 2, part(v, 1, 0, 2))
+            early, b = divmod(i - FIRST_STAGE2, 2)
+            if early < 2:
+                for m in (2 * b, 2 * b + 1):
+                    report(early, m, m < M - 1)
+            elif h == 1:
+                for m in CLOSING[v == V - 2][n]:
+                    report(q, m, m < 2)
+                    long_ones += m < 2
+            elif q < last - 1:
+                report(q, n, n % 2 == 0)
+                long_ones += n % 2 == 0
+            closing = early >= 2 and h == 1
+            if i + SORT_LEAD in turns:
+                sort(turns[i + SORT_LEAD])
             if closing and n == 3:
                 add_two(v, 2, M)
-            if i % UNITS == 0 and i > 0:
-                quantize_power(i // UNITS - 1)
-            if closing and n == 3:
-                invert(v, 2, M, recs[v][:, 2:M])
-            if i == STEPS - 2:
-                quantize_power(last, 0, HALF // 2)
-            if closing and n < 2:
-                for m in (2 * n, 2 * n + 1):
-                    stage2(bank()[:], q, 0, m)
-                    read(q, 0, m, 1, n == 0, part(v, 0, m, m + 1))
-            elif 0 <= q < last - 1 and h == 0:
-                stage2(bank()[:], q, 0, n)
-                read(q, 0, n, 0, n % 2 == 0)
-            if i > UNITS and i - 1 in turns:
-                quantize_rows(*turns[i - 1])
-            piece = to_weave[0] if to_weave and i % UNITS else None
-            if piece and piece not in widened:
-                widen(*piece)
-            for done in to_quantize:
-                quantize_factor(*done)
-            to_quantize = [piece] if piece else []
-            if piece:
-                weave(*piece)
-                to_weave = to_weave[1:]
-            if i < UNITS and i in turns:
-                quantize_rows(*turns[i])
-            if closing and n == 2:
+            if closing and n == 1 and not waiting and i - 1 not in turns:
+                invert(v, 0, 2, part(v, 1, 0, 2))
                 waiting.extend((v, m) for m in range(M))
-            if waiting and i < STEPS - 1 and not (closing and n == 0):
+                v = None
+            if waiting and long_ones < 2 and i not in (STEPS - 4, STEPS - 1):
                 finish(*waiting[0])
                 waiting.remove(waiting[0])
+            if closing and n == 3:
+                invert(v, 2, M, recs[v][:, 2:M])
+            if i - 1 in turns:
+                quantize_rows(*turns[i - 1])
+            if closing and n == 1 and v is not None:
+                invert(v, 0, 2, part(v, 1, 0, 2))
+                waiting.extend((v, m) for m in range(M))
 
         v = V - 1
-        quarter = HALF // 2
         quantize_power(last, quarter, quarter)
-        for b in range(2):
-            stage2(bank()[:], last - 1, 0, 2 * b)
-            ps = bank()
-            for e in range(2):
-                stage2(ps[:, e * quarter:(e + 1) * quarter], last, 0, 2 * b + e)
-            stage2(bank()[:], last - 1, 0, 2 * b + 1)
-            ps = bank()
-            for e in range(2):
-                stage2(ps[:, e * quarter:(e + 1) * quarter], last, quarter, 2 * b + e)
-            for m in (2 * b, 2 * b + 1):
-                read(last - 1, 0, m, 0, False)
-                read(last, 0, m, 1, False)
-                if b == 1:
-                    read(last, quarter, m, 2, False)
+        report(last - 1, 0, False)
+        stage2(bank()[:, :quarter], last, 0, 0)
+        read(last, 0, 0, 1, False)
+        report(last - 1, 1, False)
+        stage2(bank()[:, :quarter], last, quarter, 0)
         for tile in waiting:
             finish(*tile)
         add_two(v, 0, 1)
-        read(last, quarter, 0, 3, True, recs[v][:, 0:1])
-        read(last, quarter, 1, 2, True)
-        invert(v, 0, 1, part(v, 3, 0, 1))
-        finish(v, 0)
-        add_three(v, 1)
-        add_three(v, 2)
-        invert(v, 1, 2, recs[v][:, 1:2])
-        invert(v, 2, 3, recs[v][:, 2:3])
-        finish(v, 1)
-        add_three(v, 3)
-        finish(v, 2)
-        invert(v, 3, 4, recs[v][:, 3:4])
-        finish(v, 3)
+        read(last, quarter, 0, 2, True, recs[v][:, 0:1])
+        for m in range(1, M):
+            ps = bank()
+            stage2(ps[:, :quarter], last, 0, m)
+            stage2(ps[:, quarter:], last, quarter, m)
+            var[last, 0, m] = ps[:]
+            read(last, 0, m, 1, False)
+            if m < M - 1:
+                report(last - 1, m + 1, False)
+        invert(v, 0, 1, part(v, 2, 0, 1))
+        finish(v, 0, 0, HALF)
+        add_two(v, 1, 2)
+        finish(v, 0, HALF, HALF)
+        for m in range(1, M):
+            if m > 1:
+                add_two(v, m, m + 1)
+            invert(v, m, m + 1, recs[v][:, m:m + 1])
+            finish(v, m)

@@ -44,6 +44,10 @@ def tile_forecast_variance_shares_s7_kernel(tc, psi, factor_bytes, factor_scale,
         ident = keep.tile([P, P], F32, name="ident")
         make_identity(nc, ident[:])
 
+        idle = keep.tile([P, 2], F32, name="idle")
+        nc.vector.memset(idle[:, :1], 0.0)
+        nc.scalar.activation(idle[:, 1:], idle[:, :1], ACT.Square)
+
         ctx.enter_context(tc.manual_schedule())
 
         f_scale = keep.tile([P, G, 2 * T], F32, name="f_scale")
@@ -70,11 +74,11 @@ def tile_forecast_variance_shares_s7_kernel(tc, psi, factor_bytes, factor_scale,
         for g in range(G):
             load_factor(0, g, 0, 2)
             load_factor(0, g, 2, 2)
-            load_psi(0, 2 * g, 1)
-            load_psi(0, 2 * g + 1, 1)
+        for t in range(T):
+            load_psi(0, t, 1)
         for g in range(G):
-            load_psi(1, 2 * g, 2)
             load_factor(1, g, 0, T)
+            load_psi(1, 2 * g, 2)
         cum_rows = keep.tile([P, M * H], BF16, name="cum_rows")
         nc.sync.dma_start(out=cum_rows[:].rearrange("p (m h) -> p m h", m=M), in_=cum.rearrange("(m p) h -> p m h", p=P))
         rows["cum", 0] = cum_rows[:, :2 * H]
@@ -143,10 +147,11 @@ def tile_forecast_variance_shares_s7_kernel(tc, psi, factor_bytes, factor_scale,
 
         widened, woven = {}, {}
 
-        def widen(c, g, on_scalar=False):
-            widened[c, g] = keep.tile([P, T * CHUNK], BF16, name="widened%d%d" % (c, g))
+        def widen(c, g, on_scalar=False, slots=range(T)):
+            if (c, g) not in widened:
+                widened[c, g] = keep.tile([P, T * CHUNK], BF16, name="widened%d%d" % (c, g))
             h, n0 = divmod(c * CHUNK, HALF)
-            for t in range(T):
+            for t in slots:
                 dst = widened[c, g][:, t * CHUNK:(t + 1) * CHUNK]
                 src = f_bytes[h, g, t][:, n0:n0 + CHUNK].bitcast(FP8)
                 if on_scalar:
@@ -234,42 +239,40 @@ def tile_forecast_variance_shares_s7_kernel(tc, psi, factor_bytes, factor_scale,
 
         widen(0, 0)
         widen(1, 0, True)
+        widen(0, 1, False, range(2))
         weave(0, 0)
-        for key in pair(0, 0):
-            turn(key)
-            group(key)
-        weave(1, 0)
-        quantize_factor(0, 0)
-        widen(0, 1)
-        quantize_rows((0, 0))
-        weave(0, 1)
+        widen(0, 1, False, range(2, T))
         widen(1, 1, True)
-        for key in pair(0, 1):
-            turn(key)
-            group(key)
-        quantize_rows((0, 1))
+        quantize_factor(0, 0)
+        weave(0, 1)
+        weave(1, 0)
+        for t in range(T):
+            turn((0, t))
+            group((0, t))
+        widen(2, 0, True)
+        quantize_rows((0, 0))
         quantize_factor(0, 1)
+        quantize_rows((0, 1))
         quantize_factor(1, 0)
         quantize_rows((0, 2))
         quantize_rows((0, 3))
         weave(1, 1)
-        widen(2, 0, True)
 
         stage1(0, 1)
         square(0, 1)
-        quantize_factor(1, 1)
         weave(2, 0)
+        quantize_factor(1, 1)
         turn_pair(pair(1, 0))
         stage1(2)
         square(2)
         widen(2, 1)
         quantize_factor(2, 0)
         weave(2, 1)
+        widen(3, 1)
         quantize_rows(*pair(1, 0))
         turn_pair(pair(1, 1))
         stage1(3)
         square(3)
-        widen(3, 1)
         quantize_factor(2, 1)
         quantize_rows((1, 2))
         quantize_rows((1, 3))

@@ -27,6 +27,7 @@ RUN = 4
 ORDER = [(0, 0), (1, 0), (0, 1), (1, 1), (2, 0), (2, 1), (3, 0), (3, 1)]
 STEPS = len(ORDER) * UNITS
 CLOSING = (((0, 1), (2, 3), (), ()), ((0, 1, 2), (3,), (), ()))
+WARM_UPS = 8
 LAG = 6
 FIRST_STAGE2 = 10
 LATE_TURNS = 10
@@ -47,6 +48,9 @@ def tile_forecast_variance_shares_s7_kernel(tc, psi, factor_bytes, factor_scale,
         idle = keep.tile([P, 2], F32, name="idle")
         nc.vector.memset(idle[:, :1], 0.0)
         nc.scalar.activation(idle[:, 1:], idle[:, :1], ACT.Square)
+
+        zeros = keep.tile([P, HALF], BF16, name="zeros")
+        nc.vector.memset(zeros[:], 0.0)
 
         ctx.enter_context(tc.manual_schedule())
 
@@ -236,6 +240,10 @@ def tile_forecast_variance_shares_s7_kernel(tc, psi, factor_bytes, factor_scale,
             v, h = ORDER[q]
             stage2(bank()[:], q, 0, m)
             read(q, 0, m, h, on_vector, part(v, 0, m, m + 1) if h else None)
+
+        unread = bank()
+        for n in range(WARM_UPS):
+            nc.tensor.matmul(unread[:], lhsT=zeros[:, :P], rhs=zeros[:], start=True, stop=True)
 
         widen(0, 0)
         widen(1, 0, True)

@@ -27,7 +27,6 @@ RUN = 4
 ORDER = [(0, 0), (1, 0), (0, 1), (1, 1), (2, 0), (2, 1), (3, 0), (3, 1)]
 STEPS = len(ORDER) * UNITS
 CLOSING = (((0, 1), (2, 3), (), ()), ((0, 1, 2), (3,), (), ()))
-WARM_UPS = 8
 LAG = 6
 FIRST_STAGE2 = 10
 LATE_TURNS = 10
@@ -45,18 +44,16 @@ def tile_forecast_variance_shares_s7_kernel(tc, psi, factor_bytes, factor_scale,
         ident = keep.tile([P, P], F32, name="ident")
         make_identity(nc, ident[:])
 
-        idle = keep.tile([P, 2], F32, name="idle")
-        nc.vector.memset(idle[:, :1], 0.0)
-        nc.scalar.activation(idle[:, 1:], idle[:, :1], ACT.Square)
-
-        zeros = keep.tile([P, HALF], BF16, name="zeros")
-        nc.vector.memset(zeros[:], 0.0)
-
         ctx.enter_context(tc.manual_schedule())
 
         f_scale = keep.tile([P, G, 2 * T], F32, name="f_scale")
         nc.scalar.dma_start(out=f_scale[:, :, :T],
                             in_=factor_scale.rearrange("(g p t) o -> p g (t o)", p=P, t=T))
+        idle = keep.tile([P, 2], F32, name="idle")
+        nc.vector.memset(idle[:, :1], 0.0)
+        nc.scalar.activation(idle[:, 1:], idle[:, :1], ACT.Square)
+        zeros = keep.tile([P, HALF], BF16, name="zeros")
+        nc.vector.memset(zeros[:], 0.0)
         f_bytes = {}
         rows, row_pairs = {}, {}
 
@@ -78,8 +75,8 @@ def tile_forecast_variance_shares_s7_kernel(tc, psi, factor_bytes, factor_scale,
         for g in range(G):
             load_factor(0, g, 0, 2)
             load_factor(0, g, 2, 2)
-        for t in range(T):
-            load_psi(0, t, 1)
+            load_psi(0, 2 * g, 1)
+            load_psi(0, 2 * g + 1, 1)
         for g in range(G):
             load_factor(1, g, 0, T)
             load_psi(1, 2 * g, 2)
@@ -93,6 +90,11 @@ def tile_forecast_variance_shares_s7_kernel(tc, psi, factor_bytes, factor_scale,
 
         def bank():
             return psum.tile([P, HALF], F32, name="bank")
+
+        def warm(n):
+            ps = bank()
+            for i in range(n):
+                nc.tensor.matmul(ps[:], lhsT=zeros[:, :P], rhs=zeros[:], start=True, stop=True)
 
         codes, scales = {}, {}
 
@@ -149,34 +151,37 @@ def tile_forecast_variance_shares_s7_kernel(tc, psi, factor_bytes, factor_scale,
             v, t = keys[0]
             quantize(grouped[v, t // 2][:, t % 2 * K:(t % 2 + len(keys)) * K], *keys)
 
-        widened, woven = {}, {}
+        planes = [keep.tile([P, G * T * HALF], BF16, name="planes%d" % h) for h in range(J // HALF)]
+        woven = {}
 
-        def widen(c, g, on_scalar=False, slots=range(T)):
-            if (c, g) not in widened:
-                widened[c, g] = keep.tile([P, T * CHUNK], BF16, name="widened%d%d" % (c, g))
+        def widen(c, g, on_scalar=False, n=CHUNK):
             h, n0 = divmod(c * CHUNK, HALF)
-            for t in slots:
-                dst = widened[c, g][:, t * CHUNK:(t + 1) * CHUNK]
-                src = f_bytes[h, g, t][:, n0:n0 + CHUNK].bitcast(FP8)
+            for t in range(T):
+                dst = planes[h][:, (g * T + t) * HALF + n0:(g * T + t) * HALF + n0 + n]
+                src = f_bytes[h, g, t][:, n0:n0 + n].bitcast(FP8)
                 if on_scalar:
                     nc.scalar.activation(dst, src, ACT.Copy, scale=f_scale[:, g, t:t + 1])
                 else:
                     nc.vector.tensor_scalar(dst, src, f_scale[:, g, t:t + 1], None, op0=ALU.mult)
 
-        def weave(c, g):
-            woven[c, g] = work.tile([P, CHUNK * T], BF16, name="woven", align_bytes=64)
-            nc.vector.tensor_copy(woven[c, g][:].rearrange("p (n i t) -> p n t i", t=T, i=RUN),
-                                  widened[c, g][:].rearrange("p (t n i) -> p n t i", t=T, i=RUN))
+        def weave(c, *passes):
+            h, n0 = divmod(c * CHUNK, HALF)
+            g0, k = passes[0], len(passes)
+            woven[c, g0] = work.tile([P, k * CHUNK * T], BF16, name="woven", align_bytes=64)
+            src = planes[h][:].rearrange("p (g t n i) -> p g n t i", g=G, t=T, i=RUN)
+            nc.vector.tensor_copy(woven[c, g0][:].rearrange("p (g n i t) -> p g n t i", g=k, t=T, i=RUN),
+                                  src[:, g0:g0 + k, n0 // RUN:(n0 + CHUNK) // RUN])
 
-        def quantize_factor(c, g):
-            quantize(woven[c, g][:], ("factor", c, g))
+        def quantize_factor(c, *passes):
+            quantize(woven[c, passes[0]][:], *[("factor", c, g) for g in passes])
 
         theta, power, var, res, sums, recs = {}, {}, {}, {}, {}, {}
 
-        def stage1(*steps):
+        def stage1(*steps, slots=range(T)):
             for i in steps:
-                theta[i] = bank()
-            for t in range(T):
+                if i not in theta:
+                    theta[i] = bank()
+            for t in slots:
                 for i in steps:
                     v, h = ORDER[i // UNITS]
                     c, n0 = divmod(h * HALF + i % UNITS * UNIT, CHUNK)
@@ -241,30 +246,31 @@ def tile_forecast_variance_shares_s7_kernel(tc, psi, factor_bytes, factor_scale,
             stage2(bank()[:], q, 0, m)
             read(q, 0, m, h, on_vector, part(v, 0, m, m + 1) if h else None)
 
-        unread = bank()
-        for n in range(WARM_UPS):
-            nc.tensor.matmul(unread[:], lhsT=zeros[:, :P], rhs=zeros[:], start=True, stop=True)
-
+        warm(5)
         widen(0, 0)
         widen(1, 0, True)
-        widen(0, 1, False, range(2))
         weave(0, 0)
-        widen(0, 1, False, range(2, T))
-        widen(1, 1, True)
-        quantize_factor(0, 0)
-        weave(0, 1)
+        for key in pair(0, 0):
+            turn(key)
+            group(key)
+        warm(2)
         weave(1, 0)
-        for t in range(T):
-            turn((0, t))
-            group((0, t))
-        widen(2, 0, True)
+        quantize_factor(0, 0)
+        widen(0, 1)
         quantize_rows((0, 0))
-        quantize_factor(0, 1)
+        weave(0, 1)
+        widen(1, 1, True)
+        for key in pair(0, 1):
+            turn(key)
+            group(key)
+        warm(2)
         quantize_rows((0, 1))
+        quantize_factor(0, 1)
         quantize_factor(1, 0)
         quantize_rows((0, 2))
         quantize_rows((0, 3))
         weave(1, 1)
+        widen(2, 0, True)
 
         stage1(0, 1)
         square(0, 1)
@@ -272,33 +278,29 @@ def tile_forecast_variance_shares_s7_kernel(tc, psi, factor_bytes, factor_scale,
         quantize_factor(1, 1)
         turn_pair(pair(1, 0))
         stage1(2)
-        square(2)
-        widen(2, 1)
-        quantize_factor(2, 0)
-        weave(2, 1)
-        widen(3, 1)
-        quantize_rows(*pair(1, 0))
-        turn_pair(pair(1, 1))
         stage1(3)
-        square(3)
+        square(2, 3)
+        widen(2, 1, False, HALF)
+        quantize_factor(2, 0)
+        quantize_rows(*pair(1, 0))
+        weave(2, 1)
+        turn_pair(pair(1, 1))
+        sort(pair("cum", 0))
         quantize_factor(2, 1)
         quantize_rows((1, 2))
         quantize_rows((1, 3))
+        stage1(4, 5, 6, 7, slots=range(2))
         widen(3, 0, True)
-        sort(pair("cum", 0))
-        weave(3, 1)
-        stage1(4, 5, 6, 7)
-        square(4, 5)
-        weave(3, 0)
-        quantize_factor(3, 1)
-        sort(pair(2, 0))
-        quantize_factor(3, 0)
-        quantize_power(0)
         turn_pair(pair("cum", 0))
-        square(6, 7)
+        stage1(4, 5, 6, 7, slots=range(2, T))
+        square(4, 5, 6, 7)
+        sort(pair(2, 0))
+        weave(3, 0, 1)
+        quantize_rows(*pair("cum", 0))
+        quantize_factor(3, 0, 1)
+        quantize_power(0)
         stage1(8)
         square(8)
-        quantize_rows(*pair("cum", 0))
         quantize_power(1)
         stage1(9)
         square(9)

@@ -30,7 +30,6 @@ CLOSING = (((0, 1), (2, 3), (), ()), ((0, 1, 2), (3,), (), ()))
 LAG = 6
 FIRST_STAGE2 = 10
 LATE_TURNS = 10
-SORT_LEAD = 3
 
 
 def tile_forecast_variance_shares_s7_kernel(tc, psi, factor_bytes, factor_scale, cum, out):
@@ -292,7 +291,10 @@ def tile_forecast_variance_shares_s7_kernel(tc, psi, factor_bytes, factor_scale,
         stage1(4, 5, 6, 7, slots=range(2))
         widen(3, 0, True)
         turn_pair(pair("cum", 0))
-        stage1(4, 5, 6, 7, slots=range(2, T))
+        stage1(4, slots=range(2, T))
+        stage1(5, slots=range(2, T))
+        stage1(6, slots=range(2, T))
+        stage1(7, slots=range(2, T))
         square(4, 5, 6, 7)
         sort(pair(2, 0))
         weave(3, 0, 1)
@@ -326,7 +328,7 @@ def tile_forecast_variance_shares_s7_kernel(tc, psi, factor_bytes, factor_scale,
             early, b = divmod(i - FIRST_STAGE2, 2)
             if early < 2:
                 for m in (2 * b, 2 * b + 1):
-                    report(early, m, m < M - 1)
+                    report(early, m, True)
             elif h == 1:
                 for m in CLOSING[v == V - 2][n]:
                     report(q, m, m < 2)
@@ -335,8 +337,6 @@ def tile_forecast_variance_shares_s7_kernel(tc, psi, factor_bytes, factor_scale,
                 report(q, n, n % 2 == 0)
                 long_ones += n % 2 == 0
             closing = early >= 2 and h == 1
-            if i + SORT_LEAD in turns:
-                sort(turns[i + SORT_LEAD])
             if closing and n == 3:
                 add_two(v, 2, M)
             if closing and n == 1 and not waiting and i - 1 not in turns:

@@ -51,8 +51,6 @@ def tile_forecast_variance_shares_s7_kernel(tc, psi, factor_bytes, factor_scale,
         idle = keep.tile([P, 2], F32, name="idle")
         nc.vector.memset(idle[:, :1], 0.0)
         nc.scalar.activation(idle[:, 1:], idle[:, :1], ACT.Square)
-        zeros = keep.tile([P, HALF], BF16, name="zeros")
-        nc.vector.memset(zeros[:], 0.0)
         f_bytes = {}
         rows, row_pairs = {}, {}
 
@@ -71,11 +69,14 @@ def tile_forecast_variance_shares_s7_kernel(tc, psi, factor_bytes, factor_scale,
             for b in range(n // 2):
                 row_pairs[v, t0 // 2 + b] = tile[:, 2 * b * K:2 * (b + 1) * K]
 
-        for g in range(G):
-            load_factor(0, g, 0, 2)
-            load_factor(0, g, 2, 2)
-            load_psi(0, 2 * g, 1)
-            load_psi(0, 2 * g + 1, 1)
+        load_factor(0, 0, 0, 2)
+        load_factor(0, 0, 2, 2)
+        load_factor(0, 1, 0, 2)
+        load_psi(0, 0, 1)
+        load_factor(0, 1, 2, 2)
+        load_psi(0, 1, 1)
+        load_psi(0, 2, 1)
+        load_psi(0, 3, 1)
         for g in range(G):
             load_factor(1, g, 0, T)
             load_psi(1, 2 * g, 2)
@@ -89,11 +90,6 @@ def tile_forecast_variance_shares_s7_kernel(tc, psi, factor_bytes, factor_scale,
 
         def bank():
             return psum.tile([P, HALF], F32, name="bank")
-
-        def warm(n):
-            ps = bank()
-            for i in range(n):
-                nc.tensor.matmul(ps[:], lhsT=zeros[:, :P], rhs=zeros[:], start=True, stop=True)
 
         codes, scales = {}, {}
 
@@ -153,9 +149,9 @@ def tile_forecast_variance_shares_s7_kernel(tc, psi, factor_bytes, factor_scale,
         planes = [keep.tile([P, G * T * HALF], BF16, name="planes%d" % h) for h in range(J // HALF)]
         woven = {}
 
-        def widen(c, g, on_scalar=False, n=CHUNK):
+        def widen(c, g, on_scalar=False, n=CHUNK, slots=range(T)):
             h, n0 = divmod(c * CHUNK, HALF)
-            for t in range(T):
+            for t in slots:
                 dst = planes[h][:, (g * T + t) * HALF + n0:(g * T + t) * HALF + n0 + n]
                 src = f_bytes[h, g, t][:, n0:n0 + n].bitcast(FP8)
                 if on_scalar:
@@ -235,46 +231,52 @@ def tile_forecast_variance_shares_s7_kernel(tc, psi, factor_bytes, factor_scale,
         def invert(v, m0, m1, total):
             nc.vector.reciprocal(recs[v][:, M + m0:M + m1], total)
 
-        def finish(v, m, n0=0, n=J):
+        def scale(v, m, n0=0, n=J):
             row = res[v][:, m * J + n0:m * J + n0 + n]
             nc.vector.tensor_scalar(row, row, recs[v][:, M + m:M + m + 1], float(J), op0=ALU.mult, op1=ALU.mult)
-            nc.sync.dma_start(out=out[v][m * P:(m + 1) * P, n0:n0 + n], in_=row)
+
+        def store(v, m, n0=0, n=J):
+            nc.sync.dma_start(out=out[v][m * P:(m + 1) * P, n0:n0 + n], in_=res[v][:, m * J + n0:m * J + n0 + n])
+
+        def finish(v, m):
+            scale(v, m)
+            store(v, m)
 
         def report(q, m, on_vector):
             v, h = ORDER[q]
             stage2(bank()[:], q, 0, m)
             read(q, 0, m, h, on_vector, part(v, 0, m, m + 1) if h else None)
 
-        warm(5)
         widen(0, 0)
         widen(1, 0, True)
+        widen(0, 1, False, CHUNK, range(2))
         weave(0, 0)
-        for key in pair(0, 0):
-            turn(key)
-            group(key)
-        warm(2)
-        weave(1, 0)
-        quantize_factor(0, 0)
-        widen(0, 1)
-        quantize_rows((0, 0))
-        weave(0, 1)
+        widen(0, 1, False, CHUNK, range(2, T))
         widen(1, 1, True)
-        for key in pair(0, 1):
-            turn(key)
-            group(key)
-        warm(2)
-        quantize_rows((0, 1))
+        quantize_factor(0, 0)
+        weave(0, 1)
+        turn((0, 0))
+        group((0, 0))
+        turn((0, 1))
+        group((0, 1))
+        turn((0, 2))
+        group((0, 2))
+        turn((0, 3))
+        group((0, 3))
+        quantize_rows((0, 0))
         quantize_factor(0, 1)
-        quantize_factor(1, 0)
+        weave(1, 0)
+        quantize_rows((0, 1))
         quantize_rows((0, 2))
         quantize_rows((0, 3))
         weave(1, 1)
+        quantize_factor(1, 0)
+        quantize_factor(1, 1)
         widen(2, 0, True)
 
         stage1(0, 1)
         square(0, 1)
         weave(2, 0)
-        quantize_factor(1, 1)
         turn_pair(pair(1, 0))
         stage1(2)
         stage1(3)
@@ -328,7 +330,7 @@ def tile_forecast_variance_shares_s7_kernel(tc, psi, factor_bytes, factor_scale,
             early, b = divmod(i - FIRST_STAGE2, 2)
             if early < 2:
                 for m in (2 * b, 2 * b + 1):
-                    report(early, m, True)
+                    report(early, m, m < M - 1)
             elif h == 1:
                 for m in CLOSING[v == V - 2][n]:
                     report(q, m, m < 2)
@@ -374,11 +376,15 @@ def tile_forecast_variance_shares_s7_kernel(tc, psi, factor_bytes, factor_scale,
             if m < M - 1:
                 report(last - 1, m + 1, False)
         invert(v, 0, 1, part(v, 2, 0, 1))
-        finish(v, 0, 0, HALF)
-        add_two(v, 1, 2)
-        finish(v, 0, HALF, HALF)
-        for m in range(1, M):
-            if m > 1:
-                add_two(v, m, m + 1)
-            invert(v, m, m + 1, recs[v][:, m:m + 1])
-            finish(v, m)
+        for m in range(M - 1):
+            scale(v, m, 0, HALF)
+            if m == 0:
+                store(v, m, 0, HALF)
+            add_two(v, m + 1, m + 2)
+            scale(v, m, HALF, HALF)
+            if m == 0:
+                store(v, m, HALF, HALF)
+            else:
+                store(v, m)
+            invert(v, m + 1, m + 2, recs[v][:, m + 1:m + 2])
+        finish(v, M - 1)

@@ -26,10 +26,6 @@ CHUNK = 256
 RUN = 4
 ORDER = [(0, 0), (1, 0), (0, 1), (1, 1), (2, 0), (2, 1), (3, 0), (3, 1)]
 STEPS = len(ORDER) * UNITS
-CLOSING = (((0, 1), (2, 3), (), ()), ((0, 1, 2), (3,), (), ()))
-LAG = 6
-FIRST_STAGE2 = 10
-LATE_TURNS = 10
 
 
 def tile_forecast_variance_shares_s7_kernel(tc, psi, factor_bytes, factor_scale, cum, out):
@@ -242,10 +238,30 @@ def tile_forecast_variance_shares_s7_kernel(tc, psi, factor_bytes, factor_scale,
             scale(v, m)
             store(v, m)
 
-        def report(q, m, on_vector):
+        def finish_on_gpsimd(v, m):
+            row = res[v][:, m * J:(m + 1) * J]
+            nc.gpsimd.tensor_scalar(row, row, recs[v][:, M + m:M + m + 1], float(J), op0=ALU.mult, op1=ALU.mult)
+            store(v, m)
+
+        def steps(*numbers):
+            for i in numbers:
+                stage1(i)
+                square(i)
+
+        def fill(q, tiles=range(M)):
+            for m in tiles:
+                stage2(bank()[:], q, 0, m)
+
+        def empty(q, *tiles, on_vector=True):
             v, h = ORDER[q]
-            stage2(bank()[:], q, 0, m)
-            read(q, 0, m, h, on_vector, part(v, 0, m, m + 1) if h else None)
+            for m in tiles:
+                read(q, 0, m, h, on_vector, part(v, 0, m, m + 1) if h else None)
+
+        def invert_carried(v, m0, m1):
+            invert(v, m0, m1, part(v, 1, m0, m1))
+
+        def invert_added(v, m0, m1):
+            invert(v, m0, m1, recs[v][:, m0:m1])
 
         widen(0, 0)
         widen(1, 0, True)
@@ -303,65 +319,102 @@ def tile_forecast_variance_shares_s7_kernel(tc, psi, factor_bytes, factor_scale,
         quantize_rows(*pair("cum", 0))
         quantize_factor(3, 0, 1)
         quantize_power(0)
-        stage1(8)
-        square(8)
+        steps(8)
         quantize_power(1)
-        stage1(9)
-        square(9)
-        sort(pair(2, 1))
+        steps(9)
 
-        turns = {LATE_TURNS + 2 * n: pair(2 + n // 2, n % 2) for n in range(2 * (V - 2))}
         last = len(ORDER) - 1
         quarter = HALF // 2
-        waiting = []
-        for i in range(FIRST_STAGE2, STEPS):
-            if i in turns:
-                turn_pair(turns[i])
-            stage1(i)
-            square(i)
-            long_ones = 0
-            if i % UNITS == 0:
-                quantize_power(i // UNITS - 1)
-                long_ones += 1
-            if i == STEPS - 2:
-                quantize_power(last, 0, quarter)
-            q, n = divmod(i - LAG, UNITS)
-            v, h = ORDER[q]
-            early, b = divmod(i - FIRST_STAGE2, 2)
-            if early < 2:
-                for m in (2 * b, 2 * b + 1):
-                    report(early, m, m < M - 1)
-            elif h == 1:
-                for m in CLOSING[v == V - 2][n]:
-                    report(q, m, m < 2)
-                    long_ones += m < 2
-            elif q < last - 1:
-                report(q, n, n % 2 == 0)
-                long_ones += n % 2 == 0
-            closing = early >= 2 and h == 1
-            if closing and n == 3:
-                add_two(v, 2, M)
-            if closing and n == 1 and not waiting and i - 1 not in turns:
-                invert(v, 0, 2, part(v, 1, 0, 2))
-                waiting.extend((v, m) for m in range(M))
-                v = None
-            if waiting and long_ones < 2 and i not in (STEPS - 4, STEPS - 1):
-                finish(*waiting[0])
-                waiting.remove(waiting[0])
-            if closing and n == 3:
-                invert(v, 2, M, recs[v][:, 2:M])
-            if i - 1 in turns:
-                quantize_rows(*turns[i - 1])
-            if closing and n == 1 and v is not None:
-                invert(v, 0, 2, part(v, 1, 0, 2))
-                waiting.extend((v, m) for m in range(M))
+        turn_pair(pair(2, 0))
+        sort(pair(3, 0))
+        steps(10)
+        fill(0)
+        empty(0, 0)
+        empty(0, 1)
+        empty(0, 2)
+        steps(11)
+        quantize_rows(*pair(2, 0))
+        quantize_power(2)
+        empty(0, 3, on_vector=False)
+        turn_pair(pair(2, 1))
+        steps(12, 13, 14)
+        sort(pair(3, 1))
+        quantize_rows(*pair(2, 1))
+        fill(2)
+        empty(2, 0)
+        empty(2, 1)
+        invert_carried(0, 0, 1)
+        finish_on_gpsimd(0, 0)
+        empty(2, 2)
+        invert_carried(0, 1, 2)
+        finish_on_gpsimd(0, 1)
+        empty(2, 3)
+        steps(15, 16, 17)
+        fill(1)
+        empty(1, 0)
+        invert_carried(0, 2, 3)
+        empty(1, 1)
+        empty(1, 2)
+        empty(1, 3, on_vector=False)
+        turn_pair(pair(3, 0))
+        quantize_power(3)
+        quantize_rows(*pair(3, 0))
+        invert_carried(0, 3, 4)
+        finish(0, 2)
+        steps(18, 19)
+        turn_pair(pair(3, 1))
+        fill(3)
+        finish_on_gpsimd(0, 3)
+        empty(3, 0)
+        empty(3, 1)
+        empty(3, 2, on_vector=False)
+        empty(3, 3, on_vector=False)
+        steps(20, 21, 22, 23)
+        quantize_power(4)
+        invert_carried(1, 0, 1)
+        quantize_rows(*pair(3, 1))
+        add_two(1, 2, 4)
+        invert_carried(1, 1, 2)
+        finish(1, 0)
+        fill(4)
+        finish_on_gpsimd(1, 1)
+        empty(4, 0)
+        invert_added(1, 2, 3)
+        empty(4, 1)
+        empty(4, 2, on_vector=False)
+        empty(4, 3, on_vector=False)
+        quantize_power(5)
+        invert_added(1, 3, 4)
+        finish(1, 2)
+        steps(24, 25, 26)
+        fill(5)
+        finish_on_gpsimd(1, 3)
+        empty(5, 0)
+        empty(5, 1)
+        invert_carried(2, 0, 1)
+        empty(5, 2)
+        empty(5, 3, on_vector=False)
+        steps(27)
+        finish(2, 0)
+        invert_carried(2, 1, 3)
+        quantize_power(6)
+        add_two(2, 3, 4)
+        finish(2, 1)
+        steps(28, 29)
+        invert_added(2, 3, 4)
+        quantize_power(7, 0, quarter)
+        finish(2, 2)
+        steps(30, 31)
+        waiting = [(2, 3)]
 
         v = V - 1
         quantize_power(last, quarter, quarter)
-        report(last - 1, 0, False)
+        fill(last - 1, [0])
+        empty(last - 1, 0, on_vector=False)
         stage2(bank()[:, :quarter], last, 0, 0)
         read(last, 0, 0, 1, False)
-        report(last - 1, 1, False)
+        fill(last - 1, [1])
+        empty(last - 1, 1, on_vector=False)
         stage2(bank()[:, :quarter], last, quarter, 0)
         for tile in waiting:
             finish(*tile)
@@ -374,7 +427,8 @@ def tile_forecast_variance_shares_s7_kernel(tc, psi, factor_bytes, factor_scale,
             var[last, 0, m] = ps[:]
             read(last, 0, m, 1, False)
             if m < M - 1:
-                report(last - 1, m + 1, False)
+                fill(last - 1, [m + 1])
+                empty(last - 1, m + 1, on_vector=False)
         invert(v, 0, 1, part(v, 2, 0, 1))
         for m in range(M - 1):
             scale(v, m, 0, HALF)

@@ -25,7 +25,7 @@ UNITS = HALF // UNIT
 CHUNK = 256
 RUN = 4
 ORDER = [(0, 0), (1, 0), (0, 1), (1, 1), (2, 0), (2, 1), (3, 0), (3, 1)]
-STEPS = len(ORDER) * UNITS
+SHORT_SHARE = 768
 
 
 def tile_forecast_variance_shares_s7_kernel(tc, psi, factor_bytes, factor_scale, cum, out):
@@ -104,7 +104,7 @@ def tile_forecast_variance_shares_s7_kernel(tc, psi, factor_bytes, factor_scale,
 
         def sort(keys):
             v, t0 = keys[0]
-            words = work.tile([P, K], F32, name="sorted_words", bufs=2)
+            words = work.tile([P, K], F32, name="sorted_words", bufs=3)
             nc.vector.tensor_copy(words[:].rearrange("p (g u r) -> p g u r", g=4, u=2),
                                   row_pairs[v, t0 // 2].bitcast(F32).rearrange("p (g r u) -> p g u r", g=4, u=2))
             for i, key in enumerate(keys):
@@ -238,9 +238,12 @@ def tile_forecast_variance_shares_s7_kernel(tc, psi, factor_bytes, factor_scale,
             scale(v, m)
             store(v, m)
 
-        def finish_on_gpsimd(v, m):
-            row = res[v][:, m * J:(m + 1) * J]
+        def scale_on_gpsimd(v, m, n=J):
+            row = res[v][:, m * J:m * J + n]
             nc.gpsimd.tensor_scalar(row, row, recs[v][:, M + m:M + m + 1], float(J), op0=ALU.mult, op1=ALU.mult)
+
+        def finish_on_gpsimd(v, m):
+            scale_on_gpsimd(v, m)
             store(v, m)
 
         def steps(*numbers):
@@ -251,6 +254,10 @@ def tile_forecast_variance_shares_s7_kernel(tc, psi, factor_bytes, factor_scale,
         def fill(q, tiles=range(M)):
             for m in tiles:
                 stage2(bank()[:], q, 0, m)
+
+        def finish_rest(v, m):
+            scale(v, m, SHORT_SHARE, J - SHORT_SHARE)
+            store(v, m)
 
         def empty(q, *tiles, on_vector=True):
             v, h = ORDER[q]
@@ -288,7 +295,8 @@ def tile_forecast_variance_shares_s7_kernel(tc, psi, factor_bytes, factor_scale,
         weave(1, 1)
         quantize_factor(1, 0)
         quantize_factor(1, 1)
-        widen(2, 0, True)
+        widen(2, 0, True, CHUNK, range(T - 1))
+        widen(2, 0, True, HALF, range(T - 1, T))
 
         stage1(0, 1)
         square(0, 1)
@@ -307,19 +315,19 @@ def tile_forecast_variance_shares_s7_kernel(tc, psi, factor_bytes, factor_scale,
         quantize_rows((1, 2))
         quantize_rows((1, 3))
         stage1(4, 5, 6, 7, slots=range(2))
-        widen(3, 0, True)
+        widen(3, 0, True, CHUNK, range(T - 1))
         turn_pair(pair("cum", 0))
         stage1(4, slots=range(2, T))
         stage1(5, slots=range(2, T))
         stage1(6, slots=range(2, T))
         stage1(7, slots=range(2, T))
         square(4, 5, 6, 7)
-        sort(pair(2, 0))
         weave(3, 0, 1)
         quantize_rows(*pair("cum", 0))
         quantize_factor(3, 0, 1)
         quantize_power(0)
         steps(8)
+        sort(pair(2, 1))
         quantize_power(1)
         steps(9)
 
@@ -329,9 +337,7 @@ def tile_forecast_variance_shares_s7_kernel(tc, psi, factor_bytes, factor_scale,
         sort(pair(3, 0))
         steps(10)
         fill(0)
-        empty(0, 0)
-        empty(0, 1)
-        empty(0, 2)
+        empty(0, 0, 1, 2)
         steps(11)
         quantize_rows(*pair(2, 0))
         quantize_power(2)
@@ -341,8 +347,7 @@ def tile_forecast_variance_shares_s7_kernel(tc, psi, factor_bytes, factor_scale,
         sort(pair(3, 1))
         quantize_rows(*pair(2, 1))
         fill(2)
-        empty(2, 0)
-        empty(2, 1)
+        empty(2, 0, 1)
         invert_carried(0, 0, 1)
         finish_on_gpsimd(0, 0)
         empty(2, 2)
@@ -351,11 +356,9 @@ def tile_forecast_variance_shares_s7_kernel(tc, psi, factor_bytes, factor_scale,
         empty(2, 3)
         steps(15, 16, 17)
         fill(1)
-        empty(1, 0)
+        empty(1, 0, on_vector=False)
         invert_carried(0, 2, 3)
-        empty(1, 1)
-        empty(1, 2)
-        empty(1, 3, on_vector=False)
+        empty(1, 1, 2, 3)
         turn_pair(pair(3, 0))
         quantize_power(3)
         quantize_rows(*pair(3, 0))
@@ -364,48 +367,43 @@ def tile_forecast_variance_shares_s7_kernel(tc, psi, factor_bytes, factor_scale,
         steps(18, 19)
         turn_pair(pair(3, 1))
         fill(3)
-        finish_on_gpsimd(0, 3)
-        empty(3, 0)
-        empty(3, 1)
-        empty(3, 2, on_vector=False)
-        empty(3, 3, on_vector=False)
+        scale_on_gpsimd(0, 3, SHORT_SHARE)
+        empty(3, 0, 1)
+        invert_carried(1, 0, 1)
+        empty(3, 2, 3, on_vector=False)
         steps(20, 21, 22, 23)
         quantize_power(4)
-        invert_carried(1, 0, 1)
+        finish_rest(0, 3)
         quantize_rows(*pair(3, 1))
-        add_two(1, 2, 4)
+        add_two(1, 2, M)
         invert_carried(1, 1, 2)
         finish(1, 0)
         fill(4)
-        finish_on_gpsimd(1, 1)
+        scale_on_gpsimd(1, 1, SHORT_SHARE)
         empty(4, 0)
-        invert_added(1, 2, 3)
+        invert_added(1, 2, M)
         empty(4, 1)
-        empty(4, 2, on_vector=False)
-        empty(4, 3, on_vector=False)
+        empty(4, 2, 3, on_vector=False)
         quantize_power(5)
-        invert_added(1, 3, 4)
+        finish_rest(1, 1)
         finish(1, 2)
         steps(24, 25, 26)
         fill(5)
-        finish_on_gpsimd(1, 3)
-        empty(5, 0)
-        empty(5, 1)
+        empty(5, 0, 1)
         invert_carried(2, 0, 1)
-        empty(5, 2)
-        empty(5, 3, on_vector=False)
+        finish(1, 3)
+        empty(5, 2, 3, on_vector=False)
         steps(27)
         finish(2, 0)
-        invert_carried(2, 1, 3)
-        quantize_power(6)
-        add_two(2, 3, 4)
+        invert_carried(2, 1, 2)
+        quantize_power(last - 1)
+        add_two(2, 2, M)
         finish(2, 1)
         steps(28, 29)
-        invert_added(2, 3, 4)
-        quantize_power(7, 0, quarter)
+        invert_added(2, 2, M)
+        quantize_power(last, 0, quarter)
         finish(2, 2)
         steps(30, 31)
-        waiting = [(2, 3)]
 
         v = V - 1
         quantize_power(last, quarter, quarter)
@@ -416,8 +414,7 @@ def tile_forecast_variance_shares_s7_kernel(tc, psi, factor_bytes, factor_scale,
         fill(last - 1, [1])
         empty(last - 1, 1, on_vector=False)
         stage2(bank()[:, :quarter], last, quarter, 0)
-        for tile in waiting:
-            finish(*tile)
+        finish(v - 1, M - 1)
         add_two(v, 0, 1)
         read(last, quarter, 0, 2, True, recs[v][:, 0:1])
         for m in range(1, M):

@@ -378,24 +378,24 @@ def tile_forecast_variance_shares_s7_kernel(tc, psi, factor_bytes, factor_scale,
         add_two(1, 2, M)
         invert_carried(1, 1, 2)
         finish(1, 0)
+        invert_added(1, 2, 3)
+        finish(1, 1)
         fill(4)
-        scale_on_gpsimd(1, 1, SHORT_SHARE)
+        scale_on_gpsimd(1, 2, SHORT_SHARE)
         empty(4, 0)
-        invert_added(1, 2, M)
+        invert_added(1, 3, M)
         empty(4, 1)
         empty(4, 2, 3, on_vector=False)
         quantize_power(5)
-        finish_rest(1, 1)
-        finish(1, 2)
-        steps(24, 25, 26)
+        finish_rest(1, 2)
+        finish(1, 3)
+        steps(24, 25, 26, 27)
         fill(5)
         empty(5, 0, 1)
         invert_carried(2, 0, 1)
-        finish(1, 3)
-        empty(5, 2, 3, on_vector=False)
-        steps(27)
-        finish(2, 0)
         invert_carried(2, 1, 2)
+        empty(5, 2, 3, on_vector=False)
+        finish(2, 0)
         quantize_power(last - 1)
         add_two(2, 2, M)
         finish(2, 1)

@@ -33,7 +33,7 @@ def tile_forecast_variance_shares_s7_kernel(tc, psi, factor_bytes, factor_scale,
     with ExitStack() as ctx:
         keep = ctx.enter_context(tc.tile_pool(name="keep", bufs=1))
         work = ctx.enter_context(tc.tile_pool(name="work", bufs=4))
-        outs = ctx.enter_context(tc.tile_pool(name="outs", bufs=3))
+        outs = ctx.enter_context(tc.tile_pool(name="outs", bufs=2))
         psum = ctx.enter_context(tc.psum_pool(name="psum", bufs=8))
 
         ident = keep.tile([P, P], F32, name="ident")
@@ -92,8 +92,8 @@ def tile_forecast_variance_shares_s7_kernel(tc, psi, factor_bytes, factor_scale,
         def quantize(src, *keys):
             n = src.shape[1] // T
             name = "_".join(str(x) for x in keys[0])
-            code_tile = keep.tile([P, n], U32, name="codes_" + name, align_bytes=64)
-            scale_tile = keep.tile([P, n], U8, name="scales_" + name, align_bytes=64)
+            code_tile = keep.tile([P, n], U32, name="codes_" + name, align_bytes=256)
+            scale_tile = keep.tile([P, n], U8, name="scales_" + name, align_bytes=256)
             nc.vector.quantize_mx(out=code_tile[:].bitcast(FP8X4), scales=scale_tile[:], in_=src)
             each = n // len(keys)
             for i, key in enumerate(keys):
@@ -124,7 +124,7 @@ def tile_forecast_variance_shares_s7_kernel(tc, psi, factor_bytes, factor_scale,
         def group(key):
             v, t = key
             if t % 2 == 0:
-                grouped[v, t // 2] = work.tile([P, 2 * K], BF16, name="grouped", align_bytes=64, bufs=3)
+                grouped[v, t // 2] = work.tile([P, 2 * K], BF16, name="grouped", align_bytes=256, bufs=3)
             dst = grouped[v, t // 2][:, t % 2 * K:(t % 2 + 1) * K].bitcast(F32).rearrange("p (g r u) -> p g r u", g=2, u=2)
             src = turned[key][:].rearrange("p (g u r) -> p g r u", g=2, u=2)
             nc.scalar.copy(dst, src)
@@ -158,7 +158,7 @@ def tile_forecast_variance_shares_s7_kernel(tc, psi, factor_bytes, factor_scale,
         def weave(c, *passes):
             h, n0 = divmod(c * CHUNK, HALF)
             g0, k = passes[0], len(passes)
-            woven[c, g0] = work.tile([P, k * CHUNK * T], BF16, name="woven", align_bytes=64)
+            woven[c, g0] = work.tile([P, k * CHUNK * T], BF16, name="woven", align_bytes=256)
             src = planes[h][:].rearrange("p (g t n i) -> p g n t i", g=G, t=T, i=RUN)
             nc.vector.tensor_copy(woven[c, g0][:].rearrange("p (g n i t) -> p g n t i", g=k, t=T, i=RUN),
                                   src[:, g0:g0 + k, n0 // RUN:(n0 + CHUNK) // RUN])
@@ -166,7 +166,7 @@ def tile_forecast_variance_shares_s7_kernel(tc, psi, factor_bytes, factor_scale,
         def quantize_factor(c, *passes):
             quantize(woven[c, passes[0]][:], *[("factor", c, g) for g in passes])
 
-        theta, power, var, res, sums, recs = {}, {}, {}, {}, {}, {}
+        theta, power, var, res, sums, recs, shares = {}, {}, {}, {}, {}, {}, {}
 
         def stage1(*steps, slots=range(T)):
             for i in steps:
@@ -189,7 +189,7 @@ def tile_forecast_variance_shares_s7_kernel(tc, psi, factor_bytes, factor_scale,
             for i in steps:
                 q, a = divmod(i, UNITS)
                 if a == 0:
-                    power[q] = work.tile([P, HALF * T], BF16, name="power", align_bytes=64, bufs=3)
+                    power[q] = work.tile([P, HALF * T], BF16, name="power", align_bytes=256, bufs=3)
                 nc.scalar.activation(power[q][:, a * UNIT * T:(a + 1) * UNIT * T].rearrange("p (n t) -> p n t", t=T),
                                      theta[i][:].rearrange("p (t n) -> p n t", t=T), ACT.Square)
 
@@ -227,20 +227,21 @@ def tile_forecast_variance_shares_s7_kernel(tc, psi, factor_bytes, factor_scale,
         def invert(v, m0, m1, total):
             nc.vector.reciprocal(recs[v][:, M + m0:M + m1], total)
 
-        def scale(v, m, n0=0, n=J):
-            row = res[v][:, m * J + n0:m * J + n0 + n]
-            nc.vector.tensor_scalar(row, row, recs[v][:, M + m:M + m + 1], float(J), op0=ALU.mult, op1=ALU.mult)
+        def scale(v, m, n0=0, n=J, engine=nc.vector):
+            if (v, m) not in shares:
+                shares[v, m] = outs.tile([P, J], F32, name="shares", bufs=6)
+            engine.tensor_scalar(shares[v, m][:, n0:n0 + n], res[v][:, m * J + n0:m * J + n0 + n],
+                                 recs[v][:, M + m:M + m + 1], float(J), op0=ALU.mult, op1=ALU.mult)
 
         def store(v, m, n0=0, n=J):
-            nc.sync.dma_start(out=out[v][m * P:(m + 1) * P, n0:n0 + n], in_=res[v][:, m * J + n0:m * J + n0 + n])
+            nc.sync.dma_start(out=out[v][m * P:(m + 1) * P, n0:n0 + n], in_=shares[v, m][:, n0:n0 + n])
 
         def finish(v, m):
             scale(v, m)
             store(v, m)
 
         def scale_on_gpsimd(v, m, n=J):
-            row = res[v][:, m * J:m * J + n]
-            nc.gpsimd.tensor_scalar(row, row, recs[v][:, M + m:M + m + 1], float(J), op0=ALU.mult, op1=ALU.mult)
+            scale(v, m, 0, n, nc.gpsimd)
 
         def finish_on_gpsimd(v, m):
             scale_on_gpsimd(v, m)

@@ -76,11 +76,11 @@ def tile_forecast_variance_shares_s7_kernel(tc, psi, factor_bytes, factor_scale,
         for g in range(G):
             load_factor(1, g, 0, T)
             load_psi(1, 2 * g, 2)
-        cum_rows = keep.tile([P, M * H], BF16, name="cum_rows")
-        nc.sync.dma_start(out=cum_rows[:].rearrange("p (m h) -> p m h", m=M), in_=cum.rearrange("(m p) h -> p m h", p=P))
-        rows["cum", 0] = cum_rows[:, :2 * H]
-        rows["cum", 1] = cum_rows[:, 2 * H:]
-        row_pairs["cum", 0] = cum_rows[:]
+        for b in range(2):
+            cum_rows = keep.tile([P, 2 * H], BF16, name="cum_rows%d" % b)
+            nc.sync.dma_start(out=cum_rows[:].rearrange("p (m h) -> p m h", m=2),
+                              in_=cum.rearrange("(m p) h -> p m h", p=P)[:, 2 * b:2 * b + 2])
+            rows["cum", b] = cum_rows[:]
         load_psi(2, 0, T)
         load_psi(3, 0, T)
 
@@ -307,17 +307,16 @@ def tile_forecast_variance_shares_s7_kernel(tc, psi, factor_bytes, factor_scale,
         stage1(3)
         square(2, 3)
         widen(2, 1, False, HALF)
-        quantize_factor(2, 0)
         quantize_rows(*pair(1, 0))
+        quantize_factor(2, 0)
         weave(2, 1)
         turn_pair(pair(1, 1))
-        sort(pair("cum", 0))
-        quantize_factor(2, 1)
-        quantize_rows((1, 2))
-        quantize_rows((1, 3))
-        stage1(4, 5, 6, 7, slots=range(2))
         widen(3, 0, True, CHUNK, range(T - 1))
         turn_pair(pair("cum", 0))
+        quantize_rows((1, 2))
+        quantize_factor(2, 1)
+        quantize_rows((1, 3))
+        stage1(4, 5, 6, 7, slots=range(2))
         stage1(4, slots=range(2, T))
         stage1(5, slots=range(2, T))
         stage1(6, slots=range(2, T))

@@ -51,14 +51,14 @@ def tile_forecast_variance_shares_s7_kernel(tc, psi, factor_bytes, factor_scale,
         rows, row_pairs = {}, {}
 
         def load_factor(h, g, t0, n):
-            tile = keep.tile([P, n, HALF], U8, name="f_bytes%d%d%d" % (h, g, t0))
+            tile = keep.tile([P, n, HALF], U8, name="f_bytes%d%d%d" % (h, g, t0), align_bytes=256)
             src = factor_bytes.rearrange("(g p t) n -> g p t n", p=P, t=T)[g]
             nc.sync.dma_start(out=tile[:], in_=src[:, t0:t0 + n, h * HALF:(h + 1) * HALF])
             for i in range(n):
                 f_bytes[h, g, t0 + i] = tile[:, i, :]
 
         def load_psi(v, t0, n):
-            tile = keep.tile([P, n * K], BF16, name="psi_rows%d%d" % (v, t0))
+            tile = keep.tile([P, n * K], BF16, name="psi_rows%d%d" % (v, t0), align_bytes=256)
             nc.sync.dma_start(out=tile[:], in_=psi[v].rearrange("(p t) k -> p (t k)", t=T)[:, t0 * K:(t0 + n) * K])
             for i in range(n):
                 rows[v, t0 + i] = tile[:, i * K:(i + 1) * K]
@@ -77,7 +77,7 @@ def tile_forecast_variance_shares_s7_kernel(tc, psi, factor_bytes, factor_scale,
             load_factor(1, g, 0, T)
             load_psi(1, 2 * g, 2)
         for b in range(2):
-            cum_rows = keep.tile([P, 2 * H], BF16, name="cum_rows%d" % b)
+            cum_rows = keep.tile([P, 2 * H], BF16, name="cum_rows%d" % b, align_bytes=256)
             nc.sync.dma_start(out=cum_rows[:].rearrange("p (m h) -> p m h", m=2),
                               in_=cum.rearrange("(m p) h -> p m h", p=P)[:, 2 * b:2 * b + 2])
             rows["cum", b] = cum_rows[:]
@@ -104,7 +104,7 @@ def tile_forecast_variance_shares_s7_kernel(tc, psi, factor_bytes, factor_scale,
 
         def sort(keys):
             v, t0 = keys[0]
-            words = work.tile([P, K], F32, name="sorted_words", bufs=3)
+            words = work.tile([P, K], F32, name="sorted_words", bufs=3, align_bytes=256)
             nc.vector.tensor_copy(words[:].rearrange("p (g u r) -> p g u r", g=4, u=2),
                                   row_pairs[v, t0 // 2].bitcast(F32).rearrange("p (g r u) -> p g u r", g=4, u=2))
             for i, key in enumerate(keys):
@@ -142,7 +142,7 @@ def tile_forecast_variance_shares_s7_kernel(tc, psi, factor_bytes, factor_scale,
             v, t = keys[0]
             quantize(grouped[v, t // 2][:, t % 2 * K:(t % 2 + len(keys)) * K], *keys)
 
-        planes = [keep.tile([P, G * T * HALF], BF16, name="planes%d" % h) for h in range(J // HALF)]
+        planes = [keep.tile([P, G * T * HALF], BF16, name="planes%d" % h, align_bytes=256) for h in range(J // HALF)]
         woven = {}
 
         def widen(c, g, on_scalar=False, n=CHUNK, slots=range(T)):
@@ -210,7 +210,7 @@ def tile_forecast_variance_shares_s7_kernel(tc, psi, factor_bytes, factor_scale,
         def read(q, n0, m, j, on_vector, start=None):
             v, h = ORDER[q]
             if v not in res:
-                res[v] = outs.tile([P, M * J], F32, name="res")
+                res[v] = outs.tile([P, M * J], F32, name="res", align_bytes=256)
                 sums[v] = keep.tile([P, 3 * M], F32, name="sums%d" % v)
                 recs[v] = keep.tile([P, 2 * M], F32, name="recs%d" % v)
             src = var[q, n0, m]
@@ -229,7 +229,7 @@ def tile_forecast_variance_shares_s7_kernel(tc, psi, factor_bytes, factor_scale,
 
         def scale(v, m, n0=0, n=J, engine=nc.vector):
             if (v, m) not in shares:
-                shares[v, m] = outs.tile([P, J], F32, name="shares", bufs=6)
+                shares[v, m] = outs.tile([P, J], F32, name="shares", bufs=6, align_bytes=256)
             engine.tensor_scalar(shares[v, m][:, n0:n0 + n], res[v][:, m * J + n0:m * J + n0 + n],
                                  recs[v][:, M + m:M + m + 1], float(J), op0=ALU.mult, op1=ALU.mult)
 

@@ -42,8 +42,9 @@ def tile_forecast_variance_shares_s7_kernel(tc, psi, factor_bytes, factor_scale,
         ctx.enter_context(tc.manual_schedule())
 
         f_scale = keep.tile([P, G, 2 * T], F32, name="f_scale")
-        nc.scalar.dma_start(out=f_scale[:, :, :T],
-                            in_=factor_scale.rearrange("(g p t) o -> p g (t o)", p=P, t=T))
+        for g in range(G):
+            nc.scalar.dma_start(out=f_scale[:, g, :T],
+                                in_=factor_scale.rearrange("(g p t) o -> g p (t o)", p=P, t=T)[g])
         idle = keep.tile([P, 2], F32, name="idle")
         nc.vector.memset(idle[:, :1], 0.0)
         nc.scalar.activation(idle[:, 1:], idle[:, :1], ACT.Square)

from contextlib import ExitStack

import concourse.mybir as mybir
from concourse.masks import make_identity

V, H, K, J, R = 4, 512, 1024, 1024, 512
FLOPS = 2 * V * (H * K * J + R * H * J)

F32 = mybir.dt.float32
BF16 = mybir.dt.bfloat16
U32 = mybir.dt.uint32
U8 = mybir.dt.uint8
FP8 = mybir.dt.float8_e4m3fn
FP8X4 = mybir.dt.float8_e4m3fn_x4
ACT = mybir.ActivationFunctionType
ALU = mybir.AluOpType

P = 128
T = 4
G = K // (P * T)
M = R // P
UNIT = 128
HALF = 512
UNITS = HALF // UNIT
CHUNK = 256
RUN = 4
ORDER = [(0, 0), (1, 0), (0, 1), (1, 1), (2, 0), (2, 1), (3, 0), (3, 1)]
SHORT_SHARE = 768


def tile_forecast_variance_shares_s7_kernel(tc, psi, factor_bytes, factor_scale, cum, out):
    nc = tc.nc
    with ExitStack() as ctx:
        keep = ctx.enter_context(tc.tile_pool(name="keep", bufs=1))
        work = ctx.enter_context(tc.tile_pool(name="work", bufs=4))
        outs = ctx.enter_context(tc.tile_pool(name="outs", bufs=2))
        psum = ctx.enter_context(tc.psum_pool(name="psum", bufs=8))

        ident = keep.tile([P, P], F32, name="ident")
        make_identity(nc, ident[:])

        ctx.enter_context(tc.manual_schedule())

        f_scale = keep.tile([P, G, 2 * T], F32, name="f_scale")
        for g in range(G):
            nc.scalar.dma_start(out=f_scale[:, g, :T],
                                in_=factor_scale.rearrange("(g p t) o -> g p (t o)", p=P, t=T)[g])
        idle = keep.tile([P, 2], F32, name="idle")
        nc.vector.memset(idle[:, :1], 0.0)
        nc.scalar.activation(idle[:, 1:], idle[:, :1], ACT.Square)
        f_bytes = {}
        rows, row_pairs = {}, {}

        def load_factor(h, g, t0, n):
            tile = keep.tile([P, n, HALF], U8, name="f_bytes%d%d%d" % (h, g, t0), align_bytes=256)
            src = factor_bytes.rearrange("(g p t) n -> g p t n", p=P, t=T)[g]
            nc.sync.dma_start(out=tile[:], in_=src[:, t0:t0 + n, h * HALF:(h + 1) * HALF])
            for i in range(n):
                f_bytes[h, g, t0 + i] = tile[:, i, :]

        def load_psi(v, t0, n):
            tile = keep.tile([P, n * K], BF16, name="psi_rows%d%d" % (v, t0), align_bytes=256)
            nc.sync.dma_start(out=tile[:], in_=psi[v].rearrange("(p t) k -> p (t k)", t=T)[:, t0 * K:(t0 + n) * K])
            for i in range(n):
                rows[v, t0 + i] = tile[:, i * K:(i + 1) * K]
            for b in range(n // 2):
                row_pairs[v, t0 // 2 + b] = tile[:, 2 * b * K:2 * (b + 1) * K]

        load_factor(0, 0, 0, 2)
        load_factor(0, 0, 2, 2)
        load_factor(0, 1, 0, 2)
        load_psi(0, 0, 1)
        load_factor(0, 1, 2, 2)
        load_psi(0, 1, 1)
        load_psi(0, 2, 1)
        load_psi(0, 3, 1)
        for g in range(G):
            load_factor(1, g, 0, T)
            load_psi(1, 2 * g, 2)
        for b in range(2):
            cum_rows = keep.tile([P, 2 * H], BF16, name="cum_rows%d" % b, align_bytes=256)
            nc.sync.dma_start(out=cum_rows[:].rearrange("p (m h) -> p m h", m=2),
                              in_=cum.rearrange("(m p) h -> p m h", p=P)[:, 2 * b:2 * b + 2])
            rows["cum", b] = cum_rows[:]
        load_psi(2, 0, T)
        load_psi(3, 0, T)

        def bank():
            return psum.tile([P, HALF], F32, name="bank")

        codes, scales = {}, {}

        def quantize(src, *keys):
            n = src.shape[1] // T
            name = "_".join(str(x) for x in keys[0])
            code_tile = keep.tile([P, n], U32, name="codes_" + name, align_bytes=256)
            scale_tile = keep.tile([P, n], U8, name="scales_" + name, align_bytes=256)
            nc.vector.quantize_mx(out=code_tile[:].bitcast(FP8X4), scales=scale_tile[:], in_=src)
            each = n // len(keys)
            for i, key in enumerate(keys):
                codes[key] = code_tile[:, i * each:(i + 1) * each]
                scales[key] = scale_tile[:, i * each:(i + 1) * each]

        sorted_words, turned, grouped = {}, {}, {}

        def sort(keys):
            v, t0 = keys[0]
            words = work.tile([P, K], F32, name="sorted_words", bufs=3, align_bytes=256)
            nc.vector.tensor_copy(words[:].rearrange("p (g u r) -> p g u r", g=4, u=2),
                                  row_pairs[v, t0 // 2].bitcast(F32).rearrange("p (g r u) -> p g u r", g=4, u=2))
            for i, key in enumerate(keys):
                sorted_words[key] = words[:, i * K // 2:(i + 1) * K // 2]

        def turn(key):
            turned[key] = bank()
            for g in range(2):
                for u in range(2):
                    cols = slice((2 * g + u) * P, (2 * g + u + 1) * P)
                    if key in sorted_words:
                        src = sorted_words[key][:, cols]
                    else:
                        src = rows[key].bitcast(F32)[:, 2 * P * g + u:2 * P * (g + 1):2]
                    nc.tensor.transpose(turned[key][:, cols], src, ident[:])

        def group(key):
            v, t = key
            if t % 2 == 0:
                grouped[v, t // 2] = work.tile([P, 2 * K], BF16, name="grouped", align_bytes=256, bufs=3)
            dst = grouped[v, t // 2][:, t % 2 * K:(t % 2 + 1) * K].bitcast(F32).rearrange("p (g r u) -> p g r u", g=2, u=2)
            src = turned[key][:].rearrange("p (g u r) -> p g r u", g=2, u=2)
            nc.scalar.copy(dst, src)

        def pair(v, b):
            return (v, 2 * b), (v, 2 * b + 1)

        def turn_pair(keys):
            for key in keys:
                turn(key)
            for key in keys:
                group(key)

        def quantize_rows(*keys):
            v, t = keys[0]
            quantize(grouped[v, t // 2][:, t % 2 * K:(t % 2 + len(keys)) * K], *keys)

        planes = [keep.tile([P, G * T * HALF], BF16, name="planes%d" % h, align_bytes=256) for h in range(J // HALF)]
        woven = {}

        def widen(c, g, on_scalar=False, n=CHUNK, slots=range(T)):
            h, n0 = divmod(c * CHUNK, HALF)
            for t in slots:
                dst = planes[h][:, (g * T + t) * HALF + n0:(g * T + t) * HALF + n0 + n]
                src = f_bytes[h, g, t][:, n0:n0 + n].bitcast(FP8)
                if on_scalar:
                    nc.scalar.activation(dst, src, ACT.Copy, scale=f_scale[:, g, t:t + 1])
                else:
                    nc.vector.tensor_scalar(dst, src, f_scale[:, g, t:t + 1], None, op0=ALU.mult)

        def weave(c, *passes):
            h, n0 = divmod(c * CHUNK, HALF)
            g0, k = passes[0], len(passes)
            woven[c, g0] = work.tile([P, k * CHUNK * T], BF16, name="woven", align_bytes=256)
            src = planes[h][:].rearrange("p (g t n i) -> p g n t i", g=G, t=T, i=RUN)
            nc.vector.tensor_copy(woven[c, g0][:].rearrange("p (g n i t) -> p g n t i", g=k, t=T, i=RUN),
                                  src[:, g0:g0 + k, n0 // RUN:(n0 + CHUNK) // RUN])

        def quantize_factor(c, *passes):
            quantize(woven[c, passes[0]][:], *[("factor", c, g) for g in passes])

        theta, power, var, res, sums, recs, shares = {}, {}, {}, {}, {}, {}, {}

        def stage1(*steps, slots=range(T)):
            for i in steps:
                if i not in theta:
                    theta[i] = bank()
            for t in slots:
                for i in steps:
                    v, h = ORDER[i // UNITS]
                    c, n0 = divmod(h * HALF + i % UNITS * UNIT, CHUNK)
                    for g in range(G):
                        nc.tensor.matmul_mx(
                            out=theta[i][:, t * UNIT:(t + 1) * UNIT],
                            lhsT=codes[v, t][:, g * P:(g + 1) * P].bitcast(FP8X4),
                            lhsT_scale=scales[v, t][:, g * P:(g + 1) * P],
                            rhs=codes["factor", c, g][:, n0:n0 + UNIT].bitcast(FP8X4),
                            rhs_scale=scales["factor", c, g][:, n0:n0 + UNIT],
                            start=(g == 0), stop=(g == G - 1))

        def square(*steps):
            for i in steps:
                q, a = divmod(i, UNITS)
                if a == 0:
                    power[q] = work.tile([P, HALF * T], BF16, name="power", align_bytes=256, bufs=3)
                nc.scalar.activation(power[q][:, a * UNIT * T:(a + 1) * UNIT * T].rearrange("p (n t) -> p n t", t=T),
                                     theta[i][:].rearrange("p (t n) -> p n t", t=T), ACT.Square)

        def quantize_power(q, n0=0, n=HALF):
            quantize(power[q][:, n0 * T:(n0 + n) * T], ("power", q, n0))

        def stage2(ps, q, n0, m):
            cols = slice(m % 2 * P, (m % 2 + 1) * P)
            nc.tensor.matmul_mx(out=ps, lhsT=codes["cum", m // 2][:, cols].bitcast(FP8X4),
                                lhsT_scale=scales["cum", m // 2][:, cols],
                                rhs=codes["power", q, n0].bitcast(FP8X4), rhs_scale=scales["power", q, n0],
                                start=True, stop=True)
            var[q, n0, m] = ps

        def part(v, j, m0, m1):
            return sums[v][:, j * M + m0:j * M + m1]

        def read(q, n0, m, j, on_vector, start=None):
            v, h = ORDER[q]
            if v not in res:
                res[v] = outs.tile([P, M * J], F32, name="res", align_bytes=256)
                sums[v] = keep.tile([P, 3 * M], F32, name="sums%d" % v)
                recs[v] = keep.tile([P, 2 * M], F32, name="recs%d" % v)
            src = var[q, n0, m]
            c0 = m * J + h * HALF + n0
            dst = res[v][:, c0:c0 + src.shape[1]]
            if on_vector:
                nc.vector.tensor_scalar(dst, src, 1.0, start, op0=ALU.mult, op1=ALU.add, accum_out=part(v, j, m, m + 1))
            else:
                nc.scalar.activation(dst, src, ACT.Copy, accum_out=part(v, j, m, m + 1))

        def add_two(v, m0, m1):
            nc.vector.tensor_tensor(recs[v][:, m0:m1], part(v, 0, m0, m1), part(v, 1, m0, m1), op=ALU.add)

        def invert(v, m0, m1, total):
            nc.vector.reciprocal(recs[v][:, M + m0:M + m1], total)

        def scale(v, m, n0=0, n=J, engine=nc.vector):
            if (v, m) not in shares:
                shares[v, m] = outs.tile([P, J], F32, name="shares", bufs=6, align_bytes=256)
            engine.tensor_scalar(shares[v, m][:, n0:n0 + n], res[v][:, m * J + n0:m * J + n0 + n],
                                 recs[v][:, M + m:M + m + 1], float(J), op0=ALU.mult, op1=ALU.mult)

        def store(v, m, n0=0, n=J):
            nc.sync.dma_start(out=out[v][m * P:(m + 1) * P, n0:n0 + n], in_=shares[v, m][:, n0:n0 + n])

        def finish(v, m):
            scale(v, m)
            store(v, m)

        def scale_on_gpsimd(v, m, n=J):
            scale(v, m, 0, n, nc.gpsimd)

        def finish_on_gpsimd(v, m):
            scale_on_gpsimd(v, m)
            store(v, m)

        def steps(*numbers):
            for i in numbers:
                stage1(i)
                square(i)

        def fill(q, tiles=range(M)):
            for m in tiles:
                stage2(bank()[:], q, 0, m)

        def finish_rest(v, m):
            scale(v, m, SHORT_SHARE, J - SHORT_SHARE)
            store(v, m)

        def empty(q, *tiles, on_vector=True):
            v, h = ORDER[q]
            for m in tiles:
                read(q, 0, m, h, on_vector, part(v, 0, m, m + 1) if h else None)

        def invert_carried(v, m0, m1):
            invert(v, m0, m1, part(v, 1, m0, m1))

        def invert_added(v, m0, m1):
            invert(v, m0, m1, recs[v][:, m0:m1])

        widen(0, 0)
        widen(1, 0, True)
        widen(0, 1, False, CHUNK, range(2))
        weave(0, 0)
        widen(0, 1, False, CHUNK, range(2, T))
        widen(1, 1, True)
        quantize_factor(0, 0)
        weave(0, 1)
        turn((0, 0))
        group((0, 0))
        turn((0, 1))
        group((0, 1))
        turn((0, 2))
        group((0, 2))
        turn((0, 3))
        group((0, 3))
        quantize_rows((0, 0))
        quantize_factor(0, 1)
        weave(1, 0)
        quantize_rows((0, 1))
        quantize_rows((0, 2))
        quantize_rows((0, 3))
        weave(1, 1)
        quantize_factor(1, 0)
        quantize_factor(1, 1)
        widen(2, 0, True, CHUNK, range(T - 1))
        widen(2, 0, True, HALF, range(T - 1, T))

        stage1(0, 1)
        square(0, 1)
        weave(2, 0)
        turn_pair(pair(1, 0))
        stage1(2)
        stage1(3)
        square(2, 3)
        widen(2, 1, False, HALF)
        quantize_rows(*pair(1, 0))
        quantize_factor(2, 0)
        weave(2, 1)
        turn_pair(pair(1, 1))
        widen(3, 0, True, CHUNK, range(T - 1))
        turn_pair(pair("cum", 0))
        quantize_rows((1, 2))
        quantize_factor(2, 1)
        quantize_rows((1, 3))
        stage1(4, 5, 6, 7, slots=range(2))
        stage1(4, slots=range(2, T))
        stage1(5, slots=range(2, T))
        stage1(6, slots=range(2, T))
        stage1(7, slots=range(2, T))
        square(4, 5, 6, 7)
        weave(3, 0, 1)
        quantize_rows(*pair("cum", 0))
        quantize_factor(3, 0, 1)
        quantize_power(0)
        steps(8)
        sort(pair(2, 1))
        quantize_power(1)
        steps(9)

        last = len(ORDER) - 1
        quarter = HALF // 2
        turn_pair(pair(2, 0))
        sort(pair(3, 0))
        steps(10)
        fill(0)
        empty(0, 0, 1, 2)
        steps(11)
        quantize_rows(*pair(2, 0))
        quantize_power(2)
        empty(0, 3, on_vector=False)
        turn_pair(pair(2, 1))
        steps(12, 13, 14)
        sort(pair(3, 1))
        quantize_rows(*pair(2, 1))
        fill(2)
        empty(2, 0, 1)
        invert_carried(0, 0, 1)
        finish_on_gpsimd(0, 0)
        empty(2, 2)
        invert_carried(0, 1, 2)
        finish_on_gpsimd(0, 1)
        empty(2, 3)
        steps(15, 16, 17)
        fill(1)
        empty(1, 0, on_vector=False)
        invert_carried(0, 2, 3)
        empty(1, 1, 2, 3)
        turn_pair(pair(3, 0))
        quantize_power(3)
        quantize_rows(*pair(3, 0))
        invert_carried(0, 3, 4)
        finish(0, 2)
        steps(18, 19)
        turn_pair(pair(3, 1))
        fill(3)
        scale_on_gpsimd(0, 3, SHORT_SHARE)
        empty(3, 0, 1)
        invert_carried(1, 0, 1)
        empty(3, 2, 3, on_vector=False)
        steps(20, 21, 22, 23)
        quantize_power(4)
        finish_rest(0, 3)
        quantize_rows(*pair(3, 1))
        add_two(1, 2, M)
        invert_carried(1, 1, 2)
        finish(1, 0)
        invert_added(1, 2, 3)
        finish(1, 1)
        fill(4)
        scale_on_gpsimd(1, 2, SHORT_SHARE)
        empty(4, 0)
        invert_added(1, 3, M)
        empty(4, 1)
        empty(4, 2, 3, on_vector=False)
        quantize_power(5)
        finish_rest(1, 2)
        finish(1, 3)
        steps(24, 25, 26, 27)
        fill(5)
        empty(5, 0, 1)
        invert_carried(2, 0, 1)
        invert_carried(2, 1, 2)
        empty(5, 2, 3, on_vector=False)
        finish(2, 0)
        quantize_power(last - 1)
        add_two(2, 2, M)
        finish(2, 1)
        steps(28, 29)
        invert_added(2, 2, M)
        quantize_power(last, 0, quarter)
        finish(2, 2)
        steps(30, 31)

        v = V - 1
        quantize_power(last, quarter, quarter)
        fill(last - 1, [0])
        empty(last - 1, 0, on_vector=False)
        stage2(bank()[:, :quarter], last, 0, 0)
        read(last, 0, 0, 1, False)
        fill(last - 1, [1])
        empty(last - 1, 1, on_vector=False)
        stage2(bank()[:, :quarter], last, quarter, 0)
        finish(v - 1, M - 1)
        add_two(v, 0, 1)
        read(last, quarter, 0, 2, True, recs[v][:, 0:1])
        for m in range(1, M):
            ps = bank()
            stage2(ps[:, :quarter], last, 0, m)
            stage2(ps[:, quarter:], last, quarter, m)
            var[last, 0, m] = ps[:]
            read(last, 0, m, 1, False)
            if m < M - 1:
                fill(last - 1, [m + 1])
                empty(last - 1, m + 1, on_vector=False)
        invert(v, 0, 1, part(v, 2, 0, 1))
        for m in range(M - 1):
            scale(v, m, 0, HALF)
            if m == 0:
                store(v, m, 0, HALF)
            add_two(v, m + 1, m + 2)
            scale(v, m, HALF, HALF)
            if m == 0:
                store(v, m, HALF, HALF)
            else:
                store(v, m)
            invert(v, m + 1, m + 2, recs[v][:, m + 1:m + 2])
        finish(v, M - 1)
